import numpy as np, ml_dtypes
CORES = [36,164,52,180,100,228,116,244]
N = 8
import mx_ref
BF = ml_dtypes.bfloat16
def pick(q, e):
    c = np.concatenate([q[0].reshape(128, -1, 4), np.zeros((128, 1, 4), np.uint8)], axis=1); s = np.concatenate([q[1], np.ones((16, 1), np.uint8)], axis=1)
    return (np.ascontiguousarray(c[:, e].reshape(128, -1)), np.ascontiguousarray(s[:, e]))
def join(*qs):
    return (np.concatenate([q[0] for q in qs], axis=1), np.concatenate([q[1] for q in qs], axis=1))
def put(q, e, v):
    c, s = q[0].reshape(128, -1, 4).copy(), q[1].copy(); c[:, e] = v[0].reshape(128, -1, 4); s[:, e] = v[1]
    return (c.reshape(128, -1), s)
def pk(c, s):
    return (np.ascontiguousarray(c), mx_ref.live(s))
def emit(q):
    return q[0], q[1]
def decode(q):
    o = []
    for b in range(4):
        e = np.zeros((128, 128, 4), np.float32); e[np.arange(128), np.arange(128), b] = 1
        o.append(mx_ref.matmul(mx_ref.quantize(e.reshape(128, 512).astype(BF)), q))
    return np.stack(o, axis=2).reshape(128, -1)
def f(rng, *shape):
    return mx_ref.flush((rng.standard_normal(shape, dtype=np.float32) * np.exp2(rng.integers(-2, 3, shape[:-1] + (1,)))).astype(BF))
def wide(rng, *shape, cols=0):
    v = rng.standard_normal(shape, dtype=np.float32) * np.exp2(rng.integers(-12, 13, shape)).astype(np.float32)
    if cols: v *= np.repeat(np.exp2(rng.integers(-cols, cols + 1, shape[:-2] + (1, shape[-1] // 4))) * (rng.random(shape[:-2] + (1, shape[-1] // 4)) > 0.0625), 4, axis=-1).astype(np.float32)
    return mx_ref.flush(v.astype(BF))
P, CAP, M, S = 16, 8, 40, 32
def big(v):
    v = np.array(v, np.float32)
    v[np.abs(v) < np.float32(2.0 ** -16)] = 0
    return v.astype(BF)
def setup_inputs(rng):
    u = big(f(rng, N, 128, 512))
    u[:, :, 8:] = 0
    return {"r0": big(f(rng, N, 128, 4 * P)), "r1": big(f(rng, N, 128, 16 * P)), "r2": big(f(rng, N, 128, 64 * P)), "u": u, "w": f(rng, N, 128, 512)}
def setup_inputs_far(rng):
    d = setup_inputs(rng)
    low = rng.permutation(N) < N // 2
    i = np.arange(128)
    side = np.where(i < 48, -1, np.where(i < 80, 0, 1))
    o, c = rng.permutation(N), rng.permutation(N // 2 * P)[:M // 8]
    kind = np.full((N, P), -1)
    kind[o[:N // 2], rng.integers(0, P, N // 2)] = 0
    kind[o[N // 2 + c // P], c % P] = 1
    on = (side[None, :, None] == 0) | (side[None, :, None] == kind[:, None, :])
    for k, m in (("r0", on), ("r1", np.repeat(on | (kind != 0)[:, None, :], 4, axis=2))):
        v = (1.5 + 0.5 * rng.random((N, 128, m.shape[2], 4))) * 2.0 ** 26
        d[k] = big((v * m[:, :, :, None]).reshape(N, 128, -1))
    g = np.where(low[:, None], -1, side[None, :])
    d["u"][:, :, :4] = big((1.875 + 0.125 * rng.random((N, 128, 4))) * 2.0 ** 29 * g[:, :, None])
    h = d["u"][:, :, 4:8].astype(np.float32) * (side == 0)[None, :, None]
    d["u"][:, :, 4:8] = big(np.where(low[:, None, None], (1.875 + 0.125 * rng.random((N, 128, 4))) * 2.0 ** 26, h))
    return d
def setup_inputs_near(rng):
    d = setup_inputs(rng)
    t = N * np.arange(P)[None, :] + rng.permutation(N)[:, None]
    a, b, u = np.zeros((N, 128, P, 4), np.float32), np.zeros((N, 128, 4 * P, 4), np.float32), np.zeros((N, 128, 512), np.float32)
    a[:, :64] = rng.integers(4, 8, (64, 4))[None, :, None, :]
    for i in range(3): a[:, 64, :, i] = t // 8 ** i % 8
    b[:, 64, :, 3] = np.arange(4 * P) % 4
    a[:, 72:] = f(rng, N, 56, 4 * P).astype(np.float32).reshape(N, 56, P, 4)
    b[:, 72:] = f(rng, N, 56, 16 * P).astype(np.float32).reshape(N, 56, 4 * P, 4)
    u[:, :64, :4] = 1024 * rng.integers(4, 8, (N, 64, 4))
    u[:, 64, :4] = np.array([4, 32, 256, 1])[None, :] * (1 - 2 * (np.arange(N) % 2))[:, None]
    u[:, 72:, 4:8] = f(rng, N, 56, 4).astype(np.float32)
    return {**d, "r0": big(a.reshape(N, 128, -1)), "r1": big(b.reshape(N, 128, -1)), "u": big(u)}
def setup_inputs_pile(rng):
    d = setup_inputs(rng)
    of = np.arange(128) // (128 // N)
    a, b = np.zeros((N, N)), np.full((N, N), 4.0)
    for r in range(N):
        o = rng.permutation(N)
        o = o[o != r]
        o = np.concatenate([[r], o]) if r % 2 == 0 else np.concatenate([o, [r]])
        a[r, o] = 2.0 ** (10 - 2 * np.arange(N))
        b[r, o[(M - 1) // P]] = 2.0 ** 14
    d["r0"] = big((1 + rng.random((N, 128, 4 * P))) * a[of].T[:, :, None])
    d["r1"] = big((1 + rng.random((N, 128, 16 * P))) * b[of].T[:, :, None])
    d["u"][:, :, :4] = big((1 + rng.random((N, 128, 4))) * (of[None, :] == np.arange(N)[:, None])[:, :, None])
    return d
def setup_inputs_spread(rng):
    d = setup_inputs(rng)
    a = wide(rng, N, 128, 4 * P, cols=6).astype(np.float32).reshape(N, 128, P, 4)
    b = wide(rng, N, 128, 16 * P, cols=6).astype(np.float32).reshape(N, 128, 4 * P, 4)
    c = wide(rng, N, 128, 64 * P, cols=6).astype(np.float32).reshape(N, 128, 16 * P, 4)
    for q in range(N):
        n = rng.permutation(P)[:2]
        x = (1 + rng.random((128, 1, 4))) * 2.0 ** 26 * rng.choice([-1.0, 1.0], (128, 1, 4))
        a[q][:, n] = np.concatenate([x, -x], axis=1)
        b[q][:, 4 * n] = -a[q][:, n]
        b[q][:, 4 * n + 1] = 0
        c[q][:, 4 * (4 * n + 1)] = -a[q][:, n]
    return {**d, "r0": big(a.reshape(N, 128, -1)), "r1": big(b.reshape(N, 128, -1)), "r2": big(c.reshape(N, 128, -1))}
def setup_inputs_ties(rng):
    d = setup_inputs(rng)
    x = np.abs(big(f(rng, 128, 4)).astype(np.float32))
    a = np.ones((N, P), np.float32)
    for q in range(N): a[q, 1 + rng.permutation(P - 1)[:M // 2 // N]] = 2
    b = np.where(np.arange(4)[None, None, :] == rng.integers(0, 4, (N, P))[:, :, None], 3 - a[:, :, None], 0.125).reshape(N, 4 * P)
    d["r0"] = big((x[None, :, None, :] * a[:, None, :, None]).reshape(N, 128, -1))
    d["r1"] = big((x[None, :, None, :] * b[:, None, :, None]).reshape(N, 128, -1))
    d["u"][:, :, :4] = np.abs(d["u"][:, :, :4].astype(np.float32)).astype(BF)
    return d
def check_inputs(d):
    b = []
    def bad(v, lo, hi):
        v = np.abs(v.astype(np.float32))
        return not (np.isfinite(v).all() and ((v == 0) | (v >= lo) & (v <= hi)).all())
    for k in ("u", "w"):
        if bad(d[k], 2.0 ** -30, 2.0 ** 30): b.append("a value of " + k)
    for k in ("r0", "r1", "r2"):
        if bad(d[k], 2.0 ** -16, 2.0 ** 27): b.append("a value of " + k)
    if bad(d["u"][:, :, 4:8], 2.0 ** -16, 2.0 ** 27): b.append("a value of column 1 of u")
    if (d["u"][:, :, 8:].astype(np.float32) != 0).any(): b.append("u has numbers behind its first 2 columns")
    return b
def take(s, own):
    s = s + np.float32(0.0)
    at = np.flatnonzero(own >= 0)
    best = at[np.argsort(-s[at], kind="stable")][:M]
    got = np.full((N, CAP), -1)
    for q in range(N):
        k = best[own[best] == q][:CAP]
        got[q, :k.size] = k
    return got
def held(q, e):
    return decode(pick(q, np.concatenate([e, np.full(-len(e) % 4, -1)]))).reshape(128, -1, 4)[:, :len(e)]
def reference(r0, r1, r2, u, w):
    y, nm = np.zeros((N, 128, 2 * N * S), np.float32), np.full((N, 1, 2 * N * S), -1, np.float32)
    oc, osc = np.zeros((N, 128, 4 * N * S), np.uint8), np.zeros((N, 16, N * S), np.uint8)
    roots = join(*[mx_ref.quantize(np.ascontiguousarray(r0[q])) for q in range(N)])
    res = [join(*[mx_ref.quantize(np.ascontiguousarray(a[q])) for q in range(N)]) for a in (r1, r2)]
    to = np.arange(N * S) // S
    for r in range(N):
        uq, wq = mx_ref.quantize(np.ascontiguousarray(u[r])), mx_ref.quantize(np.ascontiguousarray(w[r]))
        shift = held(uq, np.arange(1, 2))[:, 0]
        pool, own, num = roots, np.repeat(np.arange(N), P), np.tile(np.arange(P), N)
        for t in range(2):
            parent = np.repeat(take(mx_ref.matmul(uq, pool)[0], own).reshape(-1), 4)
            on = np.flatnonzero(parent >= 0)
            new = np.full(N * S, -1)
            new[on] = 4 * num[parent[on]] + on % 4
            e, back = np.unique(parent[on], return_inverse=True)
            v = np.zeros((128, N * S, 4), np.float32)
            v[:, on] = (held(pool, e)[:, back] + held(res[t], 4 ** (t + 1) * P * to[on] + new[on])) + shift[:, None, :]
            pool, own, num = mx_ref.quantize(np.ascontiguousarray(v.reshape(128, -1).astype(BF))), np.where(parent >= 0, to, -1), new
            i = t * N * S
            y[r, :, i:i + N * S] = mx_ref.matmul(wq, pool)
            nm[r, 0, i:i + N * S] = num
        oc[r], osc[r] = emit(pool)
    return {"y": y, "oc": oc, "osc": osc, "nm": nm}

@@ -1,0 +1,594 @@
+from concourse.bass import DstId, RemoteDMATransfer
+from concourse.mybir import dt, AluOpType, AxisListType, ActivationFunctionType
+
+NR, P, CAP, M, S = 8, 16, 8, 40, 32
+W1 = P + 2
+L0 = NR * W1
+R1 = 4 * P
+Z = 32
+DIRECT = 2
+TINY, HUGE, CAPV = 2.0 ** -110, 2.0 ** 90, 2.0 ** 80
+Q4, U8, BF, F32, I32, U16 = "float8_e4m3fn_x4", "uint8", "bfloat16", "float32", "int32", "uint16"
+
+SCRATCH = {}
+for _n, _w in (("q1", 128), ("qr", 320), ("qw", 128), ("qk", 1408), ("l0", L0), ("u16", 128), ("u32", 256), ("ra", 128),
+               ("r4", 128), ("mq", 128), ("x0", 196), ("x1", 144), ("ch", 256), ("hp", R1), ("lr", NR * R1), ("l1", 256),
+               ("pv", 256), ("pe", 256), ("av", 256), ("ae", 256), ("gr", 256), ("h0", S), ("l2", Z + 256), ("fin", 256)):
+    SCRATCH[_n + "c"] = ("sbuf", [128, _w], Q4)
+    SCRATCH[_n + "s"] = ("sbuf", [128, _w], U8)
+for _n, _w, _d in (("t1", 512, BF), ("tr", 1280, BF), ("tw", 512, BF), ("tk", 5632, BF), ("tx0", 784, BF), ("tx1", 576, BF),
+                   ("tch", 1024, BF), ("tgr", 1024, BF), ("ta1", 1024, BF), ("ci", 16, I32), ("cf", 32, F32), ("idx", 512, F32),
+                   ("so", 128, U16), ("do0", 64, U16), ("do1", 32, U16), ("do2", 16, U16), ("do3", 32, U16),
+                   ("thr0", 16, BF), ("thra", 128, BF), ("base1", 64, BF), ("diag", 16, F32), ("lref", 112, F32), ("plc", 16, F32),
+                   ("s0", 256, F32), ("dh", 32, F32), ("hx", 1024, F32), ("dc", 32, F32), ("dm", 16, F32), ("g2", 256, F32),
+                   ("d0", 16, BF), ("c0", 128, BF), ("ms", 64, F32), ("thd", 64, BF), ("thr1", 64, BF), ("d1", 64, BF), ("c1", 64, BF),
+                   ("da", 128, BF), ("ca", 128, BF), ("junk", 592, BF), ("m4", 64, F32), ("n1", 256, F32), ("cap", 256, F32),
+                   ("val", 256, F32), ("am", 256, F32), ("db", 256, BF), ("cb", 512, BF), ("n2", 32, F32), ("n2t", 32, F32),
+                   ("v2", 16, F32), ("o2", 16, F32), ("y0", 256, F32), ("y1", 256, F32)):
+    SCRATCH[_n] = ("sbuf", [128, _w], _d)
+for _k in range(8):
+    SCRATCH["p%d" % _k] = ("psum", [128, 512], F32)
+
+DMAS = ["ld%d" % _k for _k in range(24)]
+SEMAPHORES = ["V", "S", "PE", "G", "sent", "a0c", "a0s", "ahc", "ahs", "a1c", "a1s", "a2c", "a2s", "ah0c", "ah0s"] + DMAS
+
+ADD, SUB, MUL, MAX, MIN = AluOpType.add, AluOpType.subtract, AluOpType.mult, AluOpType.max, AluOpType.min
+GE, GT, LT, EQ = AluOpType.is_ge, AluOpType.is_gt, AluOpType.is_lt, AluOpType.is_equal
+SHR, AND = AluOpType.logical_shift_right, AluOpType.bitwise_and
+AF = ActivationFunctionType
+
+
+def bits(engines):
+    m = 0
+    for e in engines:
+        m |= 1 << e
+    return m
+
+
+def deal(engines, n, flip=False):
+    k = 1
+    while 2 * k * n <= len(engines):
+        k *= 2
+    sizes = [k] * n
+    if k * (n + 1) <= len(engines):
+        sizes[0] *= 2
+    eng = engines[::-1] if flip else engines
+    return [bits(eng[sum(sizes[:i]):sum(sizes[:i + 1])]) for i in range(n)], sizes
+
+
+def helpers_of(c, T, topo):
+    ok = [h for h in topo.cores_of(c) if T.rank_of(h) is None and topo.die(h) != topo.die(c)
+          and all(topo.may_write(h, d) for d in T.cores if d != c)]
+    return ok[:2]
+
+
+def engine_sets(src, c, T, topo):
+    far = topo.engines(src, [d for d in T.cores if d != c][0])
+    near = topo.engines(c, helpers_of(c, T, topo)[0])
+    return far, [e for e in near if e not in far]
+
+
+def route2(q, half):
+    to = [(q + i) % NR for i in range(1, NR)][4 * half:4 * half + 4]
+    n = DIRECT if half == 0 else len(to)
+    return to[:n], to[n:]
+
+
+def transfer(topo, src, dsts, mask, sem, a, b, kind):
+    b = b if isinstance(b, list) else [b] * len(dsts)
+    if kind == "c":
+        a, b = a.bitcast(dt.uint8), [x.bitcast(dt.uint8) for x in b]
+    ids = []
+    for d in dsts:
+        rid, pid = topo.addr(d, src)
+        ids.append(DstId(rid=rid, pnc=pid))
+    return RemoteDMATransfer(dst_ids=ids, dma_engine_mask=mask, remote_sem=sem, src=a, dsts=b)
+
+
+def helper_program(g, core, T, topo):
+    own = [c for c in T.cores if core in helpers_of(c, T, topo)]
+    if not own:
+        return
+    q = T.rank_of(own[0])
+    k = helpers_of(own[0], T, topo).index(core)
+    far, near = engine_sets(core, own[0], T, topo)
+    to = [T.cores[(q + i) % NR] for i in range(1, NR)][k::2]
+    calls = 0
+    for kind in "cs":
+        g.wait_ge(T.sem["ah" + kind], len(near))
+        g.remote_dma_fused([transfer(topo, core, to, bits(far), T.sem["a1" + kind], T["hp" + kind][:, 0:R1],
+                                     T["lr" + kind][:, R1 * q:R1 * q + R1], kind)], local_sem=T.sem.sent)
+        calls += 1
+    via = route2(q, 0)[1]
+    if k < len(via):
+        for kind in "cs":
+            g.wait_ge(T.sem["ah0" + kind], deal(near, len(via))[1][k])
+            g.remote_dma_fused([transfer(topo, core, [T.cores[via[k]]], bits(far), T.sem["a2" + kind], T["h0" + kind][:, 0:S],
+                                         T["l2" + kind][:, Z + S * q:Z + S * q + S], kind)], local_sem=T.sem.sent)
+            calls += 1
+    g.wait_ge(T.sem.sent, calls * len(far))
+
+
+def rank_program(g, core, T, topo):
+    q = T.rank_of(core)
+    if q is None:
+        helper_program(g, core, T, topo)
+        return
+    peers = [(q + i) % NR for i in range(1, NR)]
+    helpers = helpers_of(core, T, topo)
+    far, near = engine_sets(core, core, T, topo)
+    queue = {"V": g.vector, "S": g.scalar, "PE": g.tensor, "G": g, "Y": g.sync}
+    count = {"V": 0, "S": 0, "PE": 0, "G": 0}
+    clock = {e: {} for e in queue}
+    known = {}
+    hist = {}
+    final = {}
+    free_sems = list(DMAS)
+
+    def v(name, a=None, b=None, step=None, rows=(0, 128)):
+        return (name, rows, slice(a, b, step))
+
+    def ap(x):
+        return T[x[0]][x[1][0]:x[1][1], x[2]]
+
+    def cols(x):
+        return set(range(SCRATCH[x[0]][1][1])[x[2]])
+
+    def wait(e, tok):
+        sem, n = tok
+        if clock[e].get(sem, 0) >= n:
+            return
+        queue[e].wait_ge(T.sem[sem], n)
+        clock[e][sem] = n
+        for s2, n2 in known.get(tok, {}).items():
+            if clock[e].get(s2, 0) < n2:
+                clock[e][s2] = n2
+
+    def order(e, reads, writes):
+        toks = {}
+        for x, wr in [(x, False) for x in reads] + [(x, True) for x in writes]:
+            if x[0] not in SCRATCH:
+                continue
+            psum = SCRATCH[x[0]][0] == "psum"
+            cx = cols(x)
+            for e2, tok, wr2, rows, c2 in hist.get(x[0], []):
+                if psum and e2 != e:
+                    hit = True
+                elif psum and e == "PE":
+                    hit = False
+                else:
+                    hit = (wr or wr2) and rows[0] < x[1][1] and x[1][0] < rows[1] and not cx.isdisjoint(c2)
+                if hit and toks.get(tok[0], 0) < tok[1]:
+                    toks[tok[0]] = tok[1]
+        for sem in sorted(toks, key=lambda s: s == e):
+            wait(e, (sem, toks[sem]))
+
+    def note(e, tok, reads, writes):
+        known[tok] = dict(clock.get(e, {}))
+        final[tok[0]] = max(final.get(tok[0], 0), tok[1])
+        for x, wr in [(x, False) for x in reads] + [(x, True) for x in writes]:
+            if x[0] in SCRATCH:
+                hist.setdefault(x[0], []).append((e, tok, wr, x[1], cols(x)))
+
+    def op(e, reads, writes, call):
+        reads = [x for x in reads if isinstance(x, tuple)]
+        order(e, reads, writes)
+        count[e] += 1
+        call().then_inc(T.sem[e], 1)
+        note(e, (e, count[e]), reads, writes)
+
+    def sc(x):
+        return ap(x) if isinstance(x, tuple) else x
+
+    def dma(e, out, in_, codes=False):
+        order(e, [in_], [out])
+        sem = free_sems.pop(0)
+        a, b = ap(out), ap(in_)
+        if codes:
+            b = b.bitcast(dt.uint8)
+            if out[0] in SCRATCH:
+                a = a.bitcast(dt.uint8)
+        queue[e].dma_start(a, b).then_inc(T.sem[sem], 16)
+        known[(sem, 16)] = dict(clock[e])
+        final[sem] = 16
+        for x, wr in ((in_, False), (out, True)):
+            if x[0] in SCRATCH:
+                hist.setdefault(x[0], []).append(("dma", (sem, 16), wr, x[1], cols(x)))
+
+    def arrives(sem, n, views):
+        note("far", (sem, n), [], views)
+
+    def send(transfers, reads, n):
+        order("G", reads, [])
+        g.remote_dma_fused(transfers, local_sem=T.sem.sent)
+        final["sent"] = final.get("sent", 0) + n
+
+    def ts(out, in0, s1, op0, s2=None, op1=None):
+        if op1 is None:
+            op("V", [in0, s1], [out], lambda: g.vector.tensor_scalar(ap(out), ap(in0), sc(s1), None, op0))
+        else:
+            op("V", [in0, s1, s2], [out], lambda: g.vector.tensor_scalar(ap(out), ap(in0), sc(s1), sc(s2), op0, op1))
+
+    def tt(out, in0, in1, alu, off=None):
+        a = ap(in0) if off is None else ap(in0).indirect(ap(off))
+        op("V", [in0, in1, off], [out], lambda: g.vector.tensor_tensor(ap(out), a, ap(in1), alu))
+
+    def cp(out, in_, off=None):
+        a = ap(in_) if off is None else ap(in_).indirect(ap(off))
+        op("V", [in_, off], [out], lambda: g.vector.tensor_copy(ap(out), a))
+
+    def fill(out, c):
+        op("V", [], [out], lambda: g.vector.memset(ap(out), c))
+
+    def red(out, in_):
+        op("V", [in_], [out], lambda: g.vector.tensor_reduce(ap(out), ap(in_), AxisListType.X, ADD))
+
+    def act(out, in_, func, off=None, acc=None, **kw):
+        a = ap(in_) if off is None else ap(in_).indirect(ap(off))
+        k2 = {k: sc(x) for k, x in kw.items()}
+        if acc is not None:
+            k2["accum_out"] = ap(acc)
+        op("S", [in_, off] + list(kw.values()), [out] + ([acc] if acc else []), lambda: g.scalar.activation(ap(out), a, func, **k2))
+
+    def quant(name, a, b, tile, ta):
+        c, s, t = v(name + "c", a, b), v(name + "s", a, b), v(tile, ta, ta + 4 * (b - a))
+        op("V", [t], [c, s], lambda: g.vector.quantize_mx(ap(c), ap(s), ap(t)))
+
+    def mm(bank, w, wa, x, xa, n, start=True, stop=True):
+        wc, ws, xc, xs = v(w + "c", wa, wa + 128), v(w + "s", wa, wa + 128), v(x + "c", xa, xa + n), v(x + "s", xa, xa + n)
+        o = v("p%d" % bank, 0, n)
+        op("PE", [wc, ws, xc, xs], [o], lambda: g.tensor.matmul_mx(ap(o), ap(wc), ap(ws), ap(xc), ap(xs), start, stop))
+
+    def pick_c(out, at, n, win, a, b, off):
+        o, w = v(out + "c", at, at + n), v(win + "c", a, b)
+        op("V", [w, off], [o], lambda: g.vector.tensor_copy(ap(o).bitcast(dt.uint32), ap(w).bitcast(dt.uint32).indirect(ap(off))))
+
+    def pick_s(out, at, n, win, a, b, off, on="S"):
+        if on == "S":
+            act(v(out + "s", at, at + n), v(win + "s", a, b), AF.Copy, off=off)
+        else:
+            cp(v(out + "s", at, at + n), v(win + "s", a, b), off=off)
+
+    def iota(out, pattern, base=0, cm=0):
+        if SCRATCH[out[0]][2] == I32:
+            op("G", [], [out], lambda: g.iota(ap(out), pattern, base, cm))
+        else:
+            op("G", [], [out], lambda: g.iota(ap(out), pattern, base, cm, allow_small_or_imprecise_dtypes=True))
+
+    cf = lambda k: v("cf", k, k + 1)
+    dc = lambda k: v("dc", k, k + 1)
+    pb = lambda k, a, b, step=None, rows=(0, 128): v("p%d" % k, a, b, step, rows)
+    shift = lambda x, b: v("dh", 4 * x + b, 4 * x + b + 1)
+    E, WH, SEL, WA, WB, WD, W0 = 0, 512, 768, 896, 1024, 1152, 1280
+    IO, YT, LR, U32L, HXL, THL = 0, 128, 256, 368, 384, 448
+    oU16, oU32, oRA, oR4, oMQ = v("so", 0, 8), v("so", 8, 24), v("so", 24, 32), v("so", 32, 40), v("so", 40, 48)
+    oTH, oLA0, oLA1 = v("so", 112, 116), v("so", 116, 117), v("so", 118, 120)
+    lr0, lr0b, lr1 = v("lref", 0, 64), v("lref", 64, 80), v("lref", 80, 112)
+    io = lambda a, b: v("idx", IO + a, IO + b)
+
+    dma("Y", v("t1", 0, 64), v("r0"))
+    dma("S", v("t1", 64, 72), v("u", 0, 8))
+    fill(v("t1", 72, 512), 0.0)
+    dma("Y", v("tr", 0, 256), v("r1"))
+    dma("S", v("tr", 256, 1280), v("r2"))
+    dma("Y", v("tw"), v("w"))
+
+    iota(v("ci", 0, 1), [[0, 1]], 0, 1)
+    iota(io(0, 128), [[1, 128]])
+    iota(v("idx", YT, YT + 128), [[0, 8], [1, 4], [0, 4]])
+    iota(v("idx", LR + 80, LR + 112), [[32, 4], [1, 8]])
+
+    zeros = 4 * WH
+    fill(v("tk", zeros, zeros + 1024), 0.0)
+    act(v("tk", 0, 1024), v("tk", zeros, zeros + 1024), AF.Copy)
+    for k, m in ((1, 15), (2, 112), (3, 3), (4, 31), (5, 96), (6, 64), (9, 111)):
+        ts(v("ci", k, k + 1), v("ci", 0, 1), m, AND)
+    for k, sh, m in ((7, 2, 3), (8, 4, 3), (10, 2, 27)):
+        ts(v("ci", k, k + 1), v("ci", 0, 1), sh, SHR, m, AND)
+    cp(v("cf", 0, 11), v("ci", 0, 11))
+    act(v("tx0"), v("tk", zeros, zeros + 784), AF.Copy)
+    for k, src, mul, add in ((11, 1, 16.0, 16.0), (12, 3, 4.0, 0.0), (13, 1, 1.0, -16.0), (14, 3, 1.0, -16.0),
+                             (20, 2, -1.0, 0.0), (21, 6, -1.0, 0.0), (22, 5, -1.0, 0.0)):
+        act(cf(k), cf(src), AF.Identity, scale=mul, bias=add)
+    act(v("tx1"), v("tk", zeros, zeros + 576), AF.Copy)
+
+    quant("q1", 0, 128, "t1", 0)
+    for kind in "cs":
+        x = v("q1" + kind, 0, W1)
+        at = lambda r: v("l0" + kind, W1 * ((q - r - 1) % NR), W1 * ((q - r - 1) % NR) + W1)
+        send([transfer(topo, core, [T.cores[r] for r in peers], bits(far), T.sem["a0" + kind], ap(x), [ap(at(r)) for r in peers], kind)],
+             [x], len(far))
+        dma("Y", at(q), x, codes=kind == "c")
+        arrives("a0" + kind, len(far) * len(peers), [v("l0" + kind, 0, W1 * (NR - 1))])
+    dma("Y", v("l2c", 0, 2), v("q1c", 32, 34), codes=True)
+    dma("Y", v("l2s", 0, 2), v("q1s", 32, 34))
+
+    iota(v("idx", LR, LR + 64), [[16, 8], [1, 8]])
+    iota(v("idx", LR + 64, LR + 80), [[4, 2], [64, 2], [1, 4]])
+    iota(v("idx", U32L, U32L + 16), [[W1, 8], [0, 2]], P)
+    iota(v("idx", HXL, HXL + 64), [[4, 8], [0, 8]])
+    iota(v("idx", THL, THL + 4), [[32, 2], [4, 2]])
+
+    for t in range(4):
+        ts(v("tk", 4 * SEL + t, 4 * SEL + 512, 4), v("idx", YT, YT + 128), float(t), EQ)
+    fill(v("tk", 1024, 2048), 0.0)
+    for x in range(4):
+        ts(cf(16 + x), cf(8), float(x), EQ, cf(11), MUL)
+    quant("qr", 0, 320, "tr", 0)
+    for kind in "cs":
+        x = v("qr" + kind, 0, R1)
+        send([transfer(topo, core, helpers, bits(near), T.sem["ah" + kind], ap(x), ap(v("hp" + kind)), kind)], [x], len(near))
+        dma("Y", v("lr" + kind, R1 * q, R1 * q + R1), x, codes=kind == "c")
+        arrives("a1" + kind, len(far) * len(peers), [v("lr" + kind, R1 * r, R1 * r + R1) for r in peers])
+    for b in range(4):
+        ts(v("tk", 512 * b + b, 512 * b + 512, 4), io(0, 128), cf(0), EQ)
+    sel = v("tk", 4 * SEL, 4 * SEL + 512)
+    act(v("tk", 4 * W0, 4 * W0 + 512), sel, AF.Identity, scale=0.0, bias=cf(11))
+    for at, k in ((WA, 1), (WB, 2), (WD, 12)):
+        act(v("tk", 4 * at, 4 * at + 512), sel, AF.Identity, scale=cf(k))
+    for h in range(2):
+        for x in range(4):
+            a = 4 * WH + 512 * h + 128 * x + 64 * h
+            act(v("tk", a, a + 64), v("tk", 4 * SEL, 4 * SEL + 64), AF.Identity, scale=cf(16 + x))
+    ts(oR4, io(0, 8), 4.0, MUL, cf(7), ADD)
+    quant("qk", 0, 512, "tk", 0)
+    pick_c("r4", 0, 128, "q1", 0, 128, oR4)
+    pick_s("r4", 0, 128, "q1", 0, 128, oR4, on="V")
+    for b in range(4):
+        mm(b, "qk", E + 128 * b, "r4", 0, 128, True, False)
+        mm(b, "qk", E + 128 * b, "qr", 0, 128, False, True)
+    for b in range(4):
+        act(v("s0", b, 256, 4), pb(b, 0, 64), AF.Copy)
+    for out, a, b, k in ((lr0, 0, 64, 20), (lr0b, 64, 80, 21), (lr1, 80, 112, 22)):
+        act(out, v("idx", LR + a, LR + b), AF.Identity, bias=cf(k))
+    ts(oU16, io(0, 8), float(W1), MUL, float(P), ADD)
+    ts(v("so", 24, 25 + q), io(NR - 1 - q, NR), float(W1), MUL, cf(1), ADD)
+    if q < NR - 1:
+        ts(v("so", 25 + q, 32), io(0, NR - 1 - q), float(W1), MUL, cf(1), ADD)
+    cp(oU32, v("idx", U32L, U32L + 16))
+    ts(v("so", 48, 112), v("idx", HXL, HXL + 64), cf(3), ADD)
+    ts(v("diag"), io(0, 16), cf(1), EQ)
+    ts(v("thr0"), io(0, 16), cf(1), GE, TINY, MUL)
+    ts(oTH, v("idx", THL, THL + 4), cf(10), ADD)
+    for b in range(2):
+        ts(v("base1", 32 * b, 32 * b + 32), io(0, 32), cf(4), GE, TINY, MUL)
+    fill(oMQ, P)
+    fill(v("n2", 16, 32), 0.0)
+    ts(oLA1, io(0, 2), 16.0, MUL, cf(9), ADD)
+    cp(oLA0, cf(0))
+    ts(v("thra"), io(0, 128), cf(0), GE, TINY, MUL)
+    ts(v("plc"), io(Z // 16, Z // 16 + 16), 16.0, MUL, cf(1), ADD)
+    pick_c("mq", 0, 128, "q1", 0, 128, oMQ)
+    pick_s("mq", 0, 128, "q1", 0, 128, oMQ)
+    quant("qk", 896, 1408, "tk", 3584)
+    quant("qk", 512, 896, "tk", 2048)
+
+    def one_hot(out, ref, lcol, fcol):
+        ts(out, ref, lcol, EQ, fcol, MUL)
+
+    def spread_slots(bank):
+        mm(bank, "qk", W0, "x0", 4, 128)
+
+    def spread_parents(bank):
+        mm(bank, "qk", WH, "x0", 0, 128, True, False)
+        mm(bank, "qk", WH + 128, "x0", 2, 128, False, True)
+
+    def spread_round1(lcols, fcols, mcols, bank_v, bank_e, between):
+        for b in range(2):
+            one_hot(v("tx1", 32 * b, 32 * b + 32), lr1, lcols[b], fcols[b])
+        for b in range(2):
+            one_hot(v("tx1", 64 + 32 * b, 96 + 32 * b), lr1, lcols[b], mcols[b])
+        between()
+        quant("x1", 0, 144, "tx1", 0)
+        if bank_v is not None:
+            mm(bank_v, "qk", WA, "x1", 0, 128, True, False)
+            mm(bank_v, "qk", WB, "x1", 0, 128, False, True)
+        mm(bank_e, "qk", SEL, "x1", 16, 128, True, False)
+        mm(bank_e, "qk", WD, "x1", 0, 128, False, True)
+
+    pick_c("u16", 0, 128, "l0", 0, L0, oU16)
+    pick_c("ra", 0, 128, "l0", 0, L0, oRA)
+    pick_c("u32", 0, 256, "l0", 0, L0, oU32)
+    pick_s("u16", 0, 128, "l0", 0, L0, oU16)
+    pick_s("ra", 0, 128, "l0", 0, L0, oRA, on="V")
+    quant("qw", 0, 128, "tw", 0)
+    for b in range(2):
+        mm(b, "qk", E + 128 * b, "l0", 0, L0)
+    mm(4, "u16", 0, "ra", 0, 128)
+    mm(7, "mq", 0, "ra", 0, 128)
+    mm(6, "ra", 0, "q1", 0, 128)
+    for b in range(2, 4):
+        mm(b, "qk", E + 128 * b, "l0", 0, L0)
+    pick_s("u32", 0, 256, "l0", 0, L0, oU32)
+    for b in range(4):
+        act(v("dh", b, 32, 4), pb(b, P + 1, L0, W1), AF.Copy)
+    for h in range(2):
+        act(v("hx", 512 * h, 512 * h + 512), v("dh"), AF.Copy, off=v("so", 48 + 32 * h, 80 + 32 * h))
+    o0, o1 = P * q, P * q + P
+    tt(v("dm"), pb(4, o0, o1), v("diag"), MUL)
+    red(dc(0), v("dm"))
+    ts(v("da"), pb(7, 0, 128), pb(6, P, P + 1), SUB)
+    ts(v("d0"), pb(4, o0, o1), dc(0), SUB)
+    if o0 > 0:
+        ts(v("c0", 0, o0), pb(4, 0, o0), dc(0), GE)
+    if o1 < 128:
+        ts(v("c0", o1, 128), pb(4, o1, 128), dc(0), GT)
+    tt(v("c0", o0, o1), v("d0"), v("thr0"), GE)
+    red(dc(1), v("c0"))
+    red(dc(2), v("c0", o0, o1))
+    ts(dc(3), dc(1), M - 0.5, LT)
+    one_hot(v("tx0", 16, 272, 4), lr0, dc(2), dc(3))
+    one_hot(v("tx0", 0, 16), lr0b, dc(2), dc(3))
+    quant("x0", 0, 132, "tx0", 0)
+    spread_slots(5)
+    spread_parents(6)
+    tt(v("ca"), v("da"), v("thra"), GE)
+    ts(v("do0"), pb(5, 0, 64), cf(13), ADD, 0.0, MAX)
+
+    act(v("g2"), v("s0"), AF.Copy, off=v("do0", 48, 64))
+    for x in range(2):
+        for b in range(4):
+            act(v("tch", 768 + 128 * x + b, 896 + 128 * x, 4), v("g2", 128 * x + b, 128 * x + 128, 4), AF.Identity, bias=shift(6 + x, b))
+    act(v("ms"), pb(5, 0, 64), AF.Copy)
+    act(v("thd"), v("ms"), AF.Relu, off=oTH, scale=-HUGE, bias=HUGE)
+    act(v("dc", 4, 6), pb(6, 0, 2), AF.Copy)
+    act(v("dc", 6, 8), pb(6, 0, 2), AF.Sign)
+    act(v("junk", 0, 16), v("ca"), AF.Identity, off=oLA0, acc=dc(11))
+    act(v("junk", 336, 464), v("ca"), AF.Identity, acc=dc(10))
+    for h in range(2):
+        a, n = 512 * h, 512 - 256 * h
+        tt(v("tch", a, a + n), v("s0"), v("hx", a, a + n), ADD, off=v("do0", 32 * h, 32 * h + n // 16))
+        quant("ch", 128 * h, 128 * h + 128, "tch", 512 * h)
+        mm(2 * h, "u32", 128 * h, "ch", 128 * h, 128)
+        mm(2 * h + 1, "ch", 128 * h, "l0", 0, L0)
+
+    for b in range(2):
+        for x in range(4):
+            rows, c = (32 * x, 32 * x + 32), W1 * (4 * b + x) + P
+            ts(v("d1", 32 * b, 32 * b + 32, rows=rows), pb(2 * b, 32 * x, 32 * x + 32, rows=rows), pb(2 * b + 1, c, c + 1, rows=rows), SUB)
+        if b == 0:
+            tt(v("thr1"), v("thd"), v("base1"), MAX)
+    tt(v("c1"), v("d1"), v("thr1"), GE)
+    ts(dc(12), dc(10), M - 0.5, LT)
+    for b in range(2):
+        red(dc(8 + b), v("c1", 32 * b, 32 * b + 32))
+    one_hot(v("tx0", 272, 336), lr0, dc(11), dc(12))
+    spread_round1([dc(8), dc(9)], [dc(6), dc(7)], [dc(4), dc(5)], 4, 7, lambda: one_hot(v("tx0", 16, 272, 4), lr0, dc(11), dc(12)))
+    one_hot(v("tx0", 0, 16), lr0b, dc(11), dc(12))
+    quant("x0", 0, 196, "tx0", 0)
+    mm(5, "qk", WA, "x0", 68, 128, True, False)
+    mm(5, "qk", WB, "x0", 68, 128, False, True)
+    spread_slots(6)
+    ts(v("do1", 0, 16), pb(4, 0, 16), 0.0, ADD)
+    for h in range(2):
+        for pick in (pick_c, pick_s):
+            pick("pv", 128 * h, 128, "ch", 128 * h, 128 * h + 128, v("do1", 8 * h, 8 * h + 8))
+        if h == 0:
+            ts(v("do1", 16, 32), pb(7, 0, 16), cf(14), ADD, 0.0, MAX)
+            ts(v("do3", 0, 16), pb(5, 0, 16), 0.0, ADD)
+        for pick in (pick_c, pick_s):
+            pick("pe", 128 * h, 128, "qr", R1, 320, v("do1", 16 + 8 * h, 24 + 8 * h))
+        if h == 0:
+            act(v("m4"), pb(6, 0, 64), AF.Identity, scale=0.25)
+        for b in range(4):
+            mm(4 * h + b, "qk", E + 128 * b, "pv", 128 * h, 128, True, False)
+        for b in range(4):
+            mm(4 * h + b, "qk", E + 128 * b, "pe", 128 * h, 128, False, True)
+
+    for h in range(2):
+        for b in range(3):
+            tt(v("tgr", 512 * h + b, 512 * h + 512, 4), pb(4 * h + b, 0, 128), v("hx", 512 * h + b, 512 * h + 512, 4), ADD)
+        for x in range(4):
+            a = 512 * h + 128 * x
+            act(v("tgr", a + 3, a + 128, 4), pb(4 * h + 3, 32 * x, 32 * x + 32), AF.Identity, bias=shift(4 * h + x, 3))
+        if h == 0:
+            ts(v("do3", 16, 32), v("do3", 0, 16), 4.0, MUL, cf(3), ADD)
+        quant("gr", 128 * h, 128 * h + 128, "tgr", 512 * h)
+        direct, via = route2(q, h)
+        for kind in "cs":
+            land = ap(v("l2" + kind, Z + S * q, Z + S * q + S))
+            block = lambda r: v("gr" + kind, S * ((r - q - 1) % NR), S * ((r - q - 1) % NR) + S)
+            masks, nd = deal(far, len(direct), kind == "s")
+            tr = [transfer(topo, core, [T.cores[r]], m, T.sem["a2" + kind], ap(block(r)), land, kind) for r, m in zip(direct, masks)]
+            if via:
+                masks, nh = deal(near, len(via))
+                nd = nd + nh
+                tr += [transfer(topo, core, [c], m, T.sem["ah0" + kind], ap(block(r)), ap(v("h0" + kind)), kind)
+                       for r, c, m in zip(via, helpers, masks)]
+            send(tr, [block(r) for r in direct + via], sum(nd))
+            if h == 1:
+                dma("Y", v("l2" + kind, Z + S * q, Z + S * q + S), block(q), codes=kind == "c")
+    n2 = 0
+    for h in range(2):
+        direct, via = route2(q, h)
+        n2 += sum(deal(far, len(direct))[1]) + len(far) * len(via)
+    for kind in "cs":
+        arrives("a2" + kind, n2, [v("l2" + kind, Z + S * r, Z + S * r + S) for r in peers])
+
+    spread_parents(2)
+    for h in range(2):
+        for pick in (pick_c, pick_s):
+            pick("av", 128 * h, 128, "ra", 0, 128, v("do3", 8 * h, 8 * h + 8))
+        for pick in (pick_c, pick_s):
+            pick("ae", 128 * h, 128, "lr", 0, NR * R1, v("do3", 16 + 8 * h, 24 + 8 * h))
+        if h == 0:
+            act(v("dc", 14, 16), pb(2, 0, 2), AF.Copy)
+            act(v("dc", 16, 18), pb(2, 0, 2), AF.Sign)
+        for b in range(4):
+            mm(4 - 4 * h + b, "qk", E + 128 * b, "av", 128 * h, 128, True, False)
+        for b in range(4):
+            mm(4 - 4 * h + b, "qk", E + 128 * b, "ae", 128 * h, 128, False, True)
+    for h in range(2):
+        for b in range(4):
+            out, src = v("ta1", 512 * h + b, 512 * h + 512, 4), pb(4 - 4 * h + b, 0, 128)
+            if b % 2 == 0:
+                act(out, src, AF.Identity, bias=shift(NR - 1, b))
+            else:
+                ts(out, src, shift(NR - 1, b), ADD)
+        if h == 0:
+            for k in range(2):
+                ts(v("n1", k, 256, 4), v("m4"), float(k - 4), ADD, -1.0, MAX)
+        quant("l1", 128 * h, 128 * h + 128, "ta1", 512 * h)
+        if h == 0:
+            for k in range(2, 4):
+                ts(v("n1", k, 256, 4), v("m4"), float(k - 4), ADD, -1.0, MAX)
+            dma("Y", v("nm", 0, 256, rows=(0, 1)), v("n1", rows=(0, 1)))
+            mm(5, "l1", 0, "q1", 0, 128)
+    act(v("cap"), v("n1"), AF.Identity, scale=CAPV, bias=0.5 * CAPV)
+
+    mm(4, "mq", 0, "l1", 0, 256)
+    mm(6, "l1", 128, "q1", 0, 128)
+    mm(3, "qw", 0, "l1", 0, 256)
+    for b in range(2):
+        act(dc(26 + b), pb(5 + b, P, P + 1), AF.Identity, scale=-1.0)
+        act(dc(28 + b), pb(5 + b, P, P + 1), AF.Copy)
+    tt(v("am"), pb(4, 0, 256), v("cap"), MIN)
+    for b in range(2):
+        o = 128 * (1 - b)
+        act(v("db", 128 * b, 128 * b + 128), v("am", 128 * b, 128 * b + 128), AF.Identity, bias=dc(26 + b))
+        ts(v("cb", 256 * b + o, 256 * b + o + 128), v("am", o, o + 128), dc(28 + b), GE if b else GT)
+    for b in range(2):
+        o = 256 * b + 128 * (1 - b)
+        act(v("junk", 80 + 128 * b, 208 + 128 * b), v("cb", o, o + 128), AF.Identity, acc=dc(30 + b))
+    for b in range(2):
+        own = v("cb", 384 * b, 384 * b + 128)
+        tt(own, v("db", 128 * b, 128 * b + 128), v("thra"), GE)
+        act(v("junk", 16 + 32 * b, 48 + 32 * b), own, AF.Identity, off=oLA1, acc=dc(20 + b))
+        if b == 0:
+            act(v("junk", 464, 592), own, AF.Identity, acc=dc(18))
+        else:
+            red(dc(19), own)
+    act(v("val"), v("n1"), AF.Sign, bias=1.0)
+    for b in range(2):
+        ts(dc(22 + b), dc(18 + b), dc(30 + b), ADD, M - 1.0, SUB)
+    for b in range(2):
+        ts(dc(24 + b), dc(22 + b), 128.0, MUL, dc(20 + b), MAX)
+    spread_round1([dc(24), dc(25)], [dc(16), dc(17)], [dc(14), dc(15)], None, 4, lambda: None)
+    tt(v("y0"), pb(3, 0, 256), v("val"), MUL)
+    dma("Y", v("y", 0, 256), v("y0"))
+    ts(v("v2"), pb(4, 0, 16), 0.0, GT)
+    ts(v("n2", 0, 16), pb(4, 0, 16), cf(14), ADD, -1.0, MAX)
+    tt(v("o2"), v("v2"), v("plc"), MUL)
+    a, b = v("n2t", rows=(0, 32)), v("n2", rows=(0, 32))
+    op("V", [b], [a], lambda: g.vector.transpose(ap(a), ap(b)))
+    cp(v("do2"), v("o2"))
+    dma("Y", v("nm", 256, 512, rows=(0, 1)), v("n2t", 0, 16, rows=(0, 16)))
+
+    for h in range(2):
+        pick_c("fin", 128 * h, 128, "l2", 0, Z + 256, v("do2", 8 * h, 8 * h + 8))
+    dma("Y", v("oc"), v("finc"), codes=True)
+    for h in range(2):
+        pick_s("fin", 128 * h, 128, "l2", 0, Z + 256, v("do2", 8 * h, 8 * h + 8), on="SV"[h])
+    mm(5, "qw", 0, "fin", 0, 128)
+    mm(6, "qw", 0, "fin", 128, 128)
+    for k in range(2):
+        dma("Y", v("osc", rows=(4 * k, 4 * k + 4)), v("fins", rows=(32 * k, 32 * k + 4)))
+    act(v("y1", 0, 128), pb(5, 0, 128), AF.Copy)
+    cp(v("y1", 128, 256), pb(6, 0, 128))
+    dma("S", v("y", 256, 384), v("y1", 0, 128))
+    dma("Y", v("y", 384, 512), v("y1", 128, 256))
+    for k in range(2, 4):
+        dma("S", v("osc", rows=(4 * k, 4 * k + 4)), v("fins", rows=(32 * k, 32 * k + 4)))
+
+    for sem, n in final.items():
+        wait("G", (sem, n))

@@ -12,25 +12,25 @@ Q4, U8, BF, F32, I32, U16 = "float8_e4m3fn_x4", "uint8", "bfloat16", "float32", 
 
 SCRATCH = {}
 for _n, _w in (("q1", 128), ("qr", 320), ("qw", 128), ("qk", 1408), ("l0", L0), ("u16", 128), ("u32", 256), ("ra", 128),
-               ("r4", 128), ("mq", 128), ("x0", 196), ("x1", 144), ("ch", 256), ("hp", R1), ("lr", NR * R1), ("l1", 256),
-               ("pv", 256), ("pe", 256), ("av", 256), ("ae", 256), ("gr", 256), ("h0", S), ("l2", Z + 256), ("fin", 256)):
+               ("r4", 128), ("mq", 128), ("x0", 196), ("x1", 144), ("x2", 144), ("ch", 256), ("hp", R1), ("lr", 4 * R1), ("l1", 256),
+               ("pv", 256), ("pe", 256), ("av", 128), ("ae", 128), ("gr", 256), ("h0", S), ("l2", Z + 256), ("fin", 256)):
     SCRATCH[_n + "c"] = ("sbuf", [128, _w], Q4)
     SCRATCH[_n + "s"] = ("sbuf", [128, _w], U8)
 for _n, _w, _d in (("t1", 512, BF), ("tr", 1280, BF), ("tw", 512, BF), ("tk", 5632, BF), ("tx0", 784, BF), ("tx1", 576, BF),
-                   ("tch", 1024, BF), ("tgr", 1024, BF), ("ta1", 1024, BF), ("ci", 16, I32), ("cf", 32, F32), ("idx", 512, F32),
-                   ("so", 128, U16), ("do0", 64, U16), ("do1", 32, U16), ("do2", 16, U16), ("do3", 32, U16),
+                   ("tch", 1024, BF), ("tgr", 1024, BF), ("ta1", 512, BF), ("ci", 16, I32), ("cf", 32, F32), ("idx", 512, F32),
+                   ("so", 128, U16), ("do0", 64, U16), ("do1", 32, U16), ("do2", 16, U16), ("do3", 16, U16),
                    ("thr0", 16, BF), ("thra", 128, BF), ("base1", 64, BF), ("diag", 16, F32), ("lref", 112, F32), ("plc", 16, F32),
-                   ("s0", 256, F32), ("dh", 32, F32), ("hx", 1024, F32), ("dc", 32, F32), ("dm", 16, F32), ("g2", 256, F32),
+                   ("s0", 256, F32), ("dh", 32, F32), ("hx", 1024, F32), ("dc", 40, F32), ("dm", 16, F32), ("g2", 256, F32),
                    ("d0", 16, BF), ("c0", 128, BF), ("ms", 64, F32), ("thd", 64, BF), ("thr1", 64, BF), ("d1", 64, BF), ("c1", 64, BF),
-                   ("da", 128, BF), ("ca", 128, BF), ("junk", 592, BF), ("m4", 64, F32), ("n1", 256, F32), ("cap", 256, F32),
+                   ("da", 128, BF), ("ca", 128, BF), ("junk", 720, BF), ("m4", 64, F32), ("n1", 256, F32), ("cap", 256, F32),
                    ("val", 256, F32), ("am", 256, F32), ("db", 256, BF), ("cb", 512, BF), ("n2", 32, F32), ("n2t", 32, F32),
-                   ("v2", 16, F32), ("o2", 16, F32), ("y0", 256, F32), ("y1", 256, F32)):
+                   ("o2", 16, F32), ("y0", 256, F32), ("y1", 256, F32)):
     SCRATCH[_n] = ("sbuf", [128, _w], _d)
 for _k in range(8):
     SCRATCH["p%d" % _k] = ("psum", [128, 512], F32)
 
 DMAS = ["ld%d" % _k for _k in range(24)]
-SEMAPHORES = ["V", "S", "PE", "G", "sent", "a0c", "a0s", "ahc", "ahs", "a1c", "a1s", "a2c", "a2s", "ah0c", "ah0s"] + DMAS
+SEMAPHORES = ["V", "S", "PE", "G", "sent", "a0c", "a0s", "ahc", "ahs", "a1c", "a1s", "a2c", "a2s", "a3c", "a3s", "ah0c", "ah0s"] + DMAS
 
 ADD, SUB, MUL, MAX, MIN = AluOpType.add, AluOpType.subtract, AluOpType.mult, AluOpType.max, AluOpType.min
 GE, GT, LT, EQ = AluOpType.is_ge, AluOpType.is_gt, AluOpType.is_lt, AluOpType.is_equal
@@ -68,6 +68,10 @@ def engine_sets(src, c, T, topo):
     return far, [e for e in near if e not in far]
 
 
+def peers_of(q, same):
+    return [r for r in [(q + i) % NR for i in range(1, NR)] if (r // 4 == q // 4) == same]
+
+
 def route2(q, half):
     to = [(q + i) % NR for i in range(1, NR)][4 * half:4 * half + 4]
     n = DIRECT if half == 0 else len(to)
@@ -92,12 +96,12 @@ def helper_program(g, core, T, topo):
     q = T.rank_of(own[0])
     k = helpers_of(own[0], T, topo).index(core)
     far, near = engine_sets(core, own[0], T, topo)
-    to = [T.cores[(q + i) % NR] for i in range(1, NR)][k::2]
+    to = [T.cores[r] for r in peers_of(q, False)][k::2]
     calls = 0
     for kind in "cs":
         g.wait_ge(T.sem["ah" + kind], len(near))
         g.remote_dma_fused([transfer(topo, core, to, bits(far), T.sem["a1" + kind], T["hp" + kind][:, 0:R1],
-                                     T["lr" + kind][:, R1 * q:R1 * q + R1], kind)], local_sem=T.sem.sent)
+                                     T["lr" + kind][:, R1 * (q % 4):R1 * (q % 4) + R1], kind)], local_sem=T.sem.sent)
         calls += 1
     via = route2(q, 0)[1]
     if k < len(via):
@@ -265,6 +269,7 @@ def rank_program(g, core, T, topo):
     oTH, oLA0, oLA1 = v("so", 112, 116), v("so", 116, 117), v("so", 118, 120)
     lr0, lr0b, lr1 = v("lref", 0, 64), v("lref", 64, 80), v("lref", 80, 112)
     io = lambda a, b: v("idx", IO + a, IO + b)
+    hh = 1 - q // 4
 
     dma("Y", v("t1", 0, 64), v("r0"))
     dma("S", v("t1", 64, 72), v("u", 0, 8))
@@ -318,8 +323,7 @@ def rank_program(g, core, T, topo):
     for kind in "cs":
         x = v("qr" + kind, 0, R1)
         send([transfer(topo, core, helpers, bits(near), T.sem["ah" + kind], ap(x), ap(v("hp" + kind)), kind)], [x], len(near))
-        dma("Y", v("lr" + kind, R1 * q, R1 * q + R1), x, codes=kind == "c")
-        arrives("a1" + kind, len(far) * len(peers), [v("lr" + kind, R1 * r, R1 * r + R1) for r in peers])
+        arrives("a1" + kind, len(far) * 4, [v("lr" + kind)])
     for b in range(4):
         ts(v("tk", 512 * b + b, 512 * b + 512, 4), io(0, 128), cf(0), EQ)
     sel = v("tk", 4 * SEL, 4 * SEL + 512)
@@ -373,18 +377,9 @@ def rank_program(g, core, T, topo):
         mm(bank, "qk", WH, "x0", 0, 128, True, False)
         mm(bank, "qk", WH + 128, "x0", 2, 128, False, True)
 
-    def spread_round1(lcols, fcols, mcols, bank_v, bank_e, between):
-        for b in range(2):
-            one_hot(v("tx1", 32 * b, 32 * b + 32), lr1, lcols[b], fcols[b])
-        for b in range(2):
-            one_hot(v("tx1", 64 + 32 * b, 96 + 32 * b), lr1, lcols[b], mcols[b])
-        between()
-        quant("x1", 0, 144, "tx1", 0)
-        if bank_v is not None:
-            mm(bank_v, "qk", WA, "x1", 0, 128, True, False)
-            mm(bank_v, "qk", WB, "x1", 0, 128, False, True)
-        mm(bank_e, "qk", SEL, "x1", 16, 128, True, False)
-        mm(bank_e, "qk", WD, "x1", 0, 128, False, True)
+    def spread_numbers(x, bank):
+        mm(bank, "qk", SEL, x, 16, 128, True, False)
+        mm(bank, "qk", WD, x, 0, 128, False, True)
 
     pick_c("u16", 0, 128, "l0", 0, L0, oU16)
     pick_c("ra", 0, 128, "l0", 0, L0, oRA)
@@ -441,6 +436,15 @@ def rank_program(g, core, T, topo):
         quant("ch", 128 * h, 128 * h + 128, "tch", 512 * h)
         mm(2 * h, "u32", 128 * h, "ch", 128 * h, 128)
         mm(2 * h + 1, "ch", 128 * h, "l0", 0, L0)
+    mates = peers_of(q, True)
+    for kind in "cs":
+        land = v("l1" + kind, S * q, S * q + S)
+        block = lambda r: v("ch" + kind, S * ((r - q - 1) % NR), S * ((r - q - 1) % NR) + S)
+        masks, nd = deal(far, len(mates), kind == "s")
+        send([transfer(topo, core, [T.cores[r]], m, T.sem["a3" + kind], ap(block(r)), ap(land), kind) for r, m in zip(mates, masks)],
+             [block(r) for r in mates], sum(nd))
+        dma("Y", land, block(q), codes=kind == "c")
+        arrives("a3" + kind, sum(nd[peers_of(r, True).index(q)] for r in mates), [v("l1" + kind, S * r, S * r + S) for r in mates])
 
     for b in range(2):
         for x in range(4):
@@ -453,7 +457,15 @@ def rank_program(g, core, T, topo):
     for b in range(2):
         red(dc(8 + b), v("c1", 32 * b, 32 * b + 32))
     one_hot(v("tx0", 272, 336), lr0, dc(11), dc(12))
-    spread_round1([dc(8), dc(9)], [dc(6), dc(7)], [dc(4), dc(5)], 4, 7, lambda: one_hot(v("tx0", 16, 272, 4), lr0, dc(11), dc(12)))
+    for b in range(2):
+        one_hot(v("tx1", 32 * b, 32 * b + 32), lr1, dc(8 + b), dc(6 + b))
+    for b in range(2):
+        one_hot(v("tx1", 64 + 32 * b, 96 + 32 * b), lr1, dc(8 + b), dc(4 + b))
+    one_hot(v("tx0", 16, 272, 4), lr0, dc(11), dc(12))
+    quant("x1", 0, 144, "tx1", 0)
+    mm(4, "qk", WA, "x1", 0, 128, True, False)
+    mm(4, "qk", WB, "x1", 0, 128, False, True)
+    spread_numbers("x1", 7)
     one_hot(v("tx0", 0, 16), lr0b, dc(11), dc(12))
     quant("x0", 0, 196, "tx0", 0)
     mm(5, "qk", WA, "x0", 68, 128, True, False)
@@ -465,7 +477,7 @@ def rank_program(g, core, T, topo):
             pick("pv", 128 * h, 128, "ch", 128 * h, 128 * h + 128, v("do1", 8 * h, 8 * h + 8))
         if h == 0:
             ts(v("do1", 16, 32), pb(7, 0, 16), cf(14), ADD, 0.0, MAX)
-            ts(v("do3", 0, 16), pb(5, 0, 16), 0.0, ADD)
+            ts(v("do3", 0, 8), pb(5, 8 * hh, 8 * hh + 8), -64.0 * hh, ADD, 0.0, MAX)
         for pick in (pick_c, pick_s):
             pick("pe", 128 * h, 128, "qr", R1, 320, v("do1", 16 + 8 * h, 24 + 8 * h))
         if h == 0:
@@ -482,7 +494,10 @@ def rank_program(g, core, T, topo):
             a = 512 * h + 128 * x
             act(v("tgr", a + 3, a + 128, 4), pb(4 * h + 3, 32 * x, 32 * x + 32), AF.Identity, bias=shift(4 * h + x, 3))
         if h == 0:
-            ts(v("do3", 16, 32), v("do3", 0, 16), 4.0, MUL, cf(3), ADD)
+            ts(v("do3", 8, 16), v("do3", 0, 8), 4.0, MUL, cf(3), ADD)
+            pick_s("av", 0, 128, "ra", 64 * hh, 64 * hh + 64, v("do3", 0, 8))
+        else:
+            pick_c("av", 0, 128, "ra", 64 * hh, 64 * hh + 64, v("do3", 0, 8))
         quant("gr", 128 * h, 128 * h + 128, "tgr", 512 * h)
         direct, via = route2(q, h)
         for kind in "cs":
@@ -505,41 +520,30 @@ def rank_program(g, core, T, topo):
     for kind in "cs":
         arrives("a2" + kind, n2, [v("l2" + kind, Z + S * r, Z + S * r + S) for r in peers])
 
-    spread_parents(2)
-    for h in range(2):
-        for pick in (pick_c, pick_s):
-            pick("av", 128 * h, 128, "ra", 0, 128, v("do3", 8 * h, 8 * h + 8))
-        for pick in (pick_c, pick_s):
-            pick("ae", 128 * h, 128, "lr", 0, NR * R1, v("do3", 16 + 8 * h, 24 + 8 * h))
-        if h == 0:
-            act(v("dc", 14, 16), pb(2, 0, 2), AF.Copy)
-            act(v("dc", 16, 18), pb(2, 0, 2), AF.Sign)
-        for b in range(4):
-            mm(4 - 4 * h + b, "qk", E + 128 * b, "av", 128 * h, 128, True, False)
-        for b in range(4):
-            mm(4 - 4 * h + b, "qk", E + 128 * b, "ae", 128 * h, 128, False, True)
-    for h in range(2):
-        for b in range(4):
-            out, src = v("ta1", 512 * h + b, 512 * h + 512, 4), pb(4 - 4 * h + b, 0, 128)
-            if b % 2 == 0:
-                act(out, src, AF.Identity, bias=shift(NR - 1, b))
-            else:
-                ts(out, src, shift(NR - 1, b), ADD)
-        if h == 0:
-            for k in range(2):
-                ts(v("n1", k, 256, 4), v("m4"), float(k - 4), ADD, -1.0, MAX)
-        quant("l1", 128 * h, 128 * h + 128, "ta1", 512 * h)
-        if h == 0:
-            for k in range(2, 4):
-                ts(v("n1", k, 256, 4), v("m4"), float(k - 4), ADD, -1.0, MAX)
-            dma("Y", v("nm", 0, 256, rows=(0, 1)), v("n1", rows=(0, 1)))
-            mm(5, "l1", 0, "q1", 0, 128)
+    for pick in (pick_c, pick_s):
+        pick("ae", 0, 128, "lr", 0, 4 * R1, v("do3", 8, 16))
+    for b in range(4):
+        mm(b, "qk", E + 128 * b, "av", 0, 128, True, False)
+    for b in range(4):
+        mm(b, "qk", E + 128 * b, "ae", 0, 128, False, True)
+    spread_parents(7)
+    mm(6 - hh, "l1", 128 * (1 - hh), "q1", 0, 128)
+    for k in range(4):
+        ts(v("n1", k, 256, 4), v("m4"), float(k - 4), ADD, -1.0, MAX)
+    dma("Y", v("nm", 0, 256, rows=(0, 1)), v("n1", rows=(0, 1)))
+    for b in range(4):
+        out, src = v("ta1", b, 512, 4), pb(b, 0, 128)
+        if b % 2 == 0:
+            act(out, src, AF.Identity, bias=shift(NR - 1, b))
+        else:
+            ts(out, src, shift(NR - 1, b), ADD)
     act(v("cap"), v("n1"), AF.Identity, scale=CAPV, bias=0.5 * CAPV)
+    quant("l1", 128 * hh, 128 * hh + 128, "ta1", 0)
 
     mm(4, "mq", 0, "l1", 0, 256)
-    mm(6, "l1", 128, "q1", 0, 128)
+    mm(5 + hh, "l1", 128 * hh, "q1", 0, 128)
     mm(3, "qw", 0, "l1", 0, 256)
-    for b in range(2):
+    for b in (1 - hh, hh):
         act(dc(26 + b), pb(5 + b, P, P + 1), AF.Identity, scale=-1.0)
         act(dc(28 + b), pb(5 + b, P, P + 1), AF.Copy)
     tt(v("am"), pb(4, 0, 256), v("cap"), MIN)
@@ -550,45 +554,47 @@ def rank_program(g, core, T, topo):
     for b in range(2):
         o = 256 * b + 128 * (1 - b)
         act(v("junk", 80 + 128 * b, 208 + 128 * b), v("cb", o, o + 128), AF.Identity, acc=dc(30 + b))
+    act(v("dc", 32, 34), v("dc", 30, 32), AF.Identity, bias=1.0 - M)
+    act(v("dc", 14, 16), pb(7, 0, 2), AF.Copy)
+    act(v("dc", 16, 18), pb(7, 0, 2), AF.Sign)
     for b in range(2):
         own = v("cb", 384 * b, 384 * b + 128)
         tt(own, v("db", 128 * b, 128 * b + 128), v("thra"), GE)
         act(v("junk", 16 + 32 * b, 48 + 32 * b), own, AF.Identity, off=oLA1, acc=dc(20 + b))
-        if b == 0:
-            act(v("junk", 464, 592), own, AF.Identity, acc=dc(18))
-        else:
-            red(dc(19), own)
     act(v("val"), v("n1"), AF.Sign, bias=1.0)
     for b in range(2):
-        ts(dc(22 + b), dc(18 + b), dc(30 + b), ADD, M - 1.0, SUB)
+        own, run, nil = v("cb", 384 * b, 384 * b + 128), v("junk", 464 + 128 * b, 592 + 128 * b), v("tx1", 256, 384)
+        op("V", [own, nil, dc(32 + b)], [run], lambda: g.vector.tensor_tensor_scan(ap(run), ap(own), ap(nil), ap(dc(32 + b)), ADD, ADD))
     for b in range(2):
-        ts(dc(24 + b), dc(22 + b), 128.0, MUL, dc(20 + b), MAX)
-    spread_round1([dc(24), dc(25)], [dc(16), dc(17)], [dc(14), dc(15)], None, 4, lambda: None)
+        ts(dc(24 + b), v("junk", 591 + 128 * b, 592 + 128 * b), 128.0, MUL, dc(20 + b), MAX)
+    for b in range(2):
+        one_hot(v("tx1", 32 * b, 32 * b + 32), lr1, dc(24 + b), dc(16 + b))
+    quant("x1", 0, 128, "tx1", 0)
+    mm(4, "qk", SEL, "x1", 0, 128)
     tt(v("y0"), pb(3, 0, 256), v("val"), MUL)
     dma("Y", v("y", 0, 256), v("y0"))
-    ts(v("v2"), pb(4, 0, 16), 0.0, GT)
-    ts(v("n2", 0, 16), pb(4, 0, 16), cf(14), ADD, -1.0, MAX)
-    tt(v("o2"), v("v2"), v("plc"), MUL)
-    a, b = v("n2t", rows=(0, 32)), v("n2", rows=(0, 32))
-    op("V", [b], [a], lambda: g.vector.transpose(ap(a), ap(b)))
+    tt(v("o2"), pb(4, 0, 16), v("plc"), MUL)
+    for b in range(2):
+        one_hot(v("tx1", 64 + 32 * b, 96 + 32 * b), lr1, dc(24 + b), dc(14 + b))
     cp(v("do2"), v("o2"))
-    dma("Y", v("nm", 256, 512, rows=(0, 1)), v("n2t", 0, 16, rows=(0, 16)))
+    quant("x2", 0, 144, "tx1", 0)
+    spread_numbers("x2", 7)
 
     for h in range(2):
         pick_c("fin", 128 * h, 128, "l2", 0, Z + 256, v("do2", 8 * h, 8 * h + 8))
+        pick_s("fin", 128 * h, 128, "l2", 0, Z + 256, v("do2", 8 * h, 8 * h + 8))
+        mm(5 + h, "qw", 0, "fin", 128 * h, 128)
     dma("Y", v("oc"), v("finc"), codes=True)
-    for h in range(2):
-        pick_s("fin", 128 * h, 128, "l2", 0, Z + 256, v("do2", 8 * h, 8 * h + 8), on="SV"[h])
-    mm(5, "qw", 0, "fin", 0, 128)
-    mm(6, "qw", 0, "fin", 128, 128)
-    for k in range(2):
-        dma("Y", v("osc", rows=(4 * k, 4 * k + 4)), v("fins", rows=(32 * k, 32 * k + 4)))
-    act(v("y1", 0, 128), pb(5, 0, 128), AF.Copy)
-    cp(v("y1", 128, 256), pb(6, 0, 128))
-    dma("S", v("y", 256, 384), v("y1", 0, 128))
-    dma("Y", v("y", 384, 512), v("y1", 128, 256))
-    for k in range(2, 4):
-        dma("S", v("osc", rows=(4 * k, 4 * k + 4)), v("fins", rows=(32 * k, 32 * k + 4)))
+    ts(v("n2", 0, 16), pb(7, 0, 16), cf(14), ADD, -1.0, MAX)
+    cp(v("y1", 0, 128), pb(5, 0, 128))
+    a, b = v("n2t", rows=(0, 32)), v("n2", rows=(0, 32))
+    op("V", [b], [a], lambda: g.vector.transpose(ap(a), ap(b)))
+    dma("Y", v("y", 256, 384), v("y1", 0, 128))
+    act(v("y1", 128, 256), pb(6, 0, 128), AF.Copy)
+    dma("S", v("y", 384, 512), v("y1", 128, 256))
+    dma("Y", v("nm", 256, 512, rows=(0, 1)), v("n2t", 0, 16, rows=(0, 16)))
+    for k in range(4):
+        dma("YS"[k % 2], v("osc", rows=(4 * k, 4 * k + 4)), v("fins", rows=(32 * k, 32 * k + 4)))
 
     for sem, n in final.items():
         wait("G", (sem, n))

@@ -6,31 +6,30 @@ W1 = P + 2
 L0 = NR * W1
 R1 = 4 * P
 Z = 32
-DIRECT = 2
 TINY, HUGE, CAPV = 2.0 ** -110, 2.0 ** 90, 2.0 ** 80
 Q4, U8, BF, F32, I32, U16 = "float8_e4m3fn_x4", "uint8", "bfloat16", "float32", "int32", "uint16"
 
 SCRATCH = {}
 for _n, _w in (("q1", 128), ("qr", 320), ("qw", 128), ("qk", 1408), ("l0", L0), ("u16", 128), ("u32", 256), ("ra", 128),
-               ("r4", 128), ("mq", 128), ("x0", 196), ("x1", 144), ("x2", 144), ("ch", 256), ("hp", R1), ("lr", 4 * R1), ("l1", 256),
-               ("pv", 256), ("pe", 256), ("av", 128), ("ae", 128), ("gr", 256), ("h0", S), ("l2", Z + 256), ("fin", 256)):
+               ("r4", 128), ("mq", 128), ("x0", 132), ("x1", 144), ("x2", 144), ("ch", 256), ("l1", 256), ("h1", 2 * S), ("h2", S),
+               ("pv", 256), ("pe", 256), ("gr", 256), ("l2", Z + 256), ("fin", 256)):
     SCRATCH[_n + "c"] = ("sbuf", [128, _w], Q4)
     SCRATCH[_n + "s"] = ("sbuf", [128, _w], U8)
-for _n, _w, _d in (("t1", 512, BF), ("tr", 1280, BF), ("tw", 512, BF), ("tk", 5632, BF), ("tx0", 784, BF), ("tx1", 576, BF),
-                   ("tch", 1024, BF), ("tgr", 1024, BF), ("ta1", 512, BF), ("ci", 16, I32), ("cf", 32, F32), ("idx", 512, F32),
-                   ("so", 128, U16), ("do0", 64, U16), ("do1", 32, U16), ("do2", 16, U16), ("do3", 16, U16),
+for _n, _w, _d in (("t1", 512, BF), ("tr", 1280, BF), ("tw", 512, BF), ("tk", 5632, BF), ("tx0", 528, BF), ("tx1", 576, BF),
+                   ("tch", 1024, BF), ("tgr", 1024, BF), ("ci", 16, I32), ("cf", 32, F32), ("idx", 512, F32),
+                   ("so", 128, U16), ("do0", 64, U16), ("do1", 32, U16), ("do2", 16, U16),
                    ("thr0", 16, BF), ("thra", 128, BF), ("base1", 64, BF), ("diag", 16, F32), ("lref", 112, F32), ("plc", 16, F32),
                    ("s0", 256, F32), ("dh", 32, F32), ("hx", 1024, F32), ("dc", 40, F32), ("dm", 16, F32), ("g2", 256, F32),
                    ("d0", 16, BF), ("c0", 128, BF), ("ms", 64, F32), ("thd", 64, BF), ("thr1", 64, BF), ("d1", 64, BF), ("c1", 64, BF),
                    ("da", 128, BF), ("ca", 128, BF), ("junk", 720, BF), ("m4", 64, F32), ("n1", 256, F32), ("cap", 256, F32),
                    ("val", 256, F32), ("am", 256, F32), ("db", 256, BF), ("cb", 512, BF), ("n2", 32, F32), ("n2t", 32, F32),
-                   ("o2", 16, F32), ("y0", 256, F32), ("y1", 256, F32)):
+                   ("o2", 16, F32), ("y0", 256, F32), ("y1", 256, F32), ("n1p", 256, F32)):
     SCRATCH[_n] = ("sbuf", [128, _w], _d)
 for _k in range(8):
     SCRATCH["p%d" % _k] = ("psum", [128, 512], F32)
 
 DMAS = ["ld%d" % _k for _k in range(24)]
-SEMAPHORES = ["V", "S", "PE", "G", "sent", "a0c", "a0s", "ahc", "ahs", "a1c", "a1s", "a2c", "a2s", "a3c", "a3s", "ah0c", "ah0s"] + DMAS
+SEMAPHORES = ["V", "S", "PE", "G", "sent", "a0c", "a0s", "a1c", "a1s", "a2c", "a2s", "ah1c", "ah1s", "ah2c", "ah2s"] + DMAS
 
 ADD, SUB, MUL, MAX, MIN = AluOpType.add, AluOpType.subtract, AluOpType.mult, AluOpType.max, AluOpType.min
 GE, GT, LT, EQ = AluOpType.is_ge, AluOpType.is_gt, AluOpType.is_lt, AluOpType.is_equal
@@ -68,16 +67,6 @@ def engine_sets(src, c, T, topo):
     return far, [e for e in near if e not in far]
 
 
-def peers_of(q, same):
-    return [r for r in [(q + i) % NR for i in range(1, NR)] if (r // 4 == q // 4) == same]
-
-
-def route2(q, half):
-    to = [(q + i) % NR for i in range(1, NR)][4 * half:4 * half + 4]
-    n = DIRECT if half == 0 else len(to)
-    return to[:n], to[n:]
-
-
 def transfer(topo, src, dsts, mask, sem, a, b, kind):
     b = b if isinstance(b, list) else [b] * len(dsts)
     if kind == "c":
@@ -96,21 +85,17 @@ def helper_program(g, core, T, topo):
     q = T.rank_of(own[0])
     k = helpers_of(own[0], T, topo).index(core)
     far, near = engine_sets(core, own[0], T, topo)
-    to = [T.cores[r] for r in peers_of(q, False)][k::2]
-    calls = 0
+    masks = deal(far, 2)[0]
     for kind in "cs":
-        g.wait_ge(T.sem["ah" + kind], len(near))
-        g.remote_dma_fused([transfer(topo, core, to, bits(far), T.sem["a1" + kind], T["hp" + kind][:, 0:R1],
-                                     T["lr" + kind][:, R1 * (q % 4):R1 * (q % 4) + R1], kind)], local_sem=T.sem.sent)
-        calls += 1
-    via = route2(q, 0)[1]
-    if k < len(via):
-        for kind in "cs":
-            g.wait_ge(T.sem["ah0" + kind], deal(near, len(via))[1][k])
-            g.remote_dma_fused([transfer(topo, core, [T.cores[via[k]]], bits(far), T.sem["a2" + kind], T["h0" + kind][:, 0:S],
-                                         T["l2" + kind][:, Z + S * q:Z + S * q + S], kind)], local_sem=T.sem.sent)
-            calls += 1
-    g.wait_ge(T.sem.sent, calls * len(far))
+        g.wait_ge(T.sem["ah1" + kind], len((far, near)[k]))
+        g.remote_dma_fused([transfer(topo, core, [T.cores[(q + 1 + 2 * k + i) % NR]], masks[i], T.sem["a1" + kind],
+                                     T["h1" + kind][:, S * i:S * i + S], T["l1" + kind][:, S * q:S * q + S], kind) for i in range(2)],
+                           local_sem=T.sem.sent)
+    for kind in "cs":
+        g.wait_ge(T.sem["ah2" + kind], deal(near, 2)[1][k])
+        g.remote_dma_fused([transfer(topo, core, [T.cores[(q + 3 + k) % NR]], bits(far), T.sem["a2" + kind], T["h2" + kind][:, 0:S],
+                                     T["l2" + kind][:, Z + S * q:Z + S * q + S], kind)], local_sem=T.sem.sent)
+    g.wait_ge(T.sem.sent, 4 * len(far))
 
 
 def rank_program(g, core, T, topo):
@@ -259,6 +244,30 @@ def rank_program(g, core, T, topo):
         else:
             op("G", [], [out], lambda: g.iota(ap(out), pattern, base, cm, allow_small_or_imprecise_dtypes=True))
 
+    def scatter_half(src, h, land, at, stage):
+        for kind in "cs":
+            dst = v(land + kind, at + S * q, at + S * q + S)
+            block = lambda x, n=1: v(src + kind, S * x, S * (x + n))
+            sem, hsem, hbuf = T.sem["a%d%s" % (stage, kind)], T.sem["ah%d%s" % (stage, kind)], ap(v("h%d%s" % (stage, kind)))
+            direct = [4, 5, 6] if h == 1 else [] if stage == 1 else [0, 1]
+            tr, n = [], 0
+            if direct:
+                masks, nd = deal(far, len(direct), kind == "s")
+                tr += [transfer(topo, core, [T.cores[peers[x]]], m, sem, ap(block(x)), ap(dst), kind) for x, m in zip(direct, masks)]
+                n += sum(nd)
+            if h == 0 and stage == 1:
+                tr += [transfer(topo, core, [c], bits(e), hsem, ap(block(2 * k, 2)), hbuf, kind)
+                       for k, (c, e) in enumerate(zip(helpers, (far, near)))]
+                n += len(far) + len(near)
+            elif h == 0:
+                masks, nh = deal(near, 2)
+                tr += [transfer(topo, core, [c], m, hsem, ap(block(2 + k)), hbuf, kind) for k, (c, m) in enumerate(zip(helpers, masks))]
+                n += sum(nh)
+            send(tr, [block(4 * h, 4 - h)], n)
+            if h == 1:
+                dma("Y", dst, block(NR - 1), codes=kind == "c")
+                arrives("a%d%s" % (stage, kind), (2 + stage) * len(far), [v(land + kind, at + S * r, at + S * r + S) for r in peers])
+
     cf = lambda k: v("cf", k, k + 1)
     dc = lambda k: v("dc", k, k + 1)
     pb = lambda k, a, b, step=None, rows=(0, 128): v("p%d" % k, a, b, step, rows)
@@ -269,7 +278,6 @@ def rank_program(g, core, T, topo):
     oTH, oLA0, oLA1 = v("so", 112, 116), v("so", 116, 117), v("so", 118, 120)
     lr0, lr0b, lr1 = v("lref", 0, 64), v("lref", 64, 80), v("lref", 80, 112)
     io = lambda a, b: v("idx", IO + a, IO + b)
-    hh = 1 - q // 4
 
     dma("Y", v("t1", 0, 64), v("r0"))
     dma("S", v("t1", 64, 72), v("u", 0, 8))
@@ -291,7 +299,7 @@ def rank_program(g, core, T, topo):
     for k, sh, m in ((7, 2, 3), (8, 4, 3), (10, 2, 27)):
         ts(v("ci", k, k + 1), v("ci", 0, 1), sh, SHR, m, AND)
     cp(v("cf", 0, 11), v("ci", 0, 11))
-    act(v("tx0"), v("tk", zeros, zeros + 784), AF.Copy)
+    act(v("tx0"), v("tk", zeros, zeros + 528), AF.Copy)
     for k, src, mul, add in ((11, 1, 16.0, 16.0), (12, 3, 4.0, 0.0), (13, 1, 1.0, -16.0), (14, 3, 1.0, -16.0),
                              (20, 2, -1.0, 0.0), (21, 6, -1.0, 0.0), (22, 5, -1.0, 0.0)):
         act(cf(k), cf(src), AF.Identity, scale=mul, bias=add)
@@ -319,13 +327,9 @@ def rank_program(g, core, T, topo):
     fill(v("tk", 1024, 2048), 0.0)
     for x in range(4):
         ts(cf(16 + x), cf(8), float(x), EQ, cf(11), MUL)
-    quant("qr", 0, 320, "tr", 0)
-    for kind in "cs":
-        x = v("qr" + kind, 0, R1)
-        send([transfer(topo, core, helpers, bits(near), T.sem["ah" + kind], ap(x), ap(v("hp" + kind)), kind)], [x], len(near))
-        arrives("a1" + kind, len(far) * 4, [v("lr" + kind)])
     for b in range(4):
         ts(v("tk", 512 * b + b, 512 * b + 512, 4), io(0, 128), cf(0), EQ)
+    quant("qr", 0, 320, "tr", 0)
     sel = v("tk", 4 * SEL, 4 * SEL + 512)
     act(v("tk", 4 * W0, 4 * W0 + 512), sel, AF.Identity, scale=0.0, bias=cf(11))
     for at, k in ((WA, 1), (WB, 2), (WD, 12)):
@@ -436,15 +440,7 @@ def rank_program(g, core, T, topo):
         quant("ch", 128 * h, 128 * h + 128, "tch", 512 * h)
         mm(2 * h, "u32", 128 * h, "ch", 128 * h, 128)
         mm(2 * h + 1, "ch", 128 * h, "l0", 0, L0)
-    mates = peers_of(q, True)
-    for kind in "cs":
-        land = v("l1" + kind, S * q, S * q + S)
-        block = lambda r: v("ch" + kind, S * ((r - q - 1) % NR), S * ((r - q - 1) % NR) + S)
-        masks, nd = deal(far, len(mates), kind == "s")
-        send([transfer(topo, core, [T.cores[r]], m, T.sem["a3" + kind], ap(block(r)), ap(land), kind) for r, m in zip(mates, masks)],
-             [block(r) for r in mates], sum(nd))
-        dma("Y", land, block(q), codes=kind == "c")
-        arrives("a3" + kind, sum(nd[peers_of(r, True).index(q)] for r in mates), [v("l1" + kind, S * r, S * r + S) for r in mates])
+        scatter_half("ch", h, "l1", 0, 1)
 
     for b in range(2):
         for x in range(4):
@@ -456,32 +452,29 @@ def rank_program(g, core, T, topo):
     ts(dc(12), dc(10), M - 0.5, LT)
     for b in range(2):
         red(dc(8 + b), v("c1", 32 * b, 32 * b + 32))
-    one_hot(v("tx0", 272, 336), lr0, dc(11), dc(12))
+    one_hot(v("tx0", 16, 272, 4), lr0, dc(11), dc(12))
     for b in range(2):
         one_hot(v("tx1", 32 * b, 32 * b + 32), lr1, dc(8 + b), dc(6 + b))
     for b in range(2):
         one_hot(v("tx1", 64 + 32 * b, 96 + 32 * b), lr1, dc(8 + b), dc(4 + b))
-    one_hot(v("tx0", 16, 272, 4), lr0, dc(11), dc(12))
+    one_hot(v("tx0", 0, 16), lr0b, dc(11), dc(12))
     quant("x1", 0, 144, "tx1", 0)
     mm(4, "qk", WA, "x1", 0, 128, True, False)
     mm(4, "qk", WB, "x1", 0, 128, False, True)
     spread_numbers("x1", 7)
-    one_hot(v("tx0", 0, 16), lr0b, dc(11), dc(12))
-    quant("x0", 0, 196, "tx0", 0)
-    mm(5, "qk", WA, "x0", 68, 128, True, False)
-    mm(5, "qk", WB, "x0", 68, 128, False, True)
+    quant("x0", 0, 132, "tx0", 0)
     spread_slots(6)
+    spread_parents(5)
     ts(v("do1", 0, 16), pb(4, 0, 16), 0.0, ADD)
     for h in range(2):
         for pick in (pick_c, pick_s):
             pick("pv", 128 * h, 128, "ch", 128 * h, 128 * h + 128, v("do1", 8 * h, 8 * h + 8))
         if h == 0:
             ts(v("do1", 16, 32), pb(7, 0, 16), cf(14), ADD, 0.0, MAX)
-            ts(v("do3", 0, 8), pb(5, 8 * hh, 8 * hh + 8), -64.0 * hh, ADD, 0.0, MAX)
+            act(v("m4"), pb(6, 0, 64), AF.Identity, scale=0.25)
+            act(v("dc", 14, 16), pb(5, 0, 2), AF.Copy)
         for pick in (pick_c, pick_s):
             pick("pe", 128 * h, 128, "qr", R1, 320, v("do1", 16 + 8 * h, 24 + 8 * h))
-        if h == 0:
-            act(v("m4"), pb(6, 0, 64), AF.Identity, scale=0.25)
         for b in range(4):
             mm(4 * h + b, "qk", E + 128 * b, "pv", 128 * h, 128, True, False)
         for b in range(4):
@@ -493,60 +486,22 @@ def rank_program(g, core, T, topo):
         for x in range(4):
             a = 512 * h + 128 * x
             act(v("tgr", a + 3, a + 128, 4), pb(4 * h + 3, 32 * x, 32 * x + 32), AF.Identity, bias=shift(4 * h + x, 3))
-        if h == 0:
-            ts(v("do3", 8, 16), v("do3", 0, 8), 4.0, MUL, cf(3), ADD)
-            pick_s("av", 0, 128, "ra", 64 * hh, 64 * hh + 64, v("do3", 0, 8))
-        else:
-            pick_c("av", 0, 128, "ra", 64 * hh, 64 * hh + 64, v("do3", 0, 8))
         quant("gr", 128 * h, 128 * h + 128, "tgr", 512 * h)
-        direct, via = route2(q, h)
-        for kind in "cs":
-            land = ap(v("l2" + kind, Z + S * q, Z + S * q + S))
-            block = lambda r: v("gr" + kind, S * ((r - q - 1) % NR), S * ((r - q - 1) % NR) + S)
-            masks, nd = deal(far, len(direct), kind == "s")
-            tr = [transfer(topo, core, [T.cores[r]], m, T.sem["a2" + kind], ap(block(r)), land, kind) for r, m in zip(direct, masks)]
-            if via:
-                masks, nh = deal(near, len(via))
-                nd = nd + nh
-                tr += [transfer(topo, core, [c], m, T.sem["ah0" + kind], ap(block(r)), ap(v("h0" + kind)), kind)
-                       for r, c, m in zip(via, helpers, masks)]
-            send(tr, [block(r) for r in direct + via], sum(nd))
-            if h == 1:
-                dma("Y", v("l2" + kind, Z + S * q, Z + S * q + S), block(q), codes=kind == "c")
-    n2 = 0
-    for h in range(2):
-        direct, via = route2(q, h)
-        n2 += sum(deal(far, len(direct))[1]) + len(far) * len(via)
-    for kind in "cs":
-        arrives("a2" + kind, n2, [v("l2" + kind, Z + S * r, Z + S * r + S) for r in peers])
+        scatter_half("gr", h, "l2", Z, 2)
+        if h == 0:
+            for k in range(4):
+                act(v("n1p", k, 256, 4), v("m4"), AF.Relu, bias=float(k - 3))
 
-    for pick in (pick_c, pick_s):
-        pick("ae", 0, 128, "lr", 0, 4 * R1, v("do3", 8, 16))
-    for b in range(4):
-        mm(b, "qk", E + 128 * b, "av", 0, 128, True, False)
-    for b in range(4):
-        mm(b, "qk", E + 128 * b, "ae", 0, 128, False, True)
-    spread_parents(7)
-    mm(6 - hh, "l1", 128 * (1 - hh), "q1", 0, 128)
-    for k in range(4):
-        ts(v("n1", k, 256, 4), v("m4"), float(k - 4), ADD, -1.0, MAX)
-    dma("Y", v("nm", 0, 256, rows=(0, 1)), v("n1", rows=(0, 1)))
-    for b in range(4):
-        out, src = v("ta1", b, 512, 4), pb(b, 0, 128)
-        if b % 2 == 0:
-            act(out, src, AF.Identity, bias=shift(NR - 1, b))
-        else:
-            ts(out, src, shift(NR - 1, b), ADD)
-    act(v("cap"), v("n1"), AF.Identity, scale=CAPV, bias=0.5 * CAPV)
-    quant("l1", 128 * hh, 128 * hh + 128, "ta1", 0)
-
-    mm(4, "mq", 0, "l1", 0, 256)
-    mm(5 + hh, "l1", 128 * hh, "q1", 0, 128)
+    mm(0, "mq", 0, "l1", 0, 256)
+    for b in range(2):
+        mm(1 + b, "l1", 128 * b, "q1", 0, 128)
     mm(3, "qw", 0, "l1", 0, 256)
-    for b in (1 - hh, hh):
-        act(dc(26 + b), pb(5 + b, P, P + 1), AF.Identity, scale=-1.0)
-        act(dc(28 + b), pb(5 + b, P, P + 1), AF.Copy)
-    tt(v("am"), pb(4, 0, 256), v("cap"), MIN)
+    act(v("cap"), v("n1p"), AF.Identity, scale=CAPV, bias=-0.5 * CAPV)
+    act(v("dc", 16, 18), v("dc", 14, 16), AF.Sign)
+    for b in range(2):
+        act(dc(26 + b), pb(1 + b, P, P + 1), AF.Identity, scale=-1.0)
+        act(dc(28 + b), pb(1 + b, P, P + 1), AF.Copy)
+    tt(v("am"), pb(0, 0, 256), v("cap"), MIN)
     for b in range(2):
         o = 128 * (1 - b)
         act(v("db", 128 * b, 128 * b + 128), v("am", 128 * b, 128 * b + 128), AF.Identity, bias=dc(26 + b))
@@ -555,13 +510,13 @@ def rank_program(g, core, T, topo):
         o = 256 * b + 128 * (1 - b)
         act(v("junk", 80 + 128 * b, 208 + 128 * b), v("cb", o, o + 128), AF.Identity, acc=dc(30 + b))
     act(v("dc", 32, 34), v("dc", 30, 32), AF.Identity, bias=1.0 - M)
-    act(v("dc", 14, 16), pb(7, 0, 2), AF.Copy)
-    act(v("dc", 16, 18), pb(7, 0, 2), AF.Sign)
     for b in range(2):
         own = v("cb", 384 * b, 384 * b + 128)
         tt(own, v("db", 128 * b, 128 * b + 128), v("thra"), GE)
         act(v("junk", 16 + 32 * b, 48 + 32 * b), own, AF.Identity, off=oLA1, acc=dc(20 + b))
-    act(v("val"), v("n1"), AF.Sign, bias=1.0)
+    act(v("val"), v("n1p"), AF.Sign)
+    act(v("n1", rows=(0, 1)), v("n1p", rows=(0, 1)), AF.Identity, bias=-1.0)
+    dma("Y", v("nm", 0, 256, rows=(0, 1)), v("n1", rows=(0, 1)))
     for b in range(2):
         own, run, nil = v("cb", 384 * b, 384 * b + 128), v("junk", 464 + 128 * b, 592 + 128 * b), v("tx1", 256, 384)
         op("V", [own, nil, dc(32 + b)], [run], lambda: g.vector.tensor_tensor_scan(ap(run), ap(own), ap(nil), ap(dc(32 + b)), ADD, ADD))
@@ -569,30 +524,29 @@ def rank_program(g, core, T, topo):
         ts(dc(24 + b), v("junk", 591 + 128 * b, 592 + 128 * b), 128.0, MUL, dc(20 + b), MAX)
     for b in range(2):
         one_hot(v("tx1", 32 * b, 32 * b + 32), lr1, dc(24 + b), dc(16 + b))
-    quant("x1", 0, 128, "tx1", 0)
-    mm(4, "qk", SEL, "x1", 0, 128)
+    for b in range(2):
+        one_hot(v("tx1", 64 + 32 * b, 96 + 32 * b), lr1, dc(24 + b), dc(14 + b))
+    quant("x2", 0, 144, "tx1", 0)
+    mm(4, "qk", SEL, "x2", 0, 128)
+    spread_numbers("x2", 7)
     tt(v("y0"), pb(3, 0, 256), v("val"), MUL)
     dma("Y", v("y", 0, 256), v("y0"))
     tt(v("o2"), pb(4, 0, 16), v("plc"), MUL)
-    for b in range(2):
-        one_hot(v("tx1", 64 + 32 * b, 96 + 32 * b), lr1, dc(24 + b), dc(14 + b))
+    ts(v("n2", 0, 16), pb(7, 0, 16), cf(14), ADD, -1.0, MAX)
     cp(v("do2"), v("o2"))
-    quant("x2", 0, 144, "tx1", 0)
-    spread_numbers("x2", 7)
 
+    a, b = v("n2t", rows=(0, 32)), v("n2", rows=(0, 32))
+    op("V", [b], [a], lambda: g.vector.transpose(ap(a), ap(b)))
+    dma("Y", v("nm", 256, 512, rows=(0, 1)), v("n2t", 0, 16, rows=(0, 16)))
     for h in range(2):
         pick_c("fin", 128 * h, 128, "l2", 0, Z + 256, v("do2", 8 * h, 8 * h + 8))
         pick_s("fin", 128 * h, 128, "l2", 0, Z + 256, v("do2", 8 * h, 8 * h + 8))
         mm(5 + h, "qw", 0, "fin", 128 * h, 128)
     dma("Y", v("oc"), v("finc"), codes=True)
-    ts(v("n2", 0, 16), pb(7, 0, 16), cf(14), ADD, -1.0, MAX)
     cp(v("y1", 0, 128), pb(5, 0, 128))
-    a, b = v("n2t", rows=(0, 32)), v("n2", rows=(0, 32))
-    op("V", [b], [a], lambda: g.vector.transpose(ap(a), ap(b)))
     dma("Y", v("y", 256, 384), v("y1", 0, 128))
     act(v("y1", 128, 256), pb(6, 0, 128), AF.Copy)
     dma("S", v("y", 384, 512), v("y1", 128, 256))
-    dma("Y", v("nm", 256, 512, rows=(0, 1)), v("n2t", 0, 16, rows=(0, 16)))
     for k in range(4):
         dma("YS"[k % 2], v("osc", rows=(4 * k, 4 * k + 4)), v("fins", rows=(32 * k, 32 * k + 4)))
 

@@ -1,29 +1,35 @@
 from concourse.bass import DstId, RemoteDMATransfer
 from concourse.mybir import dt, AluOpType, AxisListType, ActivationFunctionType
 
+CFG = {"h2": 4, "bv": 16, "nq": 2, "cs": "SS", "u0": "V", "u1": "S", "fs": "SS", "ty": "G", "tries": 300, "seed": 1}
+COST = {"cycle": 0.00083, "V": 64, "S": 80, "PE": 0, "G": 0, "pick0": 60, "pick": 1.5, "mm": 0.75, "issue": 0.05, "dma": 1.1,
+        "wide": 0.001, "send": 0.15, "first": 1.3, "a0c": 2.4, "a0s": 3.2, "a1c": 2.0, "a1s": 2.4, "a2c": 2.0, "a2s": 2.4,
+        "h1c": 4.1, "h1s": 4.3, "h2c": 2.9, "h2s": 3.1}
+CASES = ((1.0, 0.21, 1.0), (1.0, 0.21, 0.8), (1.2, 0.25, 1.3), (1.1, 0.15, 1.1))
 NR, P, CAP, M, S = 8, 16, 8, 40, 32
 W1 = P + 2
 L0 = NR * W1
 R1 = 4 * P
-Z = 32
-TINY, HUGE, CAPV = 2.0 ** -110, 2.0 ** 90, 2.0 ** 80
+Z = 16
+TINY, HUGE = 2.0 ** -110, 2.0 ** 90
 Q4, U8, BF, F32, I32, U16 = "float8_e4m3fn_x4", "uint8", "bfloat16", "float32", "int32", "uint16"
 
 SCRATCH = {}
-for _n, _w in (("q1", 128), ("qr", 320), ("qw", 128), ("qk", 1408), ("l0", L0), ("u16", 128), ("u32", 256), ("ra", 128),
-               ("r4", 128), ("mq", 128), ("x0", 132), ("x1", 144), ("x2", 144), ("ch", 256), ("l1", 256), ("h1", 2 * S), ("h2", S),
-               ("pv", 256), ("pe", 256), ("gr", 256), ("l2", Z + 256), ("fin", 256)):
+for _n, _w in (("q1", 128), ("qa", 128), ("qr", 256), ("qw", 128), ("qk", 1152), ("l0", L0), ("u16", 128), ("u32", 256), ("ra", 128),
+               ("r4", 128), ("mq", 256), ("rr", 256), ("al", 512), ("x0", 128), ("xa", 128), ("x1", 144), ("x2", 144), ("ch", 256),
+               ("l1", 256), ("h1", 2 * S), ("h2", 2 * S), ("pv", 256), ("pe", 256), ("gr", 256), ("l2", Z + 256), ("fin", 256)):
     SCRATCH[_n + "c"] = ("sbuf", [128, _w], Q4)
     SCRATCH[_n + "s"] = ("sbuf", [128, _w], U8)
-for _n, _w, _d in (("t1", 512, BF), ("tr", 1280, BF), ("tw", 512, BF), ("tk", 5632, BF), ("tx0", 528, BF), ("tx1", 576, BF),
-                   ("tch", 1024, BF), ("tgr", 1024, BF), ("ci", 16, I32), ("cf", 32, F32), ("idx", 512, F32),
-                   ("so", 128, U16), ("do0", 64, U16), ("do1", 32, U16), ("do2", 16, U16),
-                   ("thr0", 16, BF), ("thra", 128, BF), ("base1", 64, BF), ("diag", 16, F32), ("lref", 112, F32), ("plc", 16, F32),
-                   ("s0", 256, F32), ("dh", 32, F32), ("hx", 1024, F32), ("dc", 40, F32), ("dm", 16, F32), ("g2", 256, F32),
-                   ("d0", 16, BF), ("c0", 128, BF), ("ms", 64, F32), ("thd", 64, BF), ("thr1", 64, BF), ("d1", 64, BF), ("c1", 64, BF),
-                   ("da", 128, BF), ("ca", 128, BF), ("junk", 720, BF), ("m4", 64, F32), ("n1", 256, F32), ("cap", 256, F32),
-                   ("val", 256, F32), ("am", 256, F32), ("db", 256, BF), ("cb", 512, BF), ("n2", 32, F32), ("n2t", 32, F32),
-                   ("o2", 16, F32), ("y0", 256, F32), ("y1", 256, F32), ("n1p", 256, F32)):
+for _n, _w, _d in (("t1", 512, BF), ("ta", 512, BF), ("tr", 1024, BF), ("tw", 512, BF), ("tz", 516, BF), ("tk", 2560, BF), ("tx", 576, BF),
+                   ("ty", 576, BF), ("tch", 2048, BF), ("tgr", 1024, BF), ("ci", 16, I32), ("cf", 32, F32), ("ib", 256, BF),
+                   ("idx", 176, F32), ("of", 128, F32), ("so", 128, U16), ("do0", 16, U16), ("do1", 32, U16), ("do2", 16, U16),
+                   ("mx", 8, F32), ("iref", 64, BF), ("thra", 128, BF), ("base1", 64, BF), ("diag", 16, F32), ("mask", 64, F32),
+                   ("lr", 64, F32), ("ppb", 8, F32), ("step", 64, F32), ("s0", 256, F32), ("dh", 32, F32), ("hx", 768, F32),
+                   ("dc", 32, F32), ("dm", 16, F32), ("cl", 128, BF), ("c0", 112, BF), ("run0", 112, BF), ("k8", 8, F32),
+                   ("kb", 64, F32), ("keep", 64, BF), ("d1", 64, BF), ("c1", 64, BF), ("run1", 64, F32), ("pm", 128, F32),
+                   ("ca", 128, BF), ("runa", 128, BF), ("junk", 528, F32), ("m4", 64, F32), ("inv", 64, F32), ("pf", 64, F32),
+                   ("thr", 512, BF), ("val", 512, F32), ("cb", 512, BF), ("runb", 256, BF), ("n1", 512, F32),
+                   ("n2", 32, F32), ("n2t", 32, F32), ("yy", 512, F32)):
     SCRATCH[_n] = ("sbuf", [128, _w], _d)
 for _k in range(8):
     SCRATCH["p%d" % _k] = ("psum", [128, 512], F32)
@@ -33,8 +39,9 @@ SEMAPHORES = ["V", "S", "PE", "G", "sent", "a0c", "a0s", "a1c", "a1s", "a2c", "a
 
 ADD, SUB, MUL, MAX, MIN = AluOpType.add, AluOpType.subtract, AluOpType.mult, AluOpType.max, AluOpType.min
 GE, GT, LT, EQ = AluOpType.is_ge, AluOpType.is_gt, AluOpType.is_lt, AluOpType.is_equal
-SHR, AND = AluOpType.logical_shift_right, AluOpType.bitwise_and
+AND = AluOpType.bitwise_and
 AF = ActivationFunctionType
+ORDERS = {}
 
 
 def bits(engines):
@@ -78,6 +85,10 @@ def transfer(topo, src, dsts, mask, sem, a, b, kind):
     return RemoteDMATransfer(dst_ids=ids, dma_engine_mask=mask, remote_sem=sem, src=a, dsts=b)
 
 
+def helped(stage):
+    return 4 if stage == 1 else CFG["h2"]
+
+
 def helper_program(g, core, T, topo):
     own = [c for c in T.cores if core in helpers_of(c, T, topo)]
     if not own:
@@ -85,17 +96,99 @@ def helper_program(g, core, T, topo):
     q = T.rank_of(own[0])
     k = helpers_of(own[0], T, topo).index(core)
     far, near = engine_sets(core, own[0], T, topo)
-    masks = deal(far, 2)[0]
-    for kind in "cs":
-        g.wait_ge(T.sem["ah1" + kind], len((far, near)[k]))
-        g.remote_dma_fused([transfer(topo, core, [T.cores[(q + 1 + 2 * k + i) % NR]], masks[i], T.sem["a1" + kind],
-                                     T["h1" + kind][:, S * i:S * i + S], T["l1" + kind][:, S * q:S * q + S], kind) for i in range(2)],
-                           local_sem=T.sem.sent)
-    for kind in "cs":
-        g.wait_ge(T.sem["ah2" + kind], deal(near, 2)[1][k])
-        g.remote_dma_fused([transfer(topo, core, [T.cores[(q + 3 + k) % NR]], bits(far), T.sem["a2" + kind], T["h2" + kind][:, 0:S],
-                                     T["l2" + kind][:, Z + S * q:Z + S * q + S], kind)], local_sem=T.sem.sent)
+    for stage, at in ((1, 0), (2, Z)):
+        n = helped(stage) // 2
+        masks = deal(far, n)[0]
+        for kind in "cs":
+            g.wait_ge(T.sem["ah%d%s" % (stage, kind)], len((far, near)[k]) if n == 2 else deal(near, 2)[1][k])
+            g.remote_dma_fused([transfer(topo, core, [T.cores[(q + 5 - 2 * n + n * k + i) % NR]], masks[i], T.sem["a%d%s" % (stage, kind)],
+                                         T["h%d%s" % (stage, kind)][:, S * i:S * i + S],
+                                         T["l%d%s" % (stage, kind)][:, at + S * q:at + S * q + S], kind) for i in range(n)],
+                               local_sem=T.sem.sent)
     g.wait_ge(T.sem.sent, 4 * len(far))
+
+
+def best_order(queue, busy, lag, pred, banks):
+    n = len(queue)
+    succ = [[] for _ in range(n)]
+    for j in range(n):
+        for i in pred[j]:
+            succ[i].append(j)
+
+    def edges(case):
+        kb, wait, fly = case
+        b = [busy[i] * (kb if queue[i] in "VSPE" else fly) for i in range(n)]
+        return b, [[(i, b[i] + wait * w + fly * f) for i, (w, f) in pred[j].items()] for j in range(n)], [fly * x for x in lag], wait
+
+    cases = [edges(c) for c in CASES]
+
+    def place(way):
+        b, pre, tail, wait = cases[0]
+        start, taken, miss = [0.0] * n, {}, [len(p) for p in pred]
+        ready = [j for j in range(n) if not miss[j]]
+        while ready:
+            j = max(ready, key=lambda j: (way[j], -j))
+            ready.remove(j)
+            t = max([start[i] + d for i, d in pre[j]] + [0.0])
+            spans = taken.get(queue[j], [])
+            if banks[j]:
+                spans = sorted(spans + [(s[0] - wait, s[1] + wait) for k in banks[j] for s in taken.get(k, []) if s[2] != queue[j]])
+            for s in spans:
+                if t + b[j] <= s[0] + 1e-9:
+                    break
+                if s[1] > t:
+                    t = s[1]
+            start[j] = t
+            taken.setdefault(queue[j], []).append((t, t + b[j]))
+            taken[queue[j]].sort()
+            for k in banks[j]:
+                taken.setdefault(k, []).append((t, t + b[j], queue[j]))
+            for k in succ[j]:
+                miss[k] -= 1
+                if not miss[k]:
+                    ready.append(k)
+        return sorted(range(n), key=lambda j: (start[j], j))
+
+    def length(order):
+        total = 0.0
+        for b, pre, tail, wait in cases:
+            start, free, last, end = [0.0] * n, {}, {}, 0.0
+            for j in order:
+                t = free.get(queue[j], 0.0)
+                for i, d in pre[j]:
+                    if start[i] + d > t:
+                        t = start[i] + d
+                for k in banks[j]:
+                    for e, x in last.get(k, {}).items():
+                        if e != queue[j] and x + wait > t:
+                            t = x + wait
+                start[j] = t
+                free[queue[j]] = t + b[j]
+                for k in banks[j]:
+                    last.setdefault(k, {})[queue[j]] = t + b[j]
+                end = max(end, t + b[j] + tail[j])
+            total += end
+        return total
+
+    b, pre, tail, wait = cases[0]
+    way = [b[i] + tail[i] for i in range(n)]
+    for j in range(n - 1, -1, -1):
+        for i, d in pre[j]:
+            way[i] = max(way[i], d + way[j])
+    best = place(way)
+    least, state = length(best), CFG["seed"]
+    for k in range(CFG["tries"]):
+        trial = list(way)
+        for _ in range(1 + k % 24):
+            state = (state * 1103515245 + 12345) % 2147483648
+            j = (state >> 8) % n
+            state = (state * 1103515245 + 12345) % 2147483648
+            trial[j] += ((state >> 8) % 2001 - 1000) / 1000.0
+        order = place(trial)
+        t = length(order)
+        if t <= least:
+            best, least, way = order, t, trial
+    return best
 
 
 def rank_program(g, core, T, topo):
@@ -116,6 +209,9 @@ def rank_program(g, core, T, topo):
 
     def v(name, a=None, b=None, step=None, rows=(0, 128)):
         return (name, rows, slice(a, b, step))
+
+    def back(name, a, b):
+        return v(name, b - 1, a - 1 if a else None, -1)
 
     def ap(x):
         return T[x[0]][x[1][0]:x[1][1], x[2]]
@@ -159,78 +255,126 @@ def rank_program(g, core, T, topo):
             if x[0] in SCRATCH:
                 hist.setdefault(x[0], []).append((e, tok, wr, x[1], cols(x)))
 
-    def op(e, reads, writes, call):
+    plan = []
+
+    def later(e, reads, writes, busy, edge, emit, after=()):
+        plan.append((e, [x for x in reads if isinstance(x, tuple) and x[0] in SCRATCH], [x for x in writes if x[0] in SCRATCH],
+                     busy, edge, emit, list(after)))
+        return len(plan) - 1
+
+    def op(e, reads, writes, call, cycles, after=()):
         reads = [x for x in reads if isinstance(x, tuple)]
-        order(e, reads, writes)
-        count[e] += 1
-        call().then_inc(T.sem[e], 1)
-        note(e, (e, count[e]), reads, writes)
+
+        def emit():
+            order(e, reads, writes)
+            count[e] += 1
+            call().then_inc(T.sem[e], 1)
+            note(e, (e, count[e]), reads, writes)
+        return later(e, reads, writes, max(cycles, COST[e]) * COST["cycle"], (1, 0.05 if e == "PE" else 0.0), emit, after)
 
     def sc(x):
         return ap(x) if isinstance(x, tuple) else x
 
-    def dma(e, out, in_, codes=False):
-        order(e, [in_], [out])
-        sem = free_sems.pop(0)
-        a, b = ap(out), ap(in_)
-        if codes:
-            b = b.bitcast(dt.uint8)
-            if out[0] in SCRATCH:
-                a = a.bitcast(dt.uint8)
-        queue[e].dma_start(a, b).then_inc(T.sem[sem], 16)
-        known[(sem, 16)] = dict(clock[e])
-        final[sem] = 16
-        for x, wr in ((in_, False), (out, True)):
-            if x[0] in SCRATCH:
-                hist.setdefault(x[0], []).append(("dma", (sem, 16), wr, x[1], cols(x)))
+    def dma(e, out, in_, codes=False, behind=0.0):
+        def emit():
+            order(e, [in_], [out])
+            sem = free_sems.pop(0)
+            a, b = ap(out), ap(in_)
+            if codes:
+                b = b.bitcast(dt.uint8)
+                if out[0] in SCRATCH:
+                    a = a.bitcast(dt.uint8)
+            queue[e].dma_start(a, b).then_inc(T.sem[sem], 16)
+            known[(sem, 16)] = dict(clock[e])
+            final[sem] = 16
+            for x, wr in ((in_, False), (out, True)):
+                if x[0] in SCRATCH:
+                    hist.setdefault(x[0], []).append(("dma", (sem, 16), wr, x[1], cols(x)))
+        wide = len(cols(out if out[0] in SCRATCH else in_))
+        return later(e, [in_], [out], COST["issue"], (0, COST["dma"] + COST["wide"] * wide + behind), emit)
 
-    def arrives(sem, n, views):
-        note("far", (sem, n), [], views)
+    def arrives(sem, n, views, after):
+        later(sem, [], views, 0.0, (0, 0.0), lambda: note("far", (sem, n), [], views), after)
+
+    sends = []
 
     def send(transfers, reads, n):
-        order("G", reads, [])
-        g.remote_dma_fused(transfers, local_sem=T.sem.sent)
-        final["sent"] = final.get("sent", 0) + n
+        def emit():
+            order("G", reads, [])
+            g.remote_dma_fused(transfers, local_sem=T.sem.sent)
+            final["sent"] = final.get("sent", 0) + n
+        sends.append(later("G", reads, [], COST["send"] if sends else COST["first"], (0, 0.0), emit, [(i, 0.0) for i in sends[-1:]]))
+        return sends[-1]
+
+    def schedule():
+        key = tuple(x[0] for x in plan)
+        if key not in ORDERS:
+            pred, seen = [], {}
+            for j, (e, reads, writes, busy, edge, emit, after) in enumerate(plan):
+                d = {i: (0, f) for i, f in after}
+                mine = [(x, False, cols(x)) for x in reads] + [(x, True, cols(x)) for x in writes]
+                for x, wr, cx in mine:
+                    psum = SCRATCH[x[0]][0] == "psum"
+                    for i, wr2, rows, c2 in seen.get(x[0], []):
+                        if (wr or wr2) and (psum or rows[0] < x[1][1] and x[1][0] < rows[1] and not cx.isdisjoint(c2)):
+                            d[i] = (0, 0.0) if psum and e == plan[i][0] == "PE" else plan[i][4]
+                for x, wr, cx in mine:
+                    seen.setdefault(x[0], []).append((j, wr, x[1], cx))
+                pred.append(d)
+            banks = [{x[0] for x in p[1] + p[2] if SCRATCH[x[0]][0] == "psum"} for p in plan]
+            ORDERS[key] = best_order([p[0] for p in plan], [p[3] for p in plan], [p[4][1] for p in plan], pred, banks)
+        for j in ORDERS[key]:
+            plan[j][5]()
+
+    def size(*views):
+        return len(cols(views[0])) * (0.5 if all(SCRATCH[x[0]][2] in (BF, U16) for x in views) else 1.0)
+
+    def picked(out):
+        return COST["pick0"] + COST["pick"] * len(cols(out))
 
     def ts(out, in0, s1, op0, s2=None, op1=None):
         if op1 is None:
-            op("V", [in0, s1], [out], lambda: g.vector.tensor_scalar(ap(out), ap(in0), sc(s1), None, op0))
+            op("V", [in0, s1], [out], lambda: g.vector.tensor_scalar(ap(out), ap(in0), sc(s1), None, op0), size(out, in0))
         else:
-            op("V", [in0, s1, s2], [out], lambda: g.vector.tensor_scalar(ap(out), ap(in0), sc(s1), sc(s2), op0, op1))
+            op("V", [in0, s1, s2], [out], lambda: g.vector.tensor_scalar(ap(out), ap(in0), sc(s1), sc(s2), op0, op1), size(out, in0))
 
-    def tt(out, in0, in1, alu, off=None):
-        a = ap(in0) if off is None else ap(in0).indirect(ap(off))
-        op("V", [in0, in1, off], [out], lambda: g.vector.tensor_tensor(ap(out), a, ap(in1), alu))
+    def tt(out, in0, in1, alu):
+        n = len(cols(out)) * (1 if SCRATCH[in0[0]][0] == "psum" else 2)
+        op("V", [in0, in1], [out], lambda: g.vector.tensor_tensor(ap(out), ap(in0), ap(in1), alu), n)
 
     def cp(out, in_, off=None):
         a = ap(in_) if off is None else ap(in_).indirect(ap(off))
-        op("V", [in_, off], [out], lambda: g.vector.tensor_copy(ap(out), a))
+        op("V", [in_, off], [out], lambda: g.vector.tensor_copy(ap(out), a), picked(out) if off else size(out, in_))
 
     def fill(out, c):
-        op("V", [], [out], lambda: g.vector.memset(ap(out), c))
+        op("V", [], [out], lambda: g.vector.memset(ap(out), c), size(out))
 
     def red(out, in_):
-        op("V", [in_], [out], lambda: g.vector.tensor_reduce(ap(out), ap(in_), AxisListType.X, ADD))
+        op("V", [in_], [out], lambda: g.vector.tensor_reduce(ap(out), ap(in_), AxisListType.X, ADD), len(cols(in_)))
 
-    def act(out, in_, func, off=None, acc=None, **kw):
+    def scan(out, d0, d1, first, op1):
+        op("V", [d0, d1, first], [out], lambda: g.vector.tensor_tensor_scan(ap(out), ap(d0), ap(d1), sc(first), ADD, op1), size(out, d0, d1))
+
+    def act(out, in_, func=AF.Identity, off=None, acc=None, **kw):
         a = ap(in_) if off is None else ap(in_).indirect(ap(off))
         k2 = {k: sc(x) for k, x in kw.items()}
         if acc is not None:
             k2["accum_out"] = ap(acc)
-        op("S", [in_, off] + list(kw.values()), [out] + ([acc] if acc else []), lambda: g.scalar.activation(ap(out), a, func, **k2))
+        op("S", [in_, off] + list(kw.values()), [out] + ([acc] if acc else []), lambda: g.scalar.activation(ap(out), a, func, **k2),
+           (picked(out) + 20 if off else max(COST["S"], len(cols(out)))) + (25 if acc else 0))
 
     def quant(name, a, b, tile, ta):
         c, s, t = v(name + "c", a, b), v(name + "s", a, b), v(tile, ta, ta + 4 * (b - a))
-        op("V", [t], [c, s], lambda: g.vector.quantize_mx(ap(c), ap(s), ap(t)))
+        op("V", [t], [c, s], lambda: g.vector.quantize_mx(ap(c), ap(s), ap(t)), 15 + 1.06 * (b - a))
 
     def mm(bank, w, wa, x, xa, n, start=True, stop=True):
         wc, ws, xc, xs = v(w + "c", wa, wa + 128), v(w + "s", wa, wa + 128), v(x + "c", xa, xa + n), v(x + "s", xa, xa + n)
         o = v("p%d" % bank, 0, n)
-        op("PE", [wc, ws, xc, xs], [o], lambda: g.tensor.matmul_mx(ap(o), ap(wc), ap(ws), ap(xc), ap(xs), start, stop))
+        op("PE", [wc, ws, xc, xs], [o], lambda: g.tensor.matmul_mx(ap(o), ap(wc), ap(ws), ap(xc), ap(xs), start, stop), COST["mm"] * (n + 16))
 
     def pick_c(out, at, n, win, a, b, off):
         o, w = v(out + "c", at, at + n), v(win + "c", a, b)
-        op("V", [w, off], [o], lambda: g.vector.tensor_copy(ap(o).bitcast(dt.uint32), ap(w).bitcast(dt.uint32).indirect(ap(off))))
+        op("V", [w, off], [o], lambda: g.vector.tensor_copy(ap(o).bitcast(dt.uint32), ap(w).bitcast(dt.uint32).indirect(ap(off))), picked(o))
 
     def pick_s(out, at, n, win, a, b, off, on="S"):
         if on == "S":
@@ -238,243 +382,276 @@ def rank_program(g, core, T, topo):
         else:
             cp(v(out + "s", at, at + n), v(win + "s", a, b), off=off)
 
+    def pick(*a):
+        pick_c(*a)
+        pick_s(*a)
+
     def iota(out, pattern, base=0, cm=0):
+        n, after = 160 + 2 * len(cols(out)), [(i, 0.0) for i in sends[-1:]]
         if SCRATCH[out[0]][2] == I32:
-            op("G", [], [out], lambda: g.iota(ap(out), pattern, base, cm))
+            op("G", [], [out], lambda: g.iota(ap(out), pattern, base, cm), n, after)
         else:
-            op("G", [], [out], lambda: g.iota(ap(out), pattern, base, cm, allow_small_or_imprecise_dtypes=True))
+            op("G", [], [out], lambda: g.iota(ap(out), pattern, base, cm, allow_small_or_imprecise_dtypes=True), n, after)
+
+    j0 = {}
 
     def scatter_half(src, h, land, at, stage):
+        nh = helped(stage)
         for kind in "cs":
             dst = v(land + kind, at + S * q, at + S * q + S)
             block = lambda x, n=1: v(src + kind, S * x, S * (x + n))
-            sem, hsem, hbuf = T.sem["a%d%s" % (stage, kind)], T.sem["ah%d%s" % (stage, kind)], ap(v("h%d%s" % (stage, kind)))
-            direct = [4, 5, 6] if h == 1 else [] if stage == 1 else [0, 1]
+            sem, hsem = T.sem["a%d%s" % (stage, kind)], T.sem["ah%d%s" % (stage, kind)]
+            hbuf = ap(v("h%d%s" % (stage, kind), 0, S * nh // 2))
+            direct = [4, 5, 6] if h == 1 else list(range(4 - nh))
             tr, n = [], 0
             if direct:
                 masks, nd = deal(far, len(direct), kind == "s")
                 tr += [transfer(topo, core, [T.cores[peers[x]]], m, sem, ap(block(x)), ap(dst), kind) for x, m in zip(direct, masks)]
                 n += sum(nd)
-            if h == 0 and stage == 1:
+            if h == 0 and nh == 4:
                 tr += [transfer(topo, core, [c], bits(e), hsem, ap(block(2 * k, 2)), hbuf, kind)
                        for k, (c, e) in enumerate(zip(helpers, (far, near)))]
                 n += len(far) + len(near)
             elif h == 0:
-                masks, nh = deal(near, 2)
+                masks, nn = deal(near, 2)
                 tr += [transfer(topo, core, [c], m, hsem, ap(block(2 + k)), hbuf, kind) for k, (c, m) in enumerate(zip(helpers, masks))]
-                n += sum(nh)
-            send(tr, [block(4 * h, 4 - h)], n)
+                n += sum(nn)
+            j = send(tr, [block(4 * h, 4 - h)], n)
             if h == 1:
                 dma("Y", dst, block(NR - 1), codes=kind == "c")
-                arrives("a%d%s" % (stage, kind), (2 + stage) * len(far), [v(land + kind, at + S * r, at + S * r + S) for r in peers])
+                arrives("a%d%s" % (stage, kind), (3 if nh == 4 else 4) * len(far), [v(land + kind, at + S * r, at + S * r + S) for r in peers],
+                        [(j, COST["a%d%s" % (stage, kind)]), (j0[kind], COST["h%d%s" % (stage, kind)])])
+            j0[kind] = j
 
-    cf = lambda k: v("cf", k, k + 1)
-    dc = lambda k: v("dc", k, k + 1)
+    cf = lambda k, n=1: v("cf", k, k + n)
+    ci = lambda k, n=1: v("ci", k, k + n)
+    dc = lambda k, n=1: v("dc", k, k + n)
     pb = lambda k, a, b, step=None, rows=(0, 128): v("p%d" % k, a, b, step, rows)
     shift = lambda x, b: v("dh", 4 * x + b, 4 * x + b + 1)
-    E, WH, SEL, WA, WB, WD, W0 = 0, 512, 768, 896, 1024, 1152, 1280
-    IO, YT, LR, U32L, HXL, THL = 0, 128, 256, 368, 384, 448
-    oU16, oU32, oRA, oR4, oMQ = v("so", 0, 8), v("so", 8, 24), v("so", 24, 32), v("so", 32, 40), v("so", 40, 48)
-    oTH, oLA0, oLA1 = v("so", 112, 116), v("so", 116, 117), v("so", 118, 120)
-    lr0, lr0b, lr1 = v("lref", 0, 64), v("lref", 64, 80), v("lref", 80, 112)
-    io = lambda a, b: v("idx", IO + a, IO + b)
+    io = lambda a, b: v("ib", a, b)
+    E, ONE, SEL, WA, WB, WD = 0, 512, 640, 768, 896, 1024
+    tk = lambda at, t=None: v("tk", 4 * (at - ONE), 4 * (at - ONE) + 512) if t is None else v("tk", 4 * (at - ONE) + t, 4 * (at - ONE) + 512, 4)
+    LR, MREF, LR1, KBL, PPL = v("idx", 0, 64), v("idx", 64, 128), v("idx", 128, 160), v("idx", 160, 164), v("idx", 168, 176)
+    lr1, lr2 = v("lr", 0, 32), v("lr", 32, 64)
+    oR4, oU16, oRA, oRR, oLA0, oMQ, oKB, oLA1 = (v("so", a, b) for a, b in ((0, 8), (8, 16), (32, 40), (40, 56), (56, 57), (58, 74),
+                                                                            (122, 126), (126, 128)))
+    oU32 = lambda h: v("so", 16 + 8 * h, 24 + 8 * h)
+    PP, D16x16, M16x16, D16, M16, D4, M32, G4, M4 = cf(0), cf(3), cf(5), cf(13), cf(15), cf(16), cf(17), cf(18), cf(19)
+    NUM, D32, C14, M4x4, NB32, CUT, CLA, I8 = (cf(20 + k) for k in range(8))
 
     dma("Y", v("t1", 0, 64), v("r0"))
     dma("S", v("t1", 64, 72), v("u", 0, 8))
     fill(v("t1", 72, 512), 0.0)
-    dma("Y", v("tr", 0, 256), v("r1"))
-    dma("S", v("tr", 256, 1280), v("r2"))
-    dma("Y", v("tw"), v("w"))
-
-    iota(v("ci", 0, 1), [[0, 1]], 0, 1)
+    dma("Y", v("ta", 0, 256), v("r1"), behind=0.2)
+    dma("Y", v("tr"), v("r2"), behind=0.6)
+    dma("Y", v("tw"), v("w"), behind=1.6)
+    for k, m in enumerate((1, 4, 16)):
+        iota(ci(k), [[0, 1]], 0, m)
     iota(io(0, 128), [[1, 128]])
-    iota(v("idx", YT, YT + 128), [[0, 8], [1, 4], [0, 4]])
-    iota(v("idx", LR + 80, LR + 112), [[32, 4], [1, 8]])
-
-    zeros = 4 * WH
-    fill(v("tk", zeros, zeros + 1024), 0.0)
-    act(v("tk", 0, 1024), v("tk", zeros, zeros + 1024), AF.Copy)
-    for k, m in ((1, 15), (2, 112), (3, 3), (4, 31), (5, 96), (6, 64), (9, 111)):
-        ts(v("ci", k, k + 1), v("ci", 0, 1), m, AND)
-    for k, sh, m in ((7, 2, 3), (8, 4, 3), (10, 2, 27)):
-        ts(v("ci", k, k + 1), v("ci", 0, 1), sh, SHR, m, AND)
-    cp(v("cf", 0, 11), v("ci", 0, 11))
-    act(v("tx0"), v("tk", zeros, zeros + 528), AF.Copy)
-    for k, src, mul, add in ((11, 1, 16.0, 16.0), (12, 3, 4.0, 0.0), (13, 1, 1.0, -16.0), (14, 3, 1.0, -16.0),
-                             (20, 2, -1.0, 0.0), (21, 6, -1.0, 0.0), (22, 5, -1.0, 0.0)):
-        act(cf(k), cf(src), AF.Identity, scale=mul, bias=add)
-    act(v("tx1"), v("tk", zeros, zeros + 576), AF.Copy)
+    fill(v("tz"), 0.0)
+    fill(v("tx"), 0.0)
+    ts(ci(3, 3), ci(0, 3), 0xF0, AND)
+    ts(ci(6, 2), ci(1, 2), 0x1F0, AND)
+    ts(ci(8, 2), ci(1, 2), 0x30, AND)
+    cp(cf(0, 10), ci(0, 10))
 
     quant("q1", 0, 128, "t1", 0)
     for kind in "cs":
         x = v("q1" + kind, 0, W1)
         at = lambda r: v("l0" + kind, W1 * ((q - r - 1) % NR), W1 * ((q - r - 1) % NR) + W1)
-        send([transfer(topo, core, [T.cores[r] for r in peers], bits(far), T.sem["a0" + kind], ap(x), [ap(at(r)) for r in peers], kind)],
-             [x], len(far))
-        dma("Y", at(q), x, codes=kind == "c")
-        arrives("a0" + kind, len(far) * len(peers), [v("l0" + kind, 0, W1 * (NR - 1))])
+        j = send([transfer(topo, core, [T.cores[r] for r in peers], bits(far), T.sem["a0" + kind], ap(x), [ap(at(r)) for r in peers], kind)],
+                 [x], len(far))
+        dma("Y", at(q), x, codes=kind == "c", behind=1.5)
+        arrives("a0" + kind, len(far) * len(peers), [v("l0" + kind, 0, W1 * (NR - 1))], [(j, COST["a0" + kind])])
     dma("Y", v("l2c", 0, 2), v("q1c", 32, 34), codes=True)
     dma("Y", v("l2s", 0, 2), v("q1s", 32, 34))
 
-    iota(v("idx", LR, LR + 64), [[16, 8], [1, 8]])
-    iota(v("idx", LR + 64, LR + 80), [[4, 2], [64, 2], [1, 4]])
-    iota(v("idx", U32L, U32L + 16), [[W1, 8], [0, 2]], P)
-    iota(v("idx", HXL, HXL + 64), [[4, 8], [0, 8]])
-    iota(v("idx", THL, THL + 4), [[32, 2], [4, 2]])
+    iota(io(128, 256), [[0, 8], [1, 4], [0, 4]])
+    iota(LR, [[16, 8], [1, 8]])
+    iota(v("of", 74, 122), [[1, 3], [4, 8], [0, 2]])
+    iota(KBL, [[4, 2], [0, 2]])
+    iota(MREF, [[0, 2], [1, 32]])
+    iota(v("iref"), [[0, 2], [1, 8], [0, 4]])
+    iota(LR1, [[32, 4], [1, 8]])
+    iota(PPL, [[-128, 2], [1, 4]], 0, -1)
+    if CFG["ty"] == "G":
+        iota(v("ty"), [[0, 576]])
+    elif CFG["ty"] == "S":
+        act(v("ty"), v("tx"), AF.Copy)
+    else:
+        fill(v("ty"), 0.0)
 
-    for t in range(4):
-        ts(v("tk", 4 * SEL + t, 4 * SEL + 512, 4), v("idx", YT, YT + 128), float(t), EQ)
-    fill(v("tk", 1024, 2048), 0.0)
-    for x in range(4):
-        ts(cf(16 + x), cf(8), float(x), EQ, cf(11), MUL)
+    act(cf(10, 10), cf(0, 10), scale=1.0 / 16)
+    act(tk(ONE), v("tx", 0, 512), scale=0.0, bias=1.0)
+    act(v("ta", 256, 260), v("t1", 64, 68))
+    act(v("ta", 260, 264), v("t1", 64, 68), scale=-1.0)
+    act(v("ta", 264, 448), v("t1", 0, 184))
+    act(v("ta", 448, 512), v("t1", 0, 64), scale=-1.0)
+    act(v("ty", 256, 320, 4, rows=(0, 1)), v("ib", 1, 17, rows=(0, 1)), scale=1.0 / 32)
+    act(v("ty", 257, 320, 4, rows=(0, 1)), v("ib", 1, 17, rows=(0, 1)), scale=0.0, bias=-1.0)
+    ts(v("tz", 3, 515, 4), io(0, 128), PP, EQ)
+    ts(oR4, io(0, 8), 4.0, MUL, G4, ADD)
     for b in range(4):
-        ts(v("tk", 512 * b + b, 512 * b + 512, 4), io(0, 128), cf(0), EQ)
-    quant("qr", 0, 320, "tr", 0)
-    sel = v("tk", 4 * SEL, 4 * SEL + 512)
-    act(v("tk", 4 * W0, 4 * W0 + 512), sel, AF.Identity, scale=0.0, bias=cf(11))
-    for at, k in ((WA, 1), (WB, 2), (WD, 12)):
-        act(v("tk", 4 * at, 4 * at + 512), sel, AF.Identity, scale=cf(k))
-    for h in range(2):
-        for x in range(4):
-            a = 4 * WH + 512 * h + 128 * x + 64 * h
-            act(v("tk", a, a + 64), v("tk", 4 * SEL, 4 * SEL + 64), AF.Identity, scale=cf(16 + x))
-    ts(oR4, io(0, 8), 4.0, MUL, cf(7), ADD)
-    quant("qk", 0, 512, "tk", 0)
-    pick_c("r4", 0, 128, "q1", 0, 128, oR4)
-    pick_s("r4", 0, 128, "q1", 0, 128, oR4, on="V")
+        quant("qk", E + 128 * b, E + 128 * b + 128, "tz", 3 - b)
+    for out, src, mul, add in ((NUM, M16x16, 1.0, 16.0), (C14, M4, 1.0, -16.0), (M4x4, M4, 4.0, 0.0), (NB32, PP, -1.0, M32),
+                               (CUT, D16x16, 1.0, M - 0.5), (CLA, NB32, -1.0, M16), (I8, NB32, 0.25, D4), (D32, NB32, -1.0 / 32, 0.0)):
+        act(out, src, scale=mul, bias=add)
+    act(cf(28, 2), v("ib", 2, 49, 46), bias=M16)
+    pick("r4", 0, 128, "q1", 0, 128, oR4)
+    quant("qa", 0, 128, "ta", 0)
+    quant("qr", 0, 256, "tr", 0)
     for b in range(4):
         mm(b, "qk", E + 128 * b, "r4", 0, 128, True, False)
-        mm(b, "qk", E + 128 * b, "qr", 0, 128, False, True)
-    for b in range(4):
-        act(v("s0", b, 256, 4), pb(b, 0, 64), AF.Copy)
-    for out, a, b, k in ((lr0, 0, 64, 20), (lr0b, 64, 80, 21), (lr1, 80, 112, 22)):
-        act(out, v("idx", LR + a, LR + b), AF.Identity, bias=cf(k))
-    ts(oU16, io(0, 8), float(W1), MUL, float(P), ADD)
-    ts(v("so", 24, 25 + q), io(NR - 1 - q, NR), float(W1), MUL, cf(1), ADD)
-    if q < NR - 1:
-        ts(v("so", 25 + q, 32), io(0, NR - 1 - q), float(W1), MUL, cf(1), ADD)
-    cp(oU32, v("idx", U32L, U32L + 16))
-    ts(v("so", 48, 112), v("idx", HXL, HXL + 64), cf(3), ADD)
-    ts(v("diag"), io(0, 16), cf(1), EQ)
-    ts(v("thr0"), io(0, 16), cf(1), GE, TINY, MUL)
-    ts(oTH, v("idx", THL, THL + 4), cf(10), ADD)
-    for b in range(2):
-        ts(v("base1", 32 * b, 32 * b + 32), io(0, 32), cf(4), GE, TINY, MUL)
-    fill(oMQ, P)
+        mm(b, "qk", E + 128 * b, "qa", 0, 128, False, True)
+    for t in range(4):
+        ts(tk(SEL, t), io(128, 256), float(t), EQ)
+    act(v("of", 8, 16), io(0, 8), scale=float(W1), bias=float(P))
+    for k in range(2):
+        act(v("of", 16 + k, 32, 2), io(0, 8), scale=float(W1), bias=float(P))
+        act(v("of", 40 + 8 * k, 48 + 8 * k), io(0, 8), scale=0.0, bias=cf(28 + k))
+        fill(v("so", 58 + 8 * k, 66 + 8 * k), k)
+    turn = (NR - 1 - q) or NR // 2
+    act(v("of", 32, 40 - turn), io((NR - 1 - q) % NR, (NR - 1 - q) % NR + NR - turn), scale=float(W1), bias=M16)
+    act(v("of", 40 - turn, 40), io((NR - 1 - q + NR - turn) % NR, (NR - 1 - q + NR - turn) % NR + turn), scale=float(W1), bias=M16)
+    act(v("of", 56, 58), io(0, 2), scale=0.0, bias=PP)
+    cp(v("so", 8, 58), v("of", 8, 58))
+    act(v("of", 126, 128), io(0, 2), scale=16.0, bias=CLA)
+    act(v("of", 122, 126), KBL, bias=D32)
+    cp(v("so", 74, 128), v("of", 74, 128))
+    ts(tk(WA), tk(SEL), M16, MUL)
+    act(tk(WB), tk(SEL), scale=D16x16)
+    act(tk(WD), tk(SEL), scale=M4x4)
+    quant("qw", 0, 128, "tw", 0)
+    ts(v("diag"), io(0, 16), M16, EQ)
+    ts(v("mx"), io(0, 8), D16, EQ, CUT, MUL)
+    ts(v("thra"), io(0, 128), PP, GE, TINY, MUL)
+    pick("rr", 0, 256, "qa", R1, 128, oRR)
+    pick("mq", 0, 256, "qa", R1, 128, oMQ)
+    ts(v("base1"), MREF, M32, GE, TINY, MUL)
+    ts(v("mask"), MREF, D4, EQ)
     fill(v("n2", 16, 32), 0.0)
-    ts(oLA1, io(0, 2), 16.0, MUL, cf(9), ADD)
-    cp(oLA0, cf(0))
-    ts(v("thra"), io(0, 128), cf(0), GE, TINY, MUL)
-    ts(v("plc"), io(Z // 16, Z // 16 + 16), 16.0, MUL, cf(1), ADD)
-    pick_c("mq", 0, 128, "q1", 0, 128, oMQ)
-    pick_s("mq", 0, 128, "q1", 0, 128, oMQ)
-    quant("qk", 896, 1408, "tk", 3584)
-    quant("qk", 512, 896, "tk", 2048)
+    for b in range(4):
+        act(v("s0", 64 * b, 64 * b + 64), pb(b, 0, 64), AF.Copy)
+    for at, n in ((ONE, 256), (WA, 256), (WD, 128)):
+        quant("qk", at, at + n, "tk", 4 * (at - ONE))
+    act(lr1, LR1, bias=NB32)
+    act(lr2, lr1, bias=128.0 * (M - 1))
+    act(v("step"), io(0, 64), scale=4 * TINY)
+    act(v("ppb"), PPL, scale=TINY, bias=0.5 * TINY)
 
     def one_hot(out, ref, lcol, fcol):
         ts(out, ref, lcol, EQ, fcol, MUL)
-
-    def spread_slots(bank):
-        mm(bank, "qk", W0, "x0", 4, 128)
-
-    def spread_parents(bank):
-        mm(bank, "qk", WH, "x0", 0, 128, True, False)
-        mm(bank, "qk", WH + 128, "x0", 2, 128, False, True)
 
     def spread_numbers(x, bank):
         mm(bank, "qk", SEL, x, 16, 128, True, False)
         mm(bank, "qk", WD, x, 0, 128, False, True)
 
+    slots = lambda t: v(t, 0, 256, 4)
+    flags = lambda t, b: v(t, 256 + 32 * b, 288 + 32 * b)
+    nums = lambda t, b: v(t, 320 + 32 * b, 352 + 32 * b)
+
     pick_c("u16", 0, 128, "l0", 0, L0, oU16)
     pick_c("ra", 0, 128, "l0", 0, L0, oRA)
-    pick_c("u32", 0, 256, "l0", 0, L0, oU32)
     pick_s("u16", 0, 128, "l0", 0, L0, oU16)
     pick_s("ra", 0, 128, "l0", 0, L0, oRA, on="V")
-    quant("qw", 0, 128, "tw", 0)
-    for b in range(2):
-        mm(b, "qk", E + 128 * b, "l0", 0, L0)
-    mm(4, "u16", 0, "ra", 0, 128)
-    mm(7, "mq", 0, "ra", 0, 128)
-    mm(6, "ra", 0, "q1", 0, 128)
-    for b in range(2, 4):
-        mm(b, "qk", E + 128 * b, "l0", 0, L0)
-    pick_s("u32", 0, 256, "l0", 0, L0, oU32)
-    for b in range(4):
-        act(v("dh", b, 32, 4), pb(b, P + 1, L0, W1), AF.Copy)
     for h in range(2):
-        act(v("hx", 512 * h, 512 * h + 512), v("dh"), AF.Copy, off=v("so", 48 + 32 * h, 80 + 32 * h))
+        pick_c("u32", 128 * h, 128, "l0", 0, L0, oU32(h))
+        pick_s("u32", 128 * h, 128, "l0", 0, L0, oU32(h), on=CFG["u%d" % h])
+    for b in range(4):
+        mm(b, "qk", E + 128 * b, "l0", 0, L0)
+    mm(5, "u16", 0, "rr", 0, 128, True, False)
+    mm(5, "rr", 128, "u16", 0, 128, False, True)
+    mm(4, "u16", 0, "ra", 0, 128)
+    mm(7, "mq", 0, "ra", 0, 128, True, False)
+    mm(7, "ra", 0, "mq", 128, 128, False, True)
+    tt(v("cl"), pb(5, 0, 128), v("thra"), GE)
+    act(v("junk", 512, 528), v("cl"), off=oLA0, acc=dc(2), bias=D16)
+    ts(v("tx", 384, 448), LR, dc(2), EQ)
+    one_hot(slots("tx"), LR, dc(2), NUM)
+    quant("x0", 0, 128, "tx", 0)
+    mm(5, "qk", WA, "x0", 0, 128, True, False)
+    mm(5, "qk", WB, "x0", 0, 128, False, True)
+    ts(v("do0"), pb(5, 96, 112), 4.0, MUL, M4, ADD)
+    mm(6, "qk", ONE, "x0", 0, 128)
     o0, o1 = P * q, P * q + P
     tt(v("dm"), pb(4, o0, o1), v("diag"), MUL)
     red(dc(0), v("dm"))
-    ts(v("da"), pb(7, 0, 128), pb(6, P, P + 1), SUB)
-    ts(v("d0"), pb(4, o0, o1), dc(0), SUB)
-    if o0 > 0:
-        ts(v("c0", 0, o0), pb(4, 0, o0), dc(0), GE)
-    if o1 < 128:
-        ts(v("c0", o1, 128), pb(4, o1, 128), dc(0), GT)
-    tt(v("c0", o0, o1), v("d0"), v("thr0"), GE)
-    red(dc(1), v("c0"))
-    red(dc(2), v("c0", o0, o1))
-    ts(dc(3), dc(1), M - 0.5, LT)
-    one_hot(v("tx0", 16, 272, 4), lr0, dc(2), dc(3))
-    one_hot(v("tx0", 0, 16), lr0b, dc(2), dc(3))
-    quant("x0", 0, 132, "tx0", 0)
-    spread_slots(5)
-    spread_parents(6)
-    tt(v("ca"), v("da"), v("thra"), GE)
-    ts(v("do0"), pb(5, 0, 64), cf(13), ADD, 0.0, MAX)
+    cut = min(max(o0, 32), 80) if q in (0, NR - 1) else o0
+    for a, b in ((0, cut), (cut, 112)):
+        low = b <= o0
+        ts(v("c0", a, b), pb(4, a if low else a + P, b if low else b + P), dc(0), GE if low else GT)
+    scan(v("run0"), v("c0"), v("c0"), dc(2), MAX)
+    ts(v("ty", 448, 480, 4), v("mx"), v("run0", 111, 112), GT)
 
-    act(v("g2"), v("s0"), AF.Copy, off=v("do0", 48, 64))
-    for x in range(2):
+    for b in range(4):
+        act(v("dh", b, 32, 4), pb(b, P + 1, L0, W1), AF.Copy)
+    for x in range(NR):
         for b in range(4):
-            act(v("tch", 768 + 128 * x + b, 896 + 128 * x, 4), v("g2", 128 * x + b, 128 * x + 128, 4), AF.Identity, bias=shift(6 + x, b))
-    act(v("ms"), pb(5, 0, 64), AF.Copy)
-    act(v("thd"), v("ms"), AF.Relu, off=oTH, scale=-HUGE, bias=HUGE)
-    act(v("dc", 4, 6), pb(6, 0, 2), AF.Copy)
-    act(v("dc", 6, 8), pb(6, 0, 2), AF.Sign)
-    act(v("junk", 0, 16), v("ca"), AF.Identity, off=oLA0, acc=dc(11))
-    act(v("junk", 336, 464), v("ca"), AF.Identity, acc=dc(10))
+            o, i = v("tch", 256 * x + b, 256 * x + 256, 4), v("s0", 64 * b, 64 * b + 64)
+            if 8 * b + (x + 3 * (x % 2)) % 8 < CFG["bv"]:
+                ts(o, i, pb(b, W1 * x + P + 1, W1 * x + P + 2) if 8 * b + 8 <= CFG["bv"] else shift(x, b), ADD)
+            else:
+                act(o, i, bias=shift(x, b))
+    nq = CFG["nq"]
+    for k in range(nq):
+        quant("al", 512 // nq * k, 512 // nq * (k + 1), "tch", 2048 // nq * k)
+    for b in range(3):
+        act(v("hx", 256 * b, 256 * b + 256), v("dh"), AF.Copy, off=v("so", 74 + 16 * b, 90 + 16 * b))
+
+    tt(v("ca"), pb(7, 0, 128), v("thra"), GE)
+    scan(v("runa"), v("ca"), v("ca"), 0.0, MAX)
+    ts(dc(12), v("runa", 127, 128), M - 0.5, LT, NUM, MUL)
+    act(v("junk", 0, 16), v("ca"), off=oLA0, acc=dc(11), bias=D16)
+    one_hot(slots("ty"), LR, dc(11), dc(12))
+    quant("xa", 0, 128, "ty", 0)
+    mm(7, "qk", ONE, "xa", 0, 128)
+    act(v("m4"), pb(7, 0, 64), scale=0.25)
+    act(v("inv"), v("m4"), AF.Relu, scale=-HUGE, bias=HUGE)
+    tt(v("pm", 64, 128), pb(7, 0, 64), v("mask"), MUL)
+    tt(v("pf"), v("inv"), v("step"), ADD)
+    for k in range(8):
+        act(v("thr", 256 * (k // 4) + k % 4, 256 * (k // 4) + 256, 4), v("pf"), bias=v("ppb", k, k + 1))
+    for b in range(2):
+        act(v("junk", 80 + 32 * b, 112 + 32 * b), v("pm", 64 + 32 * b, 96 + 32 * b), acc=dc(14 + b))
+    act(dc(16, 2), dc(14, 2), AF.Sign)
+    act(v("val", 0, 256), v("thr", 0, 256), AF.Relu, scale=-1.0, bias=1.0)
+    for k in range(4):
+        act(v("n1", 256 + k, 512, 4, rows=(0, 1)), v("m4", rows=(0, 1)), AF.Relu, bias=float(k - 3))
+    act(v("n1", 0, 256, rows=(0, 1)), v("n1", 256, 512, rows=(0, 1)), bias=-1.0)
+    dma("Y", v("nm", 0, 256, rows=(0, 1)), v("n1", 0, 256, rows=(0, 1)))
+
+    act(v("k8"), pb(7, 112, 120), AF.Copy)
+    act(v("kb"), v("k8"), AF.Copy, off=oKB)
+    tt(v("keep"), v("kb"), v("iref"), GT)
+    ts(dc(6, 2), v("kb", 0, 64, 32), I8, GT)
+    tt(v("pm", 0, 64), pb(6, 0, 64), v("mask"), MUL)
+    for b in range(2):
+        act(v("junk", 16 + 32 * b, 48 + 32 * b), v("pm", 32 * b, 32 * b + 32), acc=dc(4 + b), scale=dc(6 + b))
     for h in range(2):
-        a, n = 512 * h, 512 - 256 * h
-        tt(v("tch", a, a + n), v("s0"), v("hx", a, a + n), ADD, off=v("do0", 32 * h, 32 * h + n // 16))
-        quant("ch", 128 * h, 128 * h + 128, "tch", 512 * h)
+        pick_c("ch", 128 * h, 128, "al", 0, 256 * h + 256, v("do0", 8 * h, 8 * h + 8))
+        pick_s("ch", 128 * h, 128, "al", 0, 256 * h + 256, v("do0", 8 * h, 8 * h + 8), on=CFG["cs"][h])
         mm(2 * h, "u32", 128 * h, "ch", 128 * h, 128)
         mm(2 * h + 1, "ch", 128 * h, "l0", 0, L0)
         scatter_half("ch", h, "l1", 0, 1)
 
     for b in range(2):
+        lo, hi = 32 * b, 32 * b + 32
         for x in range(4):
             rows, c = (32 * x, 32 * x + 32), W1 * (4 * b + x) + P
-            ts(v("d1", 32 * b, 32 * b + 32, rows=rows), pb(2 * b, 32 * x, 32 * x + 32, rows=rows), pb(2 * b + 1, c, c + 1, rows=rows), SUB)
-        if b == 0:
-            tt(v("thr1"), v("thd"), v("base1"), MAX)
-    tt(v("c1"), v("d1"), v("thr1"), GE)
-    ts(dc(12), dc(10), M - 0.5, LT)
-    for b in range(2):
-        red(dc(8 + b), v("c1", 32 * b, 32 * b + 32))
-    one_hot(v("tx0", 16, 272, 4), lr0, dc(11), dc(12))
-    for b in range(2):
-        one_hot(v("tx1", 32 * b, 32 * b + 32), lr1, dc(8 + b), dc(6 + b))
-    for b in range(2):
-        one_hot(v("tx1", 64 + 32 * b, 96 + 32 * b), lr1, dc(8 + b), dc(4 + b))
-    one_hot(v("tx0", 0, 16), lr0b, dc(11), dc(12))
-    quant("x1", 0, 144, "tx1", 0)
+            ts(v("d1", lo, hi, rows=rows), pb(2 * b, 32 * x, 32 * x + 32, rows=rows), pb(2 * b + 1, c, c + 1, rows=rows), SUB)
+        tt(v("c1", lo, hi), v("d1", lo, hi), v("base1", lo, hi), GE)
+        scan(v("run1", lo, hi), back("c1", lo, hi), back("keep", lo, hi), 0.0, MUL)
+        one_hot(flags("tx", b), lr1, v("run1", hi - 1, hi), dc(6 + b))
+        one_hot(nums("tx", b), lr1, v("run1", hi - 1, hi), dc(4 + b))
+    quant("x1", 0, 144, "tx", 0)
     mm(4, "qk", WA, "x1", 0, 128, True, False)
     mm(4, "qk", WB, "x1", 0, 128, False, True)
-    spread_numbers("x1", 7)
-    quant("x0", 0, 132, "tx0", 0)
-    spread_slots(6)
-    spread_parents(5)
-    ts(v("do1", 0, 16), pb(4, 0, 16), 0.0, ADD)
+    spread_numbers("x1", 5)
+    ts(v("do1", 0, 16), pb(4, 64, 80), 0.0, ADD)
+    ts(v("do1", 16, 32), pb(5, 64, 80), C14, ADD, 0.0, MAX)
     for h in range(2):
-        for pick in (pick_c, pick_s):
-            pick("pv", 128 * h, 128, "ch", 128 * h, 128 * h + 128, v("do1", 8 * h, 8 * h + 8))
-        if h == 0:
-            ts(v("do1", 16, 32), pb(7, 0, 16), cf(14), ADD, 0.0, MAX)
-            act(v("m4"), pb(6, 0, 64), AF.Identity, scale=0.25)
-            act(v("dc", 14, 16), pb(5, 0, 2), AF.Copy)
-        for pick in (pick_c, pick_s):
-            pick("pe", 128 * h, 128, "qr", R1, 320, v("do1", 16 + 8 * h, 24 + 8 * h))
+        pick("pv", 128 * h, 128, "ch", 128 * h, 128 * h + 128, v("do1", 8 * h, 8 * h + 8))
+        pick("pe", 128 * h, 128, "qr", 0, 256, v("do1", 16 + 8 * h, 24 + 8 * h))
         for b in range(4):
             mm(4 * h + b, "qk", E + 128 * b, "pv", 128 * h, 128, True, False)
         for b in range(4):
@@ -482,73 +659,60 @@ def rank_program(g, core, T, topo):
 
     for h in range(2):
         for b in range(3):
-            tt(v("tgr", 512 * h + b, 512 * h + 512, 4), pb(4 * h + b, 0, 128), v("hx", 512 * h + b, 512 * h + 512, 4), ADD)
+            tt(v("tgr", 512 * h + b, 512 * h + 512, 4), pb(4 * h + b, 0, 128), v("hx", 256 * b + 128 * h, 256 * b + 128 * h + 128), ADD)
         for x in range(4):
             a = 512 * h + 128 * x
-            act(v("tgr", a + 3, a + 128, 4), pb(4 * h + 3, 32 * x, 32 * x + 32), AF.Identity, bias=shift(4 * h + x, 3))
+            act(v("tgr", a + 3, a + 128, 4), pb(4 * h + 3, 32 * x, 32 * x + 32), bias=shift(4 * h + x, 3))
         quant("gr", 128 * h, 128 * h + 128, "tgr", 512 * h)
         scatter_half("gr", h, "l2", Z, 2)
-        if h == 0:
-            for k in range(4):
-                act(v("n1p", k, 256, 4), v("m4"), AF.Relu, bias=float(k - 3))
 
-    mm(0, "mq", 0, "l1", 0, 256)
     for b in range(2):
-        mm(1 + b, "l1", 128 * b, "q1", 0, 128)
-    mm(3, "qw", 0, "l1", 0, 256)
-    act(v("cap"), v("n1p"), AF.Identity, scale=CAPV, bias=-0.5 * CAPV)
-    act(v("dc", 16, 18), v("dc", 14, 16), AF.Sign)
+        for h in range(2):
+            mm(2 * b + h, "mq", 0, "l1", 128 * h, 128, True, False)
+            mm(2 * b + h, "l1", 128 * b, "mq", 128, 128, False, True)
+    mm(4, "qw", 0, "l1", 0, 256)
     for b in range(2):
-        act(dc(26 + b), pb(1 + b, P, P + 1), AF.Identity, scale=-1.0)
-        act(dc(28 + b), pb(1 + b, P, P + 1), AF.Copy)
-    tt(v("am"), pb(0, 0, 256), v("cap"), MIN)
+        for h in range(2):
+            a = 256 * b + 128 * h
+            tt(v("cb", a, a + 128), pb(2 * b + h, 0, 128), v("thr", a, a + 128), GE)
+        act(v("junk", 144 + 32 * b, 176 + 32 * b), v("cb", 384 * b, 384 * b + 128), off=oLA1, acc=dc(20 + b), bias=4.0 * (M - 1))
+        if b == 0:
+            act(v("junk", 256, 512), v("cb", 0, 256), acc=dc(22))
+    scan(v("runb"), v("cb", 256, 512), v("cb", 256, 512), 0.0, MAX)
+    ts(dc(24), dc(22), 128.0, MUL, dc(20), MAX)
+    ts(dc(25), v("runb", 255, 256), 128.0, MUL, dc(21), MAX)
     for b in range(2):
-        o = 128 * (1 - b)
-        act(v("db", 128 * b, 128 * b + 128), v("am", 128 * b, 128 * b + 128), AF.Identity, bias=dc(26 + b))
-        ts(v("cb", 256 * b + o, 256 * b + o + 128), v("am", o, o + 128), dc(28 + b), GE if b else GT)
-    for b in range(2):
-        o = 256 * b + 128 * (1 - b)
-        act(v("junk", 80 + 128 * b, 208 + 128 * b), v("cb", o, o + 128), AF.Identity, acc=dc(30 + b))
-    act(v("dc", 32, 34), v("dc", 30, 32), AF.Identity, bias=1.0 - M)
-    for b in range(2):
-        own = v("cb", 384 * b, 384 * b + 128)
-        tt(own, v("db", 128 * b, 128 * b + 128), v("thra"), GE)
-        act(v("junk", 16 + 32 * b, 48 + 32 * b), own, AF.Identity, off=oLA1, acc=dc(20 + b))
-    act(v("val"), v("n1p"), AF.Sign)
-    act(v("n1", rows=(0, 1)), v("n1p", rows=(0, 1)), AF.Identity, bias=-1.0)
-    dma("Y", v("nm", 0, 256, rows=(0, 1)), v("n1", rows=(0, 1)))
-    for b in range(2):
-        own, run, nil = v("cb", 384 * b, 384 * b + 128), v("junk", 464 + 128 * b, 592 + 128 * b), v("tx1", 256, 384)
-        op("V", [own, nil, dc(32 + b)], [run], lambda: g.vector.tensor_tensor_scan(ap(run), ap(own), ap(nil), ap(dc(32 + b)), ADD, ADD))
-    for b in range(2):
-        ts(dc(24 + b), v("junk", 591 + 128 * b, 592 + 128 * b), 128.0, MUL, dc(20 + b), MAX)
-    for b in range(2):
-        one_hot(v("tx1", 32 * b, 32 * b + 32), lr1, dc(24 + b), dc(16 + b))
-    for b in range(2):
-        one_hot(v("tx1", 64 + 32 * b, 96 + 32 * b), lr1, dc(24 + b), dc(14 + b))
-    quant("x2", 0, 144, "tx1", 0)
-    mm(4, "qk", SEL, "x2", 0, 128)
-    spread_numbers("x2", 7)
-    tt(v("y0"), pb(3, 0, 256), v("val"), MUL)
-    dma("Y", v("y", 0, 256), v("y0"))
-    tt(v("o2"), pb(4, 0, 16), v("plc"), MUL)
-    ts(v("n2", 0, 16), pb(7, 0, 16), cf(14), ADD, -1.0, MAX)
-    cp(v("do2"), v("o2"))
+        one_hot(flags("ty", b), lr2, dc(24 + b), dc(16 + b))
+        one_hot(v("ty", 128 * b, 128 * b + 128, 4), lr2, dc(24 + b), dc(16 + b))
+        one_hot(nums("ty", b), lr2, dc(24 + b), dc(14 + b))
+    quant("x2", 0, 144, "ty", 0)
+    mm(5, "qk", ONE, "xa", 0, 128, True, False)
+    mm(5, "qk", SEL, "x2", 0, 128, False, True)
+    mm(7, "qk", ONE, "x2", 0, 128)
+    spread_numbers("x2", 6)
+    ts(v("do2"), pb(5, 64, 80), 512.0, MUL, M16, ADD)
+    for k in range(4):
+        act(v("val", 256 + k, 512, 4), pb(7, 0, 64), AF.Copy)
+    for h in range(2):
+        tt(v("yy", 128 * h, 128 * h + 128), pb(4, 128 * h, 128 * h + 128), v("val", 128 * h, 128 * h + 128), MUL)
+    dma("Y", v("y", 0, 256), v("yy", 0, 256))
+    ts(v("n2", 0, 16), pb(6, 64, 80), C14, ADD, -1.0, MAX)
 
     a, b = v("n2t", rows=(0, 32)), v("n2", rows=(0, 32))
-    op("V", [b], [a], lambda: g.vector.transpose(ap(a), ap(b)))
+    op("V", [b], [a], lambda: g.vector.transpose(ap(a), ap(b)), 32)
     dma("Y", v("nm", 256, 512, rows=(0, 1)), v("n2t", 0, 16, rows=(0, 16)))
     for h in range(2):
         pick_c("fin", 128 * h, 128, "l2", 0, Z + 256, v("do2", 8 * h, 8 * h + 8))
-        pick_s("fin", 128 * h, 128, "l2", 0, Z + 256, v("do2", 8 * h, 8 * h + 8))
-        mm(5 + h, "qw", 0, "fin", 128 * h, 128)
     dma("Y", v("oc"), v("finc"), codes=True)
-    cp(v("y1", 0, 128), pb(5, 0, 128))
-    dma("Y", v("y", 256, 384), v("y1", 0, 128))
-    act(v("y1", 128, 256), pb(6, 0, 128), AF.Copy)
-    dma("S", v("y", 384, 512), v("y1", 128, 256))
+    for h in range(2):
+        lo, hi = 256 + 128 * h, 384 + 128 * h
+        mm(h, "qw", 0, "l2", Z + 128 * h, 128)
+        tt(v("yy", lo, hi), pb(h, 0, 128), v("val", lo, hi), MUL)
+        dma("YS"[h], v("y", lo, hi), v("yy", lo, hi))
+        pick_s("fin", 128 * h, 128, "l2", 0, Z + 256, v("do2", 8 * h, 8 * h + 8), on=CFG["fs"][h])
     for k in range(4):
-        dma("YS"[k % 2], v("osc", rows=(4 * k, 4 * k + 4)), v("fins", rows=(32 * k, 32 * k + 4)))
+        dma("YSYS"[k], v("osc", rows=(4 * k, 4 * k + 4)), v("fins", rows=(32 * k, 32 * k + 4)))
 
+    schedule()
     for sem, n in final.items():
         wait("G", (sem, n))

@@ -1,41 +1,43 @@
 from concourse.bass import DstId, RemoteDMATransfer
 from concourse.mybir import dt, AluOpType, AxisListType, ActivationFunctionType
 
-CFG = {"h2": 4, "bv": 16, "nq": 2, "cs": "SS", "u0": "V", "u1": "S", "fs": "SS", "ty": "G", "tries": 300, "seed": 1}
+CFG = {"bv": (8, 8), "fw": 0, "moves": 2500, "tries": 30, "seed": 1}
 COST = {"cycle": 0.00083, "V": 64, "S": 80, "PE": 0, "G": 0, "pick0": 60, "pick": 1.5, "mm": 0.75, "issue": 0.05, "dma": 1.1,
-        "wide": 0.001, "send": 0.15, "first": 1.3, "a0c": 2.4, "a0s": 3.2, "a1c": 2.0, "a1s": 2.4, "a2c": 2.0, "a2s": 2.4,
-        "h1c": 4.1, "h1s": 4.3, "h2c": 2.9, "h2s": 3.1}
-CASES = ((1.0, 0.21, 1.0), (1.0, 0.21, 0.8), (1.2, 0.25, 1.3), (1.1, 0.15, 1.1))
+        "wide": 0.001, "send": 0.15, "first": 1.3, "a0c": 1.5, "a0s": 1.75, "b0c": 1.3, "b0s": 1.1, "anc": 4.3, "ans": 4.6,
+        "d0c": 2.3, "d0s": 2.7, "straightc": 2.0, "straights": 2.4, "helpedc": 2.9, "helpeds": 3.1}
+CASES = ((1.0, 1.0, 0.21, 1.0), (1.0, 0.75, 0.22, 0.9), (1.45, 1.3, 0.21, 1.0), (1.4, 1.3, 0.25, 1.5), (1.1, 1.0, 0.21, 1.3),
+         (1.0, 0.7, 0.17, 1.1))
 NR, P, CAP, M, S = 8, 16, 8, 40, 32
 W1 = P + 2
-L0 = NR * W1
+HALF = NR // 2 * W1
+LB = 96 - HALF
 R1 = 4 * P
 Z = 16
 TINY, HUGE = 2.0 ** -110, 2.0 ** 90
 Q4, U8, BF, F32, I32, U16 = "float8_e4m3fn_x4", "uint8", "bfloat16", "float32", "int32", "uint16"
 
 SCRATCH = {}
-for _n, _w in (("q1", 128), ("qa", 128), ("qr", 256), ("qw", 128), ("qk", 1152), ("l0", L0), ("u16", 128), ("u32", 256), ("ra", 128),
-               ("r4", 128), ("mq", 256), ("rr", 256), ("al", 512), ("x0", 128), ("xa", 128), ("x1", 144), ("x2", 144), ("ch", 256),
-               ("l1", 256), ("h1", 2 * S), ("h2", 2 * S), ("pv", 256), ("pe", 256), ("gr", 256), ("l2", Z + 256), ("fin", 256)):
+for _n, _w in (("q1", 128), ("qa", 128), ("qr", 256), ("qw", 128), ("qk", 1152), ("l0", 224), ("u16", 128), ("u32", 256), ("ra", 128),
+               ("r4", 128), ("mq", 256), ("rr", 256), ("al", 512), ("x0", 128), ("xa", 128), ("xk", 128), ("x1", 144), ("x2", 128),
+               ("ch", 256), ("l1", 256), ("h0", S), ("ln", S * NR), ("h1", 2 * S), ("h2", 2 * S), ("pv", 256), ("pe", 256),
+               ("gr", 256), ("l2", Z + 256), ("fin", 256)):
     SCRATCH[_n + "c"] = ("sbuf", [128, _w], Q4)
     SCRATCH[_n + "s"] = ("sbuf", [128, _w], U8)
 for _n, _w, _d in (("t1", 512, BF), ("ta", 512, BF), ("tr", 1024, BF), ("tw", 512, BF), ("tz", 516, BF), ("tk", 2560, BF), ("tx", 576, BF),
-                   ("ty", 576, BF), ("tch", 2048, BF), ("tgr", 1024, BF), ("ci", 16, I32), ("cf", 32, F32), ("ib", 256, BF),
-                   ("idx", 176, F32), ("of", 128, F32), ("so", 128, U16), ("do0", 16, U16), ("do1", 32, U16), ("do2", 16, U16),
-                   ("mx", 8, F32), ("iref", 64, BF), ("thra", 128, BF), ("base1", 64, BF), ("diag", 16, F32), ("mask", 64, F32),
-                   ("lr", 64, F32), ("ppb", 8, F32), ("step", 64, F32), ("s0", 256, F32), ("dh", 32, F32), ("hx", 768, F32),
-                   ("dc", 32, F32), ("dm", 16, F32), ("cl", 128, BF), ("c0", 112, BF), ("run0", 112, BF), ("k8", 8, F32),
-                   ("kb", 64, F32), ("keep", 64, BF), ("d1", 64, BF), ("c1", 64, BF), ("run1", 64, F32), ("pm", 128, F32),
-                   ("ca", 128, BF), ("runa", 128, BF), ("junk", 528, F32), ("m4", 64, F32), ("inv", 64, F32), ("pf", 64, F32),
-                   ("thr", 512, BF), ("val", 512, F32), ("cb", 512, BF), ("runb", 256, BF), ("n1", 512, F32),
-                   ("n2", 32, F32), ("n2t", 32, F32), ("yy", 512, F32)):
+                   ("ty", 512, BF), ("tch", 2048, BF), ("tgr", 1024, BF), ("ci", 16, I32), ("cf", 40, F32), ("ib", 384, BF),
+                   ("idx", 168, F32), ("of", 100, F32), ("so", 100, U16), ("do0", 16, U16), ("do1", 32, U16), ("do2", 16, U16),
+                   ("mx", 2, F32), ("thra", 128, BF), ("diag", 16, F32), ("mask", 64, F32), ("lr", 64, F32), ("ppb", 4, F32),
+                   ("step", 64, F32), ("s0", 256, F32), ("dh", 32, F32), ("hx", 384, F32), ("dc", 32, F32), ("dm", 16, F32),
+                   ("cl", 128, BF), ("c0", 112, BF), ("run0", 112, BF), ("c1", 288, BF), ("ov", 4, U16),
+                   ("pm", 128, F32), ("ca", 128, BF), ("runa", 128, BF), ("junk", 288, F32), ("m4", 64, F32), ("inv", 64, F32),
+                   ("pf", 64, F32), ("thr", 512, F32), ("val", 512, F32), ("cb", 512, BF), ("runb", 512, BF), ("n1", 512, F32),
+                   ("n2", 256, F32), ("yy", 512, F32)):
     SCRATCH[_n] = ("sbuf", [128, _w], _d)
 for _k in range(8):
     SCRATCH["p%d" % _k] = ("psum", [128, 512], F32)
 
-DMAS = ["ld%d" % _k for _k in range(24)]
-SEMAPHORES = ["V", "S", "PE", "G", "sent", "a0c", "a0s", "a1c", "a1s", "a2c", "a2s", "ah1c", "ah1s", "ah2c", "ah2s"] + DMAS
+DMAS = ["ld%d" % _k for _k in range(32)]
+SEMAPHORES = ["V", "S", "PE", "G", "sent"] + [_a + _k for _a in ("a0", "b0", "an", "a1", "a2", "ah0", "ah1", "ah2") for _k in "cs"] + DMAS
 
 ADD, SUB, MUL, MAX, MIN = AluOpType.add, AluOpType.subtract, AluOpType.mult, AluOpType.max, AluOpType.min
 GE, GT, LT, EQ = AluOpType.is_ge, AluOpType.is_gt, AluOpType.is_lt, AluOpType.is_equal
@@ -85,10 +87,6 @@ def transfer(topo, src, dsts, mask, sem, a, b, kind):
     return RemoteDMATransfer(dst_ids=ids, dma_engine_mask=mask, remote_sem=sem, src=a, dsts=b)
 
 
-def helped(stage):
-    return 4 if stage == 1 else CFG["h2"]
-
-
 def helper_program(g, core, T, topo):
     own = [c for c in T.cores if core in helpers_of(c, T, topo)]
     if not own:
@@ -96,16 +94,21 @@ def helper_program(g, core, T, topo):
     q = T.rank_of(own[0])
     k = helpers_of(own[0], T, topo).index(core)
     far, near = engine_sets(core, own[0], T, topo)
+    to = [(q + i) % NR for i in range(1, NR)][4 * k:4 * k + 4]
+    for kind in "cs":
+        g.wait_ge(T.sem["ah0" + kind], len(near))
+        g.remote_dma_fused([transfer(topo, core, [T.cores[r] for r in to], bits(far), T.sem["an" + kind], T["h0" + kind][:, 0:S],
+                                     [T["ln" + kind][:, S * ((q - r - 1) % NR):S * ((q - r - 1) % NR) + S] for r in to], kind)],
+                           local_sem=T.sem.sent)
+    masks = deal(far, 2)[0]
     for stage, at in ((1, 0), (2, Z)):
-        n = helped(stage) // 2
-        masks = deal(far, n)[0]
         for kind in "cs":
-            g.wait_ge(T.sem["ah%d%s" % (stage, kind)], len((far, near)[k]) if n == 2 else deal(near, 2)[1][k])
-            g.remote_dma_fused([transfer(topo, core, [T.cores[(q + 5 - 2 * n + n * k + i) % NR]], masks[i], T.sem["a%d%s" % (stage, kind)],
+            g.wait_ge(T.sem["ah%d%s" % (stage, kind)], len((far, near)[k]))
+            g.remote_dma_fused([transfer(topo, core, [T.cores[(q + 1 + 2 * k + i) % NR]], masks[i], T.sem["a%d%s" % (stage, kind)],
                                          T["h%d%s" % (stage, kind)][:, S * i:S * i + S],
-                                         T["l%d%s" % (stage, kind)][:, at + S * q:at + S * q + S], kind) for i in range(n)],
+                                         T["l%d%s" % (stage, kind)][:, at + S * q:at + S * q + S], kind) for i in range(2)],
                                local_sem=T.sem.sent)
-    g.wait_ge(T.sem.sent, 4 * len(far))
+    g.wait_ge(T.sem.sent, 6 * len(far))
 
 
 def best_order(queue, busy, lag, pred, banks):
@@ -116,20 +119,27 @@ def best_order(queue, busy, lag, pred, banks):
             succ[i].append(j)
 
     def edges(case):
-        kb, wait, fly = case
-        b = [busy[i] * (kb if queue[i] in "VSPE" else fly) for i in range(n)]
-        return b, [[(i, b[i] + wait * w + fly * f) for i, (w, f) in pred[j].items()] for j in range(n)], [fly * x for x in lag], wait
+        kb, pe, wait, fly = case
+        b = [busy[i] * (kb if queue[i] in "VS" else pe if queue[i] == "PE" else fly) for i in range(n)]
+        return (b, [[(i, b[i] + wait * w + fly * f) for i, (w, f) in pred[j].items()] for j in range(n)], [fly * x for x in lag], wait,
+                20.0 / (8 + 6 * kb + 6 * fly))
 
     cases = [edges(c) for c in CASES]
 
-    def place(way):
-        b, pre, tail, wait = cases[0]
-        start, taken, miss = [0.0] * n, {}, [len(p) for p in pred]
+    def place(way, back=False):
+        b, pre, tail, wait = cases[0][:4]
+        nxt, first = succ, [0.0] * n
+        if back:
+            nxt, first, fore, pre = pred, tail, pre, [[] for _ in range(n)]
+            for j in range(n):
+                for i, d in fore[j]:
+                    pre[i].append((j, d - b[i] + b[j]))
+        start, taken, miss = [0.0] * n, {}, [len(p) for p in pre]
         ready = [j for j in range(n) if not miss[j]]
         while ready:
             j = max(ready, key=lambda j: (way[j], -j))
             ready.remove(j)
-            t = max([start[i] + d for i, d in pre[j]] + [0.0])
+            t = max([start[i] + d for i, d in pre[j]] + [first[j]])
             spans = taken.get(queue[j], [])
             if banks[j]:
                 spans = sorted(spans + [(s[0] - wait, s[1] + wait) for k in banks[j] for s in taken.get(k, []) if s[2] != queue[j]])
@@ -143,51 +153,103 @@ def best_order(queue, busy, lag, pred, banks):
             taken[queue[j]].sort()
             for k in banks[j]:
                 taken.setdefault(k, []).append((t, t + b[j], queue[j]))
-            for k in succ[j]:
+            for k in nxt[j]:
                 miss[k] -= 1
                 if not miss[k]:
                     ready.append(k)
+        return start
+
+    def sort(start):
         return sorted(range(n), key=lambda j: (start[j], j))
 
     def length(order):
-        total = 0.0
-        for b, pre, tail, wait in cases:
-            start, free, last, end = [0.0] * n, {}, {}, 0.0
+        total, chains = 0.0, []
+        for b, pre, tail, wait, weight in cases:
+            start, why, free, last, end, j1 = [0.0] * n, [-1] * n, {}, {}, 0.0, 0
             for j in order:
-                t = free.get(queue[j], 0.0)
+                t, w = free.get(queue[j], (0.0, -1))
                 for i, d in pre[j]:
                     if start[i] + d > t:
-                        t = start[i] + d
+                        t, w = start[i] + d, i
                 for k in banks[j]:
-                    for e, x in last.get(k, {}).items():
+                    for e, (x, i) in last.get(k, {}).items():
                         if e != queue[j] and x + wait > t:
-                            t = x + wait
-                start[j] = t
-                free[queue[j]] = t + b[j]
+                            t, w = x + wait, i
+                start[j], why[j] = t, w
+                free[queue[j]] = (t + b[j], j)
                 for k in banks[j]:
-                    last.setdefault(k, {})[queue[j]] = t + b[j]
-                end = max(end, t + b[j] + tail[j])
-            total += end
-        return total
+                    last.setdefault(k, {})[queue[j]] = (t + b[j], j)
+                if t + b[j] + tail[j] > end:
+                    end, j1 = t + b[j] + tail[j], j
+            total += end * weight
+            chain = []
+            while why[j1] >= 0:
+                if why[j1] not in pred[j1]:
+                    chain.append((why[j1], j1))
+                j1 = why[j1]
+            chains.append(chain)
+        return total, chains
 
-    b, pre, tail, wait = cases[0]
+    b, pre, tail, wait = cases[0][:4]
     way = [b[i] + tail[i] for i in range(n)]
     for j in range(n - 1, -1, -1):
         for i, d in pre[j]:
             way[i] = max(way[i], d + way[j])
-    best = place(way)
-    least, state = length(best), CFG["seed"]
+    best = sort(place(way))
+    state = [CFG["seed"]]
+
+    def draw(m):
+        state[0] = (state[0] * 1103515245 + 12345) % 2147483648
+        return (state[0] >> 8) % m
+
+    least = length(best)[0]
     for k in range(CFG["tries"]):
         trial = list(way)
         for _ in range(1 + k % 24):
-            state = (state * 1103515245 + 12345) % 2147483648
-            j = (state >> 8) % n
-            state = (state * 1103515245 + 12345) % 2147483648
-            trial[j] += ((state >> 8) % 2001 - 1000) / 1000.0
-        order = place(trial)
-        t = length(order)
-        if t <= least:
-            best, least, way = order, t, trial
+            trial[draw(n)] += (draw(2001) - 1000) / 1000.0
+        start = place(trial)
+        for _ in range(2):
+            late = place([start[j] + b[j] for j in range(n)], True)
+            trial = [late[j] + b[j] for j in range(n)]
+            start = place(trial)
+            order = sort(start)
+            t = length(order)[0]
+            if t <= least:
+                best, least, way = order, t, trial
+    now, (t0, chains) = best, length(best)
+    for k in range(CFG["moves"]):
+        chain = chains[draw(len(chains))]
+        if not chain:
+            continue
+        i, j = chain[draw(len(chain))]
+        order = list(now)
+        a, z = order.index(i), order.index(j)
+        if draw(2):
+            more = draw(3)
+            while more and a > 0:
+                a -= 1
+                more -= queue[order[a]] == queue[j]
+            lift = {j}
+            for x in reversed(order[a:z]):
+                if any(x in pred[y] for y in lift):
+                    lift.add(x)
+            order[a:z + 1] = [x for x in order[a:z + 1] if x in lift] + [x for x in order[a:z + 1] if x not in lift]
+        else:
+            more = draw(4)
+            while more and z < n - 1:
+                z += 1
+                more -= queue[order[z]] == queue[i]
+            sink = {i}
+            for x in order[a + 1:z + 1]:
+                if not sink.isdisjoint(pred[x]):
+                    sink.add(x)
+            order[a:z + 1] = [x for x in order[a:z + 1] if x not in sink] + [x for x in order[a:z + 1] if x in sink]
+        t, c = length(order)
+        if t <= t0 + 0.25 * (1 - k / CFG["moves"]) * draw(1000) / 1000.0:
+            now, t0, chains = order, t, c
+            if t < least:
+                best, least = order, t
+    ORDERS["least"] = least / len(cases)
     return best
 
 
@@ -209,9 +271,6 @@ def rank_program(g, core, T, topo):
 
     def v(name, a=None, b=None, step=None, rows=(0, 128)):
         return (name, rows, slice(a, b, step))
-
-    def back(name, a, b):
-        return v(name, b - 1, a - 1 if a else None, -1)
 
     def ap(x):
         return T[x[0]][x[1][0]:x[1][1], x[2]]
@@ -275,9 +334,9 @@ def rank_program(g, core, T, topo):
     def sc(x):
         return ap(x) if isinstance(x, tuple) else x
 
-    def dma(e, out, in_, codes=False, behind=0.0):
+    def dma(e, out, in_, codes=False, behind=0.0, landed=()):
         def emit():
-            order(e, [in_], [out])
+            order(e, [in_] + list(landed), [out])
             sem = free_sems.pop(0)
             a, b = ap(out), ap(in_)
             if codes:
@@ -291,7 +350,10 @@ def rank_program(g, core, T, topo):
                 if x[0] in SCRATCH:
                     hist.setdefault(x[0], []).append(("dma", (sem, 16), wr, x[1], cols(x)))
         wide = len(cols(out if out[0] in SCRATCH else in_))
-        return later(e, [in_], [out], COST["issue"], (0, COST["dma"] + COST["wide"] * wide + behind), emit)
+        if out[0] not in SCRATCH:
+            j = later(e, [in_], [], COST["issue"], (0, 0.9), emit)
+            return later("D", [], [], 0.03 + (in_[1][1] - in_[1][0] == 128) * (0.04 + 0.002 * wide), (0, 0.15), lambda: None, [(j, 0.9)])
+        return later(e, [in_] + list(landed), [out], COST["issue"], (0, COST["dma"] + COST["wide"] * wide + behind), emit)
 
     def arrives(sem, n, views, after):
         later(sem, [], views, 0.0, (0, 0.0), lambda: note("far", (sem, n), [], views), after)
@@ -305,6 +367,15 @@ def rank_program(g, core, T, topo):
             final["sent"] = final.get("sent", 0) + n
         sends.append(later("G", reads, [], COST["send"] if sends else COST["first"], (0, 0.0), emit, [(i, 0.0) for i in sends[-1:]]))
         return sends[-1]
+
+    def in_turn(first, queues):
+        last = {}
+        for j in range(first, len(plan)):
+            e = plan[j][0]
+            if e in queues:
+                if e in last:
+                    plan[j][6].append((last[e], 0.0))
+                last[e] = j
 
     def schedule():
         key = tuple(x[0] for x in plan)
@@ -321,7 +392,7 @@ def rank_program(g, core, T, topo):
                 for x, wr, cx in mine:
                     seen.setdefault(x[0], []).append((j, wr, x[1], cx))
                 pred.append(d)
-            banks = [{x[0] for x in p[1] + p[2] if SCRATCH[x[0]][0] == "psum"} for p in plan]
+            banks = [sorted({x[0] for x in p[1] + p[2] if SCRATCH[x[0]][0] == "psum"}) for p in plan]
             ORDERS[key] = best_order([p[0] for p in plan], [p[3] for p in plan], [p[4][1] for p in plan], pred, banks)
         for j in ORDERS[key]:
             plan[j][5]()
@@ -334,9 +405,8 @@ def rank_program(g, core, T, topo):
 
     def ts(out, in0, s1, op0, s2=None, op1=None):
         if op1 is None:
-            op("V", [in0, s1], [out], lambda: g.vector.tensor_scalar(ap(out), ap(in0), sc(s1), None, op0), size(out, in0))
-        else:
-            op("V", [in0, s1, s2], [out], lambda: g.vector.tensor_scalar(ap(out), ap(in0), sc(s1), sc(s2), op0, op1), size(out, in0))
+            return op("V", [in0, s1], [out], lambda: g.vector.tensor_scalar(ap(out), ap(in0), sc(s1), None, op0), size(out, in0))
+        return op("V", [in0, s1, s2], [out], lambda: g.vector.tensor_scalar(ap(out), ap(in0), sc(s1), sc(s2), op0, op1), size(out, in0))
 
     def tt(out, in0, in1, alu):
         n = len(cols(out)) * (1 if SCRATCH[in0[0]][0] == "psum" else 2)
@@ -352,8 +422,8 @@ def rank_program(g, core, T, topo):
     def red(out, in_):
         op("V", [in_], [out], lambda: g.vector.tensor_reduce(ap(out), ap(in_), AxisListType.X, ADD), len(cols(in_)))
 
-    def scan(out, d0, d1, first, op1):
-        op("V", [d0, d1, first], [out], lambda: g.vector.tensor_tensor_scan(ap(out), ap(d0), ap(d1), sc(first), ADD, op1), size(out, d0, d1))
+    def running_sum(out, x, first):
+        op("V", [x, first], [out], lambda: g.vector.tensor_tensor_scan(ap(out), ap(x), ap(x), sc(first), ADD, MAX), size(out, x))
 
     def act(out, in_, func=AF.Identity, off=None, acc=None, **kw):
         a = ap(in_) if off is None else ap(in_).indirect(ap(off))
@@ -363,14 +433,15 @@ def rank_program(g, core, T, topo):
         op("S", [in_, off] + list(kw.values()), [out] + ([acc] if acc else []), lambda: g.scalar.activation(ap(out), a, func, **k2),
            (picked(out) + 20 if off else max(COST["S"], len(cols(out)))) + (25 if acc else 0))
 
-    def quant(name, a, b, tile, ta):
+    def quant(name, a, b, tile, ta, after=()):
         c, s, t = v(name + "c", a, b), v(name + "s", a, b), v(tile, ta, ta + 4 * (b - a))
-        op("V", [t], [c, s], lambda: g.vector.quantize_mx(ap(c), ap(s), ap(t)), 15 + 1.06 * (b - a))
+        return op("V", [t], [c, s], lambda: g.vector.quantize_mx(ap(c), ap(s), ap(t)), 15 + 1.06 * (b - a), after)
 
-    def mm(bank, w, wa, x, xa, n, start=True, stop=True):
+    def mm(bank, w, wa, x, xa, n, start=True, stop=True, after=()):
         wc, ws, xc, xs = v(w + "c", wa, wa + 128), v(w + "s", wa, wa + 128), v(x + "c", xa, xa + n), v(x + "s", xa, xa + n)
         o = v("p%d" % bank, 0, n)
-        op("PE", [wc, ws, xc, xs], [o], lambda: g.tensor.matmul_mx(ap(o), ap(wc), ap(ws), ap(xc), ap(xs), start, stop), COST["mm"] * (n + 16))
+        return op("PE", [wc, ws, xc, xs], [o], lambda: g.tensor.matmul_mx(ap(o), ap(wc), ap(ws), ap(xc), ap(xs), start, stop),
+                  COST["mm"] * (n + 16), after)
 
     def pick_c(out, at, n, win, a, b, off):
         o, w = v(out + "c", at, at + n), v(win + "c", a, b)
@@ -382,12 +453,12 @@ def rank_program(g, core, T, topo):
         else:
             cp(v(out + "s", at, at + n), v(win + "s", a, b), off=off)
 
-    def pick(*a):
-        pick_c(*a)
-        pick_s(*a)
+    def pick(out, at, n, win, a, b, off, on="S"):
+        pick_c(out, at, n, win, a, b, off)
+        pick_s(out, at, n, win, a, b, off, on)
 
-    def iota(out, pattern, base=0, cm=0):
-        n, after = 160 + 2 * len(cols(out)), [(i, 0.0) for i in sends[-1:]]
+    def iota(out, pattern, base=0, cm=0, behind=None):
+        n, after = 160 + 2 * len(cols(out)), [] if behind is None else [(sends[behind], 0.0)]
         if SCRATCH[out[0]][2] == I32:
             op("G", [], [out], lambda: g.iota(ap(out), pattern, base, cm), n, after)
         else:
@@ -396,48 +467,38 @@ def rank_program(g, core, T, topo):
     j0 = {}
 
     def scatter_half(src, h, land, at, stage):
-        nh = helped(stage)
         for kind in "cs":
             dst = v(land + kind, at + S * q, at + S * q + S)
             block = lambda x, n=1: v(src + kind, S * x, S * (x + n))
-            sem, hsem = T.sem["a%d%s" % (stage, kind)], T.sem["ah%d%s" % (stage, kind)]
-            hbuf = ap(v("h%d%s" % (stage, kind), 0, S * nh // 2))
-            direct = [4, 5, 6] if h == 1 else list(range(4 - nh))
-            tr, n = [], 0
-            if direct:
-                masks, nd = deal(far, len(direct), kind == "s")
-                tr += [transfer(topo, core, [T.cores[peers[x]]], m, sem, ap(block(x)), ap(dst), kind) for x, m in zip(direct, masks)]
-                n += sum(nd)
-            if h == 0 and nh == 4:
-                tr += [transfer(topo, core, [c], bits(e), hsem, ap(block(2 * k, 2)), hbuf, kind)
-                       for k, (c, e) in enumerate(zip(helpers, (far, near)))]
-                n += len(far) + len(near)
-            elif h == 0:
-                masks, nn = deal(near, 2)
-                tr += [transfer(topo, core, [c], m, hsem, ap(block(2 + k)), hbuf, kind) for k, (c, m) in enumerate(zip(helpers, masks))]
-                n += sum(nn)
-            j = send(tr, [block(4 * h, 4 - h)], n)
-            if h == 1:
+            name = "%d%s" % (stage, kind)
+            if h == 0:
+                j0[kind] = send([transfer(topo, core, [c], bits(e), T.sem["ah" + name], ap(block(2 * k, 2)), ap(v("h" + name)), kind)
+                                 for k, (c, e) in enumerate(zip(helpers, (far, near)))], [block(0, 4)], len(far) + len(near))
+            else:
+                masks = deal(far, 3, kind == "s")[0]
+                j = send([transfer(topo, core, [T.cores[peers[4 + k]]], m, T.sem["a" + name], ap(block(4 + k)), ap(dst), kind)
+                          for k, m in enumerate(masks)], [block(4, 3)], len(far))
                 dma("Y", dst, block(NR - 1), codes=kind == "c")
-                arrives("a%d%s" % (stage, kind), (3 if nh == 4 else 4) * len(far), [v(land + kind, at + S * r, at + S * r + S) for r in peers],
-                        [(j, COST["a%d%s" % (stage, kind)]), (j0[kind], COST["h%d%s" % (stage, kind)])])
-            j0[kind] = j
+                arrives("a" + name, 3 * len(far), [v(land + kind, at + S * r, at + S * r + S) for r in peers],
+                        [(j, COST["straight" + kind]), (j0[kind], COST["helped" + kind])])
 
     cf = lambda k, n=1: v("cf", k, k + n)
     ci = lambda k, n=1: v("ci", k, k + n)
     dc = lambda k, n=1: v("dc", k, k + n)
-    pb = lambda k, a, b, step=None, rows=(0, 128): v("p%d" % k, a, b, step, rows)
+    pb = lambda k, a, b, step=None: v("p%d" % k, a, b, step)
     shift = lambda x, b: v("dh", 4 * x + b, 4 * x + b + 1)
-    io = lambda a, b: v("ib", a, b)
+    io = lambda a, b, step=None: v("ib", a, b, step)
+    of = lambda a, b: v("of", a, b)
+    so = lambda a, b: v("so", a, b)
+    junk = lambda k: v("junk", 32 * k, 32 * k + 32)
+    row = lambda name, a=None, b=None, step=None: v(name, a, b, step, (0, 1))
     E, ONE, SEL, WA, WB, WD = 0, 512, 640, 768, 896, 1024
     tk = lambda at, t=None: v("tk", 4 * (at - ONE), 4 * (at - ONE) + 512) if t is None else v("tk", 4 * (at - ONE) + t, 4 * (at - ONE) + 512, 4)
-    LR, MREF, LR1, KBL, PPL = v("idx", 0, 64), v("idx", 64, 128), v("idx", 128, 160), v("idx", 160, 164), v("idx", 168, 176)
+    LR, MREF, LR1, PPL = v("idx", 0, 64), v("idx", 64, 128), v("idx", 128, 160), v("idx", 160, 164)
     lr1, lr2 = v("lr", 0, 32), v("lr", 32, 64)
-    oR4, oU16, oRA, oRR, oLA0, oMQ, oKB, oLA1 = (v("so", a, b) for a, b in ((0, 8), (8, 16), (32, 40), (40, 56), (56, 57), (58, 74),
-                                                                            (122, 126), (126, 128)))
-    oU32 = lambda h: v("so", 16 + 8 * h, 24 + 8 * h)
-    PP, D16x16, M16x16, D16, M16, D4, M32, G4, M4 = cf(0), cf(3), cf(5), cf(13), cf(15), cf(16), cf(17), cf(18), cf(19)
-    NUM, D32, C14, M4x4, NB32, CUT, CLA, I8 = (cf(20 + k) for k in range(8))
+    oR4, oRA, oRR, oLA0, oLA1 = so(0, 8), so(16, 24), so(24, 40), so(40, 41), so(74, 76)
+    PP, D16x16, M16x16, Q16x16, D16, M16, D4, M32, G4, M4 = (cf(k) for k in (0, 3, 5, 8, 14, 16, 17, 18, 20, 21))
+    NUM, CRA, C14, M4x4, NB32, CUT, CLA, I8, G4x, I8x = (cf(22 + k) for k in range(10))
 
     dma("Y", v("t1", 0, 64), v("r0"))
     dma("S", v("t1", 64, 72), v("u", 0, 8))
@@ -448,88 +509,105 @@ def rank_program(g, core, T, topo):
     for k, m in enumerate((1, 4, 16)):
         iota(ci(k), [[0, 1]], 0, m)
     iota(io(0, 128), [[1, 128]])
+    iota(io(128, 256), [[0, 8], [1, 4], [0, 4]])
     fill(v("tz"), 0.0)
-    fill(v("tx"), 0.0)
     ts(ci(3, 3), ci(0, 3), 0xF0, AND)
     ts(ci(6, 2), ci(1, 2), 0x1F0, AND)
-    ts(ci(8, 2), ci(1, 2), 0x30, AND)
-    cp(cf(0, 10), ci(0, 10))
+    ts(ci(8, 3), ci(0, 3), 0x30, AND)
+    cp(cf(0, 11), ci(0, 11))
 
     quant("q1", 0, 128, "t1", 0)
+    place = lambda kind, k: ap(v("l0" + kind, LB + W1 * (NR - 2 - k), LB + W1 * (NR - 1 - k)))
     for kind in "cs":
         x = v("q1" + kind, 0, W1)
-        at = lambda r: v("l0" + kind, W1 * ((q - r - 1) % NR), W1 * ((q - r - 1) % NR) + W1)
-        j = send([transfer(topo, core, [T.cores[r] for r in peers], bits(far), T.sem["a0" + kind], ap(x), [ap(at(r)) for r in peers], kind)],
-                 [x], len(far))
-        dma("Y", at(q), x, codes=kind == "c", behind=1.5)
-        arrives("a0" + kind, len(far) * len(peers), [v("l0" + kind, 0, W1 * (NR - 1))], [(j, COST["a0" + kind])])
-    dma("Y", v("l2c", 0, 2), v("q1c", 32, 34), codes=True)
-    dma("Y", v("l2s", 0, 2), v("q1s", 32, 34))
-
-    iota(io(128, 256), [[0, 8], [1, 4], [0, 4]])
-    iota(LR, [[16, 8], [1, 8]])
-    iota(v("of", 74, 122), [[1, 3], [4, 8], [0, 2]])
-    iota(KBL, [[4, 2], [0, 2]])
-    iota(MREF, [[0, 2], [1, 32]])
-    iota(v("iref"), [[0, 2], [1, 8], [0, 4]])
-    iota(LR1, [[32, 4], [1, 8]])
-    iota(PPL, [[-128, 2], [1, 4]], 0, -1)
-    if CFG["ty"] == "G":
-        iota(v("ty"), [[0, 576]])
-    elif CFG["ty"] == "S":
-        act(v("ty"), v("tx"), AF.Copy)
-    else:
-        fill(v("ty"), 0.0)
-
-    act(cf(10, 10), cf(0, 10), scale=1.0 / 16)
-    act(tk(ONE), v("tx", 0, 512), scale=0.0, bias=1.0)
-    act(v("ta", 256, 260), v("t1", 64, 68))
-    act(v("ta", 260, 264), v("t1", 64, 68), scale=-1.0)
-    act(v("ta", 264, 448), v("t1", 0, 184))
+        j = send([transfer(topo, core, [T.cores[r] for r in peers[:3]], bits(far), T.sem["a0" + kind], ap(x),
+                           [place(kind, k) for k in range(3)], kind)], [x], len(far))
+        dma("Y", v("l0" + kind, 96 + 3 * W1, 224), v("q1" + kind, 0, 128 - 3 * W1), codes=kind == "c", behind=1.0)
+        arrives("a0" + kind, 3 * len(far), [v("l0" + kind, 96, 96 + 3 * W1)], [(j, COST["a0" + kind])])
+    if not CFG["fw"]:
+        for kind in "cs":
+            x = v("q1" + kind, 0, W1)
+            j = send([transfer(topo, core, [T.cores[r] for r in peers[3:]], bits(far), T.sem["b0" + kind], ap(x),
+                               [place(kind, k) for k in range(3, 7)], kind)], [x], len(far))
+            arrives("b0" + kind, 4 * len(far), [v("l0" + kind, LB, 96)], [(j, COST["d0" + kind])])
+    act(v("ta", 256, 328), v("t1", 0, 72))
+    act(v("ta", 328, 332), v("t1", 64, 68), scale=-1.0)
+    act(v("ta", 332, 448), v("t1", 76, 192))
     act(v("ta", 448, 512), v("t1", 0, 64), scale=-1.0)
-    act(v("ty", 256, 320, 4, rows=(0, 1)), v("ib", 1, 17, rows=(0, 1)), scale=1.0 / 32)
-    act(v("ty", 257, 320, 4, rows=(0, 1)), v("ib", 1, 17, rows=(0, 1)), scale=0.0, bias=-1.0)
+    quant("qa", 0, 128, "ta", 0)
+    for k, n in ((0, S), (1, 128)):
+        fill(so(42 + 8 * k, 50 + 8 * k), P + 2 * k)
+        pick("mq", 128 * k, n, "qa", R1, 128, so(42 + 8 * k, 42 + 8 * k + n // 16))
+    for kind in "cs":
+        x = v("mq" + kind, 128, 128 + S)
+        j = send([transfer(topo, core, helpers, bits(near), T.sem["ah0" + kind], ap(x), ap(v("h0" + kind)), kind)], [x], len(near))
+        arrives("an" + kind, len(far) * len(peers), [v("ln" + kind, 0, S * NR - S)], [(j, COST["an" + kind])])
+    for kind in "cs" if CFG["fw"] else ():
+        x = v("l0" + kind, 96, 96 + HALF)
+        j = send([transfer(topo, core, [T.cores[peers[3]]], bits(far), T.sem["b0" + kind], ap(x), ap(v("l0" + kind, LB, 96)), kind)],
+                 [x], len(far))
+        arrives("b0" + kind, len(far), [v("l0" + kind, LB, 96)], [(j, COST["b0" + kind])])
+    gone = [v("l0s", 96, 98)]
+    for kind in "cs":
+        dma("Y", v("ln" + kind, S * NR - S, S * NR), v("mq" + kind, 128, 128 + S), codes=kind == "c", landed=gone)
+        dma("Y", v("l2" + kind, 0, 2), v("q1" + kind, 32, 34), codes=kind == "c", landed=gone)
+        for n in (S, 2 * S):
+            dma("Y", v("mq" + kind, n, 2 * n), v("mq" + kind, 0, n), codes=kind == "c", landed=gone)
+
+    iota(LR, [[16, 8], [1, 8]], behind=1)
+    iota(io(256, 384), [[16, 4], [0, 32]], behind=1)
+    iota(of(58, 66), [[W1, 4], [0, 2]], P + LB, behind=1)
+    iota(v("tx"), [[0, 576]], behind=5)
+    iota(v("ty"), [[0, 512]], behind=5)
+    iota(MREF, [[0, 2], [1, 32]], behind=5)
+    iota(LR1, [[32, 4], [1, 8]], behind=5)
+    iota(of(76, 100), [[1, 3], [4, 8]], behind=5)
+    iota(PPL, [[1, 4]], 0, -1, behind=5)
+
+    act(cf(11, 11), cf(0, 11), scale=1.0 / 16)
+    for t in range(4):
+        ts(tk(SEL, t), io(128, 256), float(t), EQ)
+    act(tk(ONE), tk(SEL), scale=0.0, bias=1.0)
+    ts(tk(ONE, 1), io(256, 384), Q16x16, EQ)
+    act(row("ty", 256, 320, 4), row("ib", 1, 17), scale=1.0 / 32)
+    act(row("ty", 258, 320, 4), row("ib", 1, 17), scale=0.0, bias=-1.0)
     ts(v("tz", 3, 515, 4), io(0, 128), PP, EQ)
     ts(oR4, io(0, 8), 4.0, MUL, G4, ADD)
     for b in range(4):
         quant("qk", E + 128 * b, E + 128 * b + 128, "tz", 3 - b)
     for out, src, mul, add in ((NUM, M16x16, 1.0, 16.0), (C14, M4, 1.0, -16.0), (M4x4, M4, 4.0, 0.0), (NB32, PP, -1.0, M32),
-                               (CUT, D16x16, 1.0, M - 0.5), (CLA, NB32, -1.0, M16), (I8, NB32, 0.25, D4), (D32, NB32, -1.0 / 32, 0.0)):
+                               (CUT, D16x16, 1.0, M - 0.5), (CLA, NB32, -1.0, M16), (I8, NB32, 0.25, D4), (CRA, M16, 1.0, float(LB)),
+                               (G4x, G4, 192.0, 0.0), (I8x, I8, 192.0, 0.0)):
         act(out, src, scale=mul, bias=add)
-    act(cf(28, 2), v("ib", 2, 49, 46), bias=M16)
+    act(cf(32, 2), io(0, 49, 48), bias=M16)
     pick("r4", 0, 128, "q1", 0, 128, oR4)
-    quant("qa", 0, 128, "ta", 0)
-    quant("qr", 0, 256, "tr", 0)
     for b in range(4):
         mm(b, "qk", E + 128 * b, "r4", 0, 128, True, False)
         mm(b, "qk", E + 128 * b, "qa", 0, 128, False, True)
-    for t in range(4):
-        ts(tk(SEL, t), io(128, 256), float(t), EQ)
-    act(v("of", 8, 16), io(0, 8), scale=float(W1), bias=float(P))
     for k in range(2):
-        act(v("of", 16 + k, 32, 2), io(0, 8), scale=float(W1), bias=float(P))
-        act(v("of", 40 + 8 * k, 48 + 8 * k), io(0, 8), scale=0.0, bias=cf(28 + k))
-        fill(v("so", 58 + 8 * k, 66 + 8 * k), k)
-    turn = (NR - 1 - q) or NR // 2
-    act(v("of", 32, 40 - turn), io((NR - 1 - q) % NR, (NR - 1 - q) % NR + NR - turn), scale=float(W1), bias=M16)
-    act(v("of", 40 - turn, 40), io((NR - 1 - q + NR - turn) % NR, (NR - 1 - q + NR - turn) % NR + turn), scale=float(W1), bias=M16)
-    act(v("of", 56, 58), io(0, 2), scale=0.0, bias=PP)
-    cp(v("so", 8, 58), v("of", 8, 58))
-    act(v("of", 126, 128), io(0, 2), scale=16.0, bias=CLA)
-    act(v("of", 122, 126), KBL, bias=D32)
-    cp(v("so", 74, 128), v("of", 74, 128))
+        act(of(8 + 4 * k, 12 + 4 * k), io(0, 4), scale=float(W1), bias=float(P + LB * (1 - k)))
+        act(of(24 + 8 * k, 32 + 8 * k), io(0, 8), scale=0.0, bias=cf(32 + k))
+    x0, turn = NR - 1 - q, (NR - 1 - q) or NR // 2
+    act(of(16, 24 - turn), io(x0, x0 + NR - turn), scale=float(W1), bias=CRA)
+    act(of(24 - turn, 24), io((x0 - turn) % NR, (x0 - turn) % NR + turn), scale=float(W1), bias=CRA)
+    act(of(40, 42), io(0, 2), scale=0.0, bias=PP)
+    cp(so(8, 42), of(8, 42))
+    act(of(66, 74), of(58, 66), bias=float(-LB))
+    act(of(74, 76), io(0, 2), scale=16.0, bias=CLA)
+    cp(so(58, 76), of(58, 76))
+    cp(so(76, 100), of(76, 100))
+    act(cf(34, 2), io(0, 2), scale=768.0, bias=G4x)
+    act(cf(36, 2), io(1, 3), scale=16.0, bias=CLA)
+    fill(v("c1", 0, 288, 144), 0.0)
     ts(tk(WA), tk(SEL), M16, MUL)
     act(tk(WB), tk(SEL), scale=D16x16)
     act(tk(WD), tk(SEL), scale=M4x4)
-    quant("qw", 0, 128, "tw", 0)
     ts(v("diag"), io(0, 16), M16, EQ)
-    ts(v("mx"), io(0, 8), D16, EQ, CUT, MUL)
+    ts(v("mx", 0, 1), D16, 4.0, LT, CUT, MUL)
+    ts(v("mx", 1, 2), D16, 4.0, GE, CUT, MUL)
     ts(v("thra"), io(0, 128), PP, GE, TINY, MUL)
     pick("rr", 0, 256, "qa", R1, 128, oRR)
-    pick("mq", 0, 256, "qa", R1, 128, oMQ)
-    ts(v("base1"), MREF, M32, GE, TINY, MUL)
     ts(v("mask"), MREF, D4, EQ)
-    fill(v("n2", 16, 32), 0.0)
     for b in range(4):
         act(v("s0", 64 * b, 64 * b + 64), pb(b, 0, 64), AF.Copy)
     for at, n in ((ONE, 256), (WA, 256), (WD, 128)):
@@ -542,174 +620,169 @@ def rank_program(g, core, T, topo):
     def one_hot(out, ref, lcol, fcol):
         ts(out, ref, lcol, EQ, fcol, MUL)
 
-    def spread_numbers(x, bank):
-        mm(bank, "qk", SEL, x, 16, 128, True, False)
-        mm(bank, "qk", WD, x, 0, 128, False, True)
-
     slots = lambda t: v(t, 0, 256, 4)
     flags = lambda t, b: v(t, 256 + 32 * b, 288 + 32 * b)
-    nums = lambda t, b: v(t, 320 + 32 * b, 352 + 32 * b)
 
-    pick_c("u16", 0, 128, "l0", 0, L0, oU16)
-    pick_c("ra", 0, 128, "l0", 0, L0, oRA)
-    pick_s("u16", 0, 128, "l0", 0, L0, oU16)
-    pick_s("ra", 0, 128, "l0", 0, L0, oRA, on="V")
+    pick("ra", 0, 128, "l0", 0, 96 + HALF, oRA, "V")
     for h in range(2):
-        pick_c("u32", 128 * h, 128, "l0", 0, L0, oU32(h))
-        pick_s("u32", 128 * h, 128, "l0", 0, L0, oU32(h), on=CFG["u%d" % h])
-    for b in range(4):
-        mm(b, "qk", E + 128 * b, "l0", 0, L0)
+        pick("u16", 64 * h, 64, "l0", 96 * h, 96 + HALF * h, so(8 + 4 * h, 12 + 4 * h))
+        pick("u32", 128 * h, 128, "l0", 96 * h, 96 + HALF * h, so(58 + 8 * h, 66 + 8 * h))
     mm(5, "u16", 0, "rr", 0, 128, True, False)
     mm(5, "rr", 128, "u16", 0, 128, False, True)
     mm(4, "u16", 0, "ra", 0, 128)
     mm(7, "mq", 0, "ra", 0, 128, True, False)
     mm(7, "ra", 0, "mq", 128, 128, False, True)
     tt(v("cl"), pb(5, 0, 128), v("thra"), GE)
-    act(v("junk", 512, 528), v("cl"), off=oLA0, acc=dc(2), bias=D16)
+    act(v("junk", 16, 32), v("cl"), off=oLA0, acc=dc(2), bias=D16)
     ts(v("tx", 384, 448), LR, dc(2), EQ)
     one_hot(slots("tx"), LR, dc(2), NUM)
     quant("x0", 0, 128, "tx", 0)
     mm(5, "qk", WA, "x0", 0, 128, True, False)
     mm(5, "qk", WB, "x0", 0, 128, False, True)
-    ts(v("do0"), pb(5, 96, 112), 4.0, MUL, M4, ADD)
+    listed = [(ts(v("do0"), pb(5, 96, 112), 4.0, MUL, M4, ADD), 0.0)]
+    for k in range(2):
+        quant("qr", 128 * k, 128 * k + 128, "tr", 512 * k, listed)
+    quant("qw", 0, 128, "tw", 0, listed)
     mm(6, "qk", ONE, "x0", 0, 128)
-    o0, o1 = P * q, P * q + P
-    tt(v("dm"), pb(4, o0, o1), v("diag"), MUL)
+    o0 = P * q
+    tt(v("dm"), pb(4, o0, o0 + P), v("diag"), MUL)
     red(dc(0), v("dm"))
     cut = min(max(o0, 32), 80) if q in (0, NR - 1) else o0
     for a, b in ((0, cut), (cut, 112)):
         low = b <= o0
         ts(v("c0", a, b), pb(4, a if low else a + P, b if low else b + P), dc(0), GE if low else GT)
-    scan(v("run0"), v("c0"), v("c0"), dc(2), MAX)
-    ts(v("ty", 448, 480, 4), v("mx"), v("run0", 111, 112), GT)
+    running_sum(v("run0"), v("c0"), dc(2))
+    ts(v("ty", 449, 457, 4), v("mx"), v("run0", 111, 112), GT, 192.0, MUL)
+    quant("xk", 0, 128, "ty", 0)
+    mm(4, "qk", ONE, "xk", 0, 128)
 
-    for b in range(4):
-        act(v("dh", b, 32, 4), pb(b, P + 1, L0, W1), AF.Copy)
-    for x in range(NR):
+    for h in (1, 0):
         for b in range(4):
-            o, i = v("tch", 256 * x + b, 256 * x + 256, 4), v("s0", 64 * b, 64 * b + 64)
-            if 8 * b + (x + 3 * (x % 2)) % 8 < CFG["bv"]:
-                ts(o, i, pb(b, W1 * x + P + 1, W1 * x + P + 2) if 8 * b + 8 <= CFG["bv"] else shift(x, b), ADD)
-            else:
-                act(o, i, bias=shift(x, b))
-    nq = CFG["nq"]
-    for k in range(nq):
-        quant("al", 512 // nq * k, 512 // nq * (k + 1), "tch", 2048 // nq * k)
+            mm(b, "qk", E + 128 * b, "l0", LB + HALF * h, 128)
+            act(v("dh", 16 * h + b, 16 * h + 16, 4), pb(b, P + 1, HALF, W1), AF.Copy)
+        for x in range(4):
+            for b in range(4):
+                a = 1024 * h + 256 * x
+                o, i = v("tch", a + b, a + 256, 4), v("s0", 64 * b, 64 * b + 64)
+                if 4 * b + x < CFG["bv"][h]:
+                    ts(o, i, pb(b, W1 * x + P + 1, W1 * x + P + 2) if 4 * b + 4 <= CFG["bv"][h] else shift(4 * h + x, b), ADD)
+                else:
+                    act(o, i, bias=shift(4 * h + x, b))
+        quant("al", 256 * h, 256 * h + 256, "tch", 1024 * h)
     for b in range(3):
-        act(v("hx", 256 * b, 256 * b + 256), v("dh"), AF.Copy, off=v("so", 74 + 16 * b, 90 + 16 * b))
+        act(v("hx", 128 * b, 128 * b + 128), v("dh"), AF.Copy, off=so(76 + 8 * b, 84 + 8 * b))
 
     tt(v("ca"), pb(7, 0, 128), v("thra"), GE)
-    scan(v("runa"), v("ca"), v("ca"), 0.0, MAX)
+    running_sum(v("runa"), v("ca"), 0.0)
     ts(dc(12), v("runa", 127, 128), M - 0.5, LT, NUM, MUL)
     act(v("junk", 0, 16), v("ca"), off=oLA0, acc=dc(11), bias=D16)
     one_hot(slots("ty"), LR, dc(11), dc(12))
     quant("xa", 0, 128, "ty", 0)
     mm(7, "qk", ONE, "xa", 0, 128)
     act(v("m4"), pb(7, 0, 64), scale=0.25)
-    act(v("inv"), v("m4"), AF.Relu, scale=-HUGE, bias=HUGE)
+    act(v("inv"), pb(7, 0, 64), AF.Relu, scale=-HUGE, bias=HUGE)
     tt(v("pm", 64, 128), pb(7, 0, 64), v("mask"), MUL)
     tt(v("pf"), v("inv"), v("step"), ADD)
-    for k in range(8):
-        act(v("thr", 256 * (k // 4) + k % 4, 256 * (k // 4) + 256, 4), v("pf"), bias=v("ppb", k, k + 1))
+    for k in range(4):
+        act(v("thr", k, 256, 4), v("pf"), bias=v("ppb", k, k + 1))
+    act(v("thr", 256, 512), v("thr", 0, 256), bias=-128 * TINY)
     for b in range(2):
-        act(v("junk", 80 + 32 * b, 112 + 32 * b), v("pm", 64 + 32 * b, 96 + 32 * b), acc=dc(14 + b))
+        act(junk(1 + b), v("pm", 64 + 32 * b, 96 + 32 * b), acc=dc(14 + b))
     act(dc(16, 2), dc(14, 2), AF.Sign)
+    act(dc(18, 2), dc(16, 2), scale=M4x4)
     act(v("val", 0, 256), v("thr", 0, 256), AF.Relu, scale=-1.0, bias=1.0)
     for k in range(4):
-        act(v("n1", 256 + k, 512, 4, rows=(0, 1)), v("m4", rows=(0, 1)), AF.Relu, bias=float(k - 3))
-    act(v("n1", 0, 256, rows=(0, 1)), v("n1", 256, 512, rows=(0, 1)), bias=-1.0)
-    dma("Y", v("nm", 0, 256, rows=(0, 1)), v("n1", 0, 256, rows=(0, 1)))
+        act(row("n1", 256 + k, 512, 4), row("m4"), AF.Relu, bias=float(k - 3))
+    act(row("n1", 0, 256), row("n1", 256, 512), bias=-1.0)
+    dma("Y", row("nm", 0, 256), row("n1", 0, 256))
 
-    act(v("k8"), pb(7, 112, 120), AF.Copy)
-    act(v("kb"), v("k8"), AF.Copy, off=oKB)
-    tt(v("keep"), v("kb"), v("iref"), GT)
-    ts(dc(6, 2), v("kb", 0, 64, 32), I8, GT)
+    for c in range(2):
+        ts(v("ov", c, 4, 2), pb(4, 112, 114), cf(34 + c), SUB, cf(36 + c), MIN)
+    ts(dc(6, 2), pb(4, 112, 114), I8x, GT)
     tt(v("pm", 0, 64), pb(6, 0, 64), v("mask"), MUL)
     for b in range(2):
-        act(v("junk", 16 + 32 * b, 48 + 32 * b), v("pm", 32 * b, 32 * b + 32), acc=dc(4 + b), scale=dc(6 + b))
+        act(junk(3 + b), v("pm", 32 * b, 32 * b + 32), acc=dc(4 + b), scale=dc(6 + b))
     for h in range(2):
-        pick_c("ch", 128 * h, 128, "al", 0, 256 * h + 256, v("do0", 8 * h, 8 * h + 8))
-        pick_s("ch", 128 * h, 128, "al", 0, 256 * h + 256, v("do0", 8 * h, 8 * h + 8), on=CFG["cs"][h])
-        mm(2 * h, "u32", 128 * h, "ch", 128 * h, 128)
-        mm(2 * h + 1, "ch", 128 * h, "l0", 0, L0)
+        pick("ch", 128 * h, 128, "al", 0, 256 * h + 256, v("do0", 8 * h, 8 * h + 8))
+        mm(h, "u32", 128 * h, "ch", 128 * h, 128, True, False)
+        mm(h, "ch", 128 * h, "ln", 128 * h, 128, False, True)
         scatter_half("ch", h, "l1", 0, 1)
 
     for b in range(2):
-        lo, hi = 32 * b, 32 * b + 32
-        for x in range(4):
-            rows, c = (32 * x, 32 * x + 32), W1 * (4 * b + x) + P
-            ts(v("d1", lo, hi, rows=rows), pb(2 * b, 32 * x, 32 * x + 32, rows=rows), pb(2 * b + 1, c, c + 1, rows=rows), SUB)
-        tt(v("c1", lo, hi), v("d1", lo, hi), v("base1", lo, hi), GE)
-        scan(v("run1", lo, hi), back("c1", lo, hi), back("keep", lo, hi), 0.0, MUL)
-        one_hot(flags("tx", b), lr1, v("run1", hi - 1, hi), dc(6 + b))
-        one_hot(nums("tx", b), lr1, v("run1", hi - 1, hi), dc(4 + b))
+        tt(v("c1", 144 * b + 16, 144 * b + 144), pb(b, 0, 128), v("thra"), GE)
+        act(junk(5 + b), v("c1", 144 * b, 144 * b + 144), off=v("ov", 2 * b, 2 * b + 2), acc=dc(8 + b))
+        one_hot(flags("tx", b), lr1, dc(8 + b), dc(6 + b))
+        one_hot(flags("tx", 2 + b), lr1, dc(8 + b), dc(4 + b))
     quant("x1", 0, 144, "tx", 0)
     mm(4, "qk", WA, "x1", 0, 128, True, False)
     mm(4, "qk", WB, "x1", 0, 128, False, True)
-    spread_numbers("x1", 5)
+    mm(5, "qk", SEL, "x1", 16, 128, True, False)
+    mm(5, "qk", WD, "x1", 0, 128, False, True)
+    first = len(plan)
     ts(v("do1", 0, 16), pb(4, 64, 80), 0.0, ADD)
     ts(v("do1", 16, 32), pb(5, 64, 80), C14, ADD, 0.0, MAX)
     for h in range(2):
         pick("pv", 128 * h, 128, "ch", 128 * h, 128 * h + 128, v("do1", 8 * h, 8 * h + 8))
         pick("pe", 128 * h, 128, "qr", 0, 256, v("do1", 16 + 8 * h, 24 + 8 * h))
-        for b in range(4):
-            mm(4 * h + b, "qk", E + 128 * b, "pv", 128 * h, 128, True, False)
-        for b in range(4):
-            mm(4 * h + b, "qk", E + 128 * b, "pe", 128 * h, 128, False, True)
+    turns = (((0, 3), (0, 0), (0, 1), (1, 3), (1, 0), (0, 2), (1, 1), (1, 2)), [(x, b) for b in (3, 0, 1, 2) for x in (0, 1)])
+    for h in range(2):
+        made = [(mm(4 * h + b, "qk", E + 128 * b, ("pv", "pe")[x], 128 * h, 128, x == 0, x == 1), 0.0) for x, b in turns[h]]
 
     for h in range(2):
         for b in range(3):
-            tt(v("tgr", 512 * h + b, 512 * h + 512, 4), pb(4 * h + b, 0, 128), v("hx", 256 * b + 128 * h, 256 * b + 128 * h + 128), ADD)
+            for r in range(2):
+                a = 64 * (2 * b + h)
+                tt(v("tgr", 512 * h + 4 * r + b, 512 * h + 512, 8), pb(4 * h + b, r, 128, 2), v("hx", a, a + 64), ADD)
         for x in range(4):
             a = 512 * h + 128 * x
             act(v("tgr", a + 3, a + 128, 4), pb(4 * h + 3, 32 * x, 32 * x + 32), bias=shift(4 * h + x, 3))
         quant("gr", 128 * h, 128 * h + 128, "tgr", 512 * h)
         scatter_half("gr", h, "l2", Z, 2)
+    in_turn(first, ("S", "PE"))
 
     for b in range(2):
         for h in range(2):
-            mm(2 * b + h, "mq", 0, "l1", 128 * h, 128, True, False)
+            mm(2 * b + h, "mq", 0, "l1", 128 * h, 128, True, False, made)
             mm(2 * b + h, "l1", 128 * b, "mq", 128, 128, False, True)
     mm(4, "qw", 0, "l1", 0, 256)
     for b in range(2):
         for h in range(2):
             a = 256 * b + 128 * h
             tt(v("cb", a, a + 128), pb(2 * b + h, 0, 128), v("thr", a, a + 128), GE)
-        act(v("junk", 144 + 32 * b, 176 + 32 * b), v("cb", 384 * b, 384 * b + 128), off=oLA1, acc=dc(20 + b), bias=4.0 * (M - 1))
-        if b == 0:
-            act(v("junk", 256, 512), v("cb", 0, 256), acc=dc(22))
-    scan(v("runb"), v("cb", 256, 512), v("cb", 256, 512), 0.0, MAX)
-    ts(dc(24), dc(22), 128.0, MUL, dc(20), MAX)
-    ts(dc(25), v("runb", 255, 256), 128.0, MUL, dc(21), MAX)
+        act(junk(7 + b), v("cb", 384 * b, 384 * b + 128), off=oLA1, acc=dc(20 + b), bias=4.0 * (M - 1))
+        running_sum(v("runb", 256 * b, 256 * b + 256), v("cb", 256 * b, 256 * b + 256), 0.0)
+        ts(dc(24 + b), v("runb", 256 * b + 255, 256 * b + 256), 128.0, MUL, dc(20 + b), MAX)
     for b in range(2):
         one_hot(flags("ty", b), lr2, dc(24 + b), dc(16 + b))
-        one_hot(v("ty", 128 * b, 128 * b + 128, 4), lr2, dc(24 + b), dc(16 + b))
-        one_hot(nums("ty", b), lr2, dc(24 + b), dc(14 + b))
-    quant("x2", 0, 144, "ty", 0)
+        one_hot(v("ty", 128 * b, 128 * b + 128, 4), lr2, dc(24 + b), dc(14 + b))
+        one_hot(v("ty", 128 * b + 2, 128 * b + 128, 4), lr2, dc(24 + b), dc(18 + b))
+    quant("x2", 0, 128, "ty", 0)
     mm(5, "qk", ONE, "xa", 0, 128, True, False)
     mm(5, "qk", SEL, "x2", 0, 128, False, True)
     mm(7, "qk", ONE, "x2", 0, 128)
-    spread_numbers("x2", 6)
+    mm(6, "qk", ONE, "x2", 0, 128)
     ts(v("do2"), pb(5, 64, 80), 512.0, MUL, M16, ADD)
     for k in range(4):
-        act(v("val", 256 + k, 512, 4), pb(7, 0, 64), AF.Copy)
+        act(v("val", 256 + k, 512, 4), pb(7, 0, 64), AF.Sign)
+    for k in range(4):
+        ts(row("n2", k, 256, 4), row("p6", 0, 64), float(k - 16), ADD, -1.0, MAX)
+    dma("Y", row("nm", 256, 512), row("n2"))
     for h in range(2):
         tt(v("yy", 128 * h, 128 * h + 128), pb(4, 128 * h, 128 * h + 128), v("val", 128 * h, 128 * h + 128), MUL)
     dma("Y", v("y", 0, 256), v("yy", 0, 256))
-    ts(v("n2", 0, 16), pb(6, 64, 80), C14, ADD, -1.0, MAX)
 
-    a, b = v("n2t", rows=(0, 32)), v("n2", rows=(0, 32))
-    op("V", [b], [a], lambda: g.vector.transpose(ap(a), ap(b)), 32)
-    dma("Y", v("nm", 256, 512, rows=(0, 1)), v("n2t", 0, 16, rows=(0, 16)))
     for h in range(2):
         pick_c("fin", 128 * h, 128, "l2", 0, Z + 256, v("do2", 8 * h, 8 * h + 8))
-    dma("Y", v("oc"), v("finc"), codes=True)
+        dma("Y", v("oc", 512 * h, 512 * h + 512), v("finc", 128 * h, 128 * h + 128), codes=True)
+    first = len(plan)
+    for h in range(2):
+        pick_s("fin", 128 * h, 128, "l2", 0, Z + 256, v("do2", 8 * h, 8 * h + 8))
     for h in range(2):
         lo, hi = 256 + 128 * h, 384 + 128 * h
         mm(h, "qw", 0, "l2", Z + 128 * h, 128)
         tt(v("yy", lo, hi), pb(h, 0, 128), v("val", lo, hi), MUL)
         dma("YS"[h], v("y", lo, hi), v("yy", lo, hi))
-        pick_s("fin", 128 * h, 128, "l2", 0, Z + 256, v("do2", 8 * h, 8 * h + 8), on=CFG["fs"][h])
+    in_turn(first, ("S", "V"))
     for k in range(4):
         dma("YSYS"[k], v("osc", rows=(4 * k, 4 * k + 4)), v("fins", rows=(32 * k, 32 * k + 4)))
 

from concourse.bass import DstId, RemoteDMATransfer
from concourse.mybir import dt, AluOpType, AxisListType, ActivationFunctionType

CFG = {"bv": (8, 8), "fw": 0, "moves": 2500, "tries": 30, "seed": 1}
COST = {"cycle": 0.00083, "V": 64, "S": 80, "PE": 0, "G": 0, "pick0": 60, "pick": 1.5, "mm": 0.75, "issue": 0.05, "dma": 1.1,
        "wide": 0.001, "send": 0.15, "first": 1.3, "a0c": 1.5, "a0s": 1.75, "b0c": 1.3, "b0s": 1.1, "anc": 4.3, "ans": 4.6,
        "d0c": 2.3, "d0s": 2.7, "straightc": 2.0, "straights": 2.4, "helpedc": 2.9, "helpeds": 3.1}
CASES = ((1.0, 1.0, 0.21, 1.0), (1.0, 0.75, 0.22, 0.9), (1.45, 1.3, 0.21, 1.0), (1.4, 1.3, 0.25, 1.5), (1.1, 1.0, 0.21, 1.3),
         (1.0, 0.7, 0.17, 1.1))
NR, P, CAP, M, S = 8, 16, 8, 40, 32
W1 = P + 2
HALF = NR // 2 * W1
LB = 96 - HALF
R1 = 4 * P
Z = 16
TINY, HUGE = 2.0 ** -110, 2.0 ** 90
Q4, U8, BF, F32, I32, U16 = "float8_e4m3fn_x4", "uint8", "bfloat16", "float32", "int32", "uint16"

SCRATCH = {}
for _n, _w in (("q1", 128), ("qa", 128), ("qr", 256), ("qw", 128), ("qk", 1152), ("l0", 224), ("u16", 128), ("u32", 256), ("ra", 128),
               ("r4", 128), ("mq", 256), ("rr", 256), ("al", 512), ("x0", 128), ("xa", 128), ("xk", 128), ("x1", 144), ("x2", 128),
               ("ch", 256), ("l1", 256), ("h0", S), ("ln", S * NR), ("h1", 2 * S), ("h2", 2 * S), ("pv", 256), ("pe", 256),
               ("gr", 256), ("l2", Z + 256), ("fin", 256)):
    SCRATCH[_n + "c"] = ("sbuf", [128, _w], Q4)
    SCRATCH[_n + "s"] = ("sbuf", [128, _w], U8)
for _n, _w, _d in (("t1", 512, BF), ("ta", 512, BF), ("tr", 1024, BF), ("tw", 512, BF), ("tz", 516, BF), ("tk", 2560, BF), ("tx", 576, BF),
                   ("ty", 512, BF), ("tch", 2048, BF), ("tgr", 1024, BF), ("ci", 16, I32), ("cf", 40, F32), ("ib", 384, BF),
                   ("idx", 168, F32), ("of", 100, F32), ("so", 100, U16), ("do0", 16, U16), ("do1", 32, U16), ("do2", 16, U16),
                   ("mx", 2, F32), ("thra", 128, BF), ("diag", 16, F32), ("mask", 64, F32), ("lr", 64, F32), ("ppb", 4, F32),
                   ("step", 64, F32), ("s0", 256, F32), ("dh", 32, F32), ("hx", 384, F32), ("dc", 32, F32), ("dm", 16, F32),
                   ("cl", 128, BF), ("c0", 112, BF), ("run0", 112, BF), ("c1", 288, BF), ("ov", 4, U16),
                   ("pm", 128, F32), ("ca", 128, BF), ("runa", 128, BF), ("junk", 288, F32), ("m4", 64, F32), ("inv", 64, F32),
                   ("pf", 64, F32), ("thr", 512, F32), ("val", 512, F32), ("cb", 512, BF), ("runb", 512, BF), ("n1", 512, F32),
                   ("n2", 256, F32), ("yy", 512, F32)):
    SCRATCH[_n] = ("sbuf", [128, _w], _d)
for _k in range(8):
    SCRATCH["p%d" % _k] = ("psum", [128, 512], F32)

DMAS = ["ld%d" % _k for _k in range(32)]
SEMAPHORES = ["V", "S", "PE", "G", "sent"] + [_a + _k for _a in ("a0", "b0", "an", "a1", "a2", "ah0", "ah1", "ah2") for _k in "cs"] + DMAS

ADD, SUB, MUL, MAX, MIN = AluOpType.add, AluOpType.subtract, AluOpType.mult, AluOpType.max, AluOpType.min
GE, GT, LT, EQ = AluOpType.is_ge, AluOpType.is_gt, AluOpType.is_lt, AluOpType.is_equal
AND = AluOpType.bitwise_and
AF = ActivationFunctionType
ORDERS = {}


def bits(engines):
    m = 0
    for e in engines:
        m |= 1 << e
    return m


def deal(engines, n, flip=False):
    k = 1
    while 2 * k * n <= len(engines):
        k *= 2
    sizes = [k] * n
    if k * (n + 1) <= len(engines):
        sizes[0] *= 2
    eng = engines[::-1] if flip else engines
    return [bits(eng[sum(sizes[:i]):sum(sizes[:i + 1])]) for i in range(n)], sizes


def helpers_of(c, T, topo):
    ok = [h for h in topo.cores_of(c) if T.rank_of(h) is None and topo.die(h) != topo.die(c)
          and all(topo.may_write(h, d) for d in T.cores if d != c)]
    return ok[:2]


def engine_sets(src, c, T, topo):
    far = topo.engines(src, [d for d in T.cores if d != c][0])
    near = topo.engines(c, helpers_of(c, T, topo)[0])
    return far, [e for e in near if e not in far]


def transfer(topo, src, dsts, mask, sem, a, b, kind):
    b = b if isinstance(b, list) else [b] * len(dsts)
    if kind == "c":
        a, b = a.bitcast(dt.uint8), [x.bitcast(dt.uint8) for x in b]
    ids = []
    for d in dsts:
        rid, pid = topo.addr(d, src)
        ids.append(DstId(rid=rid, pnc=pid))
    return RemoteDMATransfer(dst_ids=ids, dma_engine_mask=mask, remote_sem=sem, src=a, dsts=b)


def helper_program(g, core, T, topo):
    own = [c for c in T.cores if core in helpers_of(c, T, topo)]
    if not own:
        return
    q = T.rank_of(own[0])
    k = helpers_of(own[0], T, topo).index(core)
    far, near = engine_sets(core, own[0], T, topo)
    to = [(q + i) % NR for i in range(1, NR)][4 * k:4 * k + 4]
    for kind in "cs":
        g.wait_ge(T.sem["ah0" + kind], len(near))
        g.remote_dma_fused([transfer(topo, core, [T.cores[r] for r in to], bits(far), T.sem["an" + kind], T["h0" + kind][:, 0:S],
                                     [T["ln" + kind][:, S * ((q - r - 1) % NR):S * ((q - r - 1) % NR) + S] for r in to], kind)],
                           local_sem=T.sem.sent)
    masks = deal(far, 2)[0]
    for stage, at in ((1, 0), (2, Z)):
        for kind in "cs":
            g.wait_ge(T.sem["ah%d%s" % (stage, kind)], len((far, near)[k]))
            g.remote_dma_fused([transfer(topo, core, [T.cores[(q + 1 + 2 * k + i) % NR]], masks[i], T.sem["a%d%s" % (stage, kind)],
                                         T["h%d%s" % (stage, kind)][:, S * i:S * i + S],
                                         T["l%d%s" % (stage, kind)][:, at + S * q:at + S * q + S], kind) for i in range(2)],
                               local_sem=T.sem.sent)
    g.wait_ge(T.sem.sent, 6 * len(far))


def best_order(queue, busy, lag, pred, banks):
    n = len(queue)
    succ = [[] for _ in range(n)]
    for j in range(n):
        for i in pred[j]:
            succ[i].append(j)

    def edges(case):
        kb, pe, wait, fly = case
        b = [busy[i] * (kb if queue[i] in "VS" else pe if queue[i] == "PE" else fly) for i in range(n)]
        return (b, [[(i, b[i] + wait * w + fly * f) for i, (w, f) in pred[j].items()] for j in range(n)], [fly * x for x in lag], wait,
                20.0 / (8 + 6 * kb + 6 * fly))

    cases = [edges(c) for c in CASES]

    def place(way, back=False):
        b, pre, tail, wait = cases[0][:4]
        nxt, first = succ, [0.0] * n
        if back:
            nxt, first, fore, pre = pred, tail, pre, [[] for _ in range(n)]
            for j in range(n):
                for i, d in fore[j]:
                    pre[i].append((j, d - b[i] + b[j]))
        start, taken, miss = [0.0] * n, {}, [len(p) for p in pre]
        ready = [j for j in range(n) if not miss[j]]
        while ready:
            j = max(ready, key=lambda j: (way[j], -j))
            ready.remove(j)
            t = max([start[i] + d for i, d in pre[j]] + [first[j]])
            spans = taken.get(queue[j], [])
            if banks[j]:
                spans = sorted(spans + [(s[0] - wait, s[1] + wait) for k in banks[j] for s in taken.get(k, []) if s[2] != queue[j]])
            for s in spans:
                if t + b[j] <= s[0] + 1e-9:
                    break
                if s[1] > t:
                    t = s[1]
            start[j] = t
            taken.setdefault(queue[j], []).append((t, t + b[j]))
            taken[queue[j]].sort()
            for k in banks[j]:
                taken.setdefault(k, []).append((t, t + b[j], queue[j]))
            for k in nxt[j]:
                miss[k] -= 1
                if not miss[k]:
                    ready.append(k)
        return start

    def sort(start):
        return sorted(range(n), key=lambda j: (start[j], j))

    def length(order):
        total, chains = 0.0, []
        for b, pre, tail, wait, weight in cases:
            start, why, free, last, end, j1 = [0.0] * n, [-1] * n, {}, {}, 0.0, 0
            for j in order:
                t, w = free.get(queue[j], (0.0, -1))
                for i, d in pre[j]:
                    if start[i] + d > t:
                        t, w = start[i] + d, i
                for k in banks[j]:
                    for e, (x, i) in last.get(k, {}).items():
                        if e != queue[j] and x + wait > t:
                            t, w = x + wait, i
                start[j], why[j] = t, w
                free[queue[j]] = (t + b[j], j)
                for k in banks[j]:
                    last.setdefault(k, {})[queue[j]] = (t + b[j], j)
                if t + b[j] + tail[j] > end:
                    end, j1 = t + b[j] + tail[j], j
            total += end * weight
            chain = []
            while why[j1] >= 0:
                if why[j1] not in pred[j1]:
                    chain.append((why[j1], j1))
                j1 = why[j1]
            chains.append(chain)
        return total, chains

    b, pre, tail, wait = cases[0][:4]
    way = [b[i] + tail[i] for i in range(n)]
    for j in range(n - 1, -1, -1):
        for i, d in pre[j]:
            way[i] = max(way[i], d + way[j])
    best = sort(place(way))
    state = [CFG["seed"]]

    def draw(m):
        state[0] = (state[0] * 1103515245 + 12345) % 2147483648
        return (state[0] >> 8) % m

    least = length(best)[0]
    for k in range(CFG["tries"]):
        trial = list(way)
        for _ in range(1 + k % 24):
            trial[draw(n)] += (draw(2001) - 1000) / 1000.0
        start = place(trial)
        for _ in range(2):
            late = place([start[j] + b[j] for j in range(n)], True)
            trial = [late[j] + b[j] for j in range(n)]
            start = place(trial)
            order = sort(start)
            t = length(order)[0]
            if t <= least:
                best, least, way = order, t, trial
    now, (t0, chains) = best, length(best)
    for k in range(CFG["moves"]):
        chain = chains[draw(len(chains))]
        if not chain:
            continue
        i, j = chain[draw(len(chain))]
        order = list(now)
        a, z = order.index(i), order.index(j)
        if draw(2):
            more = draw(3)
            while more and a > 0:
                a -= 1
                more -= queue[order[a]] == queue[j]
            lift = {j}
            for x in reversed(order[a:z]):
                if any(x in pred[y] for y in lift):
                    lift.add(x)
            order[a:z + 1] = [x for x in order[a:z + 1] if x in lift] + [x for x in order[a:z + 1] if x not in lift]
        else:
            more = draw(4)
            while more and z < n - 1:
                z += 1
                more -= queue[order[z]] == queue[i]
            sink = {i}
            for x in order[a + 1:z + 1]:
                if not sink.isdisjoint(pred[x]):
                    sink.add(x)
            order[a:z + 1] = [x for x in order[a:z + 1] if x not in sink] + [x for x in order[a:z + 1] if x in sink]
        t, c = length(order)
        if t <= t0 + 0.25 * (1 - k / CFG["moves"]) * draw(1000) / 1000.0:
            now, t0, chains = order, t, c
            if t < least:
                best, least = order, t
    ORDERS["least"] = least / len(cases)
    return best


def rank_program(g, core, T, topo):
    q = T.rank_of(core)
    if q is None:
        helper_program(g, core, T, topo)
        return
    peers = [(q + i) % NR for i in range(1, NR)]
    helpers = helpers_of(core, T, topo)
    far, near = engine_sets(core, core, T, topo)
    queue = {"V": g.vector, "S": g.scalar, "PE": g.tensor, "G": g, "Y": g.sync}
    count = {"V": 0, "S": 0, "PE": 0, "G": 0}
    clock = {e: {} for e in queue}
    known = {}
    hist = {}
    final = {}
    free_sems = list(DMAS)

    def v(name, a=None, b=None, step=None, rows=(0, 128)):
        return (name, rows, slice(a, b, step))

    def ap(x):
        return T[x[0]][x[1][0]:x[1][1], x[2]]

    def cols(x):
        return set(range(SCRATCH[x[0]][1][1])[x[2]])

    def wait(e, tok):
        sem, n = tok
        if clock[e].get(sem, 0) >= n:
            return
        queue[e].wait_ge(T.sem[sem], n)
        clock[e][sem] = n
        for s2, n2 in known.get(tok, {}).items():
            if clock[e].get(s2, 0) < n2:
                clock[e][s2] = n2

    def order(e, reads, writes):
        toks = {}
        for x, wr in [(x, False) for x in reads] + [(x, True) for x in writes]:
            if x[0] not in SCRATCH:
                continue
            psum = SCRATCH[x[0]][0] == "psum"
            cx = cols(x)
            for e2, tok, wr2, rows, c2 in hist.get(x[0], []):
                if psum and e2 != e:
                    hit = True
                elif psum and e == "PE":
                    hit = False
                else:
                    hit = (wr or wr2) and rows[0] < x[1][1] and x[1][0] < rows[1] and not cx.isdisjoint(c2)
                if hit and toks.get(tok[0], 0) < tok[1]:
                    toks[tok[0]] = tok[1]
        for sem in sorted(toks, key=lambda s: s == e):
            wait(e, (sem, toks[sem]))

    def note(e, tok, reads, writes):
        known[tok] = dict(clock.get(e, {}))
        final[tok[0]] = max(final.get(tok[0], 0), tok[1])
        for x, wr in [(x, False) for x in reads] + [(x, True) for x in writes]:
            if x[0] in SCRATCH:
                hist.setdefault(x[0], []).append((e, tok, wr, x[1], cols(x)))

    plan = []

    def later(e, reads, writes, busy, edge, emit, after=()):
        plan.append((e, [x for x in reads if isinstance(x, tuple) and x[0] in SCRATCH], [x for x in writes if x[0] in SCRATCH],
                     busy, edge, emit, list(after)))
        return len(plan) - 1

    def op(e, reads, writes, call, cycles, after=()):
        reads = [x for x in reads if isinstance(x, tuple)]

        def emit():
            order(e, reads, writes)
            count[e] += 1
            call().then_inc(T.sem[e], 1)
            note(e, (e, count[e]), reads, writes)
        return later(e, reads, writes, max(cycles, COST[e]) * COST["cycle"], (1, 0.05 if e == "PE" else 0.0), emit, after)

    def sc(x):
        return ap(x) if isinstance(x, tuple) else x

    def dma(e, out, in_, codes=False, behind=0.0, landed=()):
        def emit():
            order(e, [in_] + list(landed), [out])
            sem = free_sems.pop(0)
            a, b = ap(out), ap(in_)
            if codes:
                b = b.bitcast(dt.uint8)
                if out[0] in SCRATCH:
                    a = a.bitcast(dt.uint8)
            queue[e].dma_start(a, b).then_inc(T.sem[sem], 16)
            known[(sem, 16)] = dict(clock[e])
            final[sem] = 16
            for x, wr in ((in_, False), (out, True)):
                if x[0] in SCRATCH:
                    hist.setdefault(x[0], []).append(("dma", (sem, 16), wr, x[1], cols(x)))
        wide = len(cols(out if out[0] in SCRATCH else in_))
        if out[0] not in SCRATCH:
            j = later(e, [in_], [], COST["issue"], (0, 0.9), emit)
            return later("D", [], [], 0.03 + (in_[1][1] - in_[1][0] == 128) * (0.04 + 0.002 * wide), (0, 0.15), lambda: None, [(j, 0.9)])
        return later(e, [in_] + list(landed), [out], COST["issue"], (0, COST["dma"] + COST["wide"] * wide + behind), emit)

    def arrives(sem, n, views, after):
        later(sem, [], views, 0.0, (0, 0.0), lambda: note("far", (sem, n), [], views), after)

    sends = []

    def send(transfers, reads, n):
        def emit():
            order("G", reads, [])
            g.remote_dma_fused(transfers, local_sem=T.sem.sent)
            final["sent"] = final.get("sent", 0) + n
        sends.append(later("G", reads, [], COST["send"] if sends else COST["first"], (0, 0.0), emit, [(i, 0.0) for i in sends[-1:]]))
        return sends[-1]

    def in_turn(first, queues):
        last = {}
        for j in range(first, len(plan)):
            e = plan[j][0]
            if e in queues:
                if e in last:
                    plan[j][6].append((last[e], 0.0))
                last[e] = j

    def schedule():
        key = tuple(x[0] for x in plan)
        if key not in ORDERS:
            pred, seen = [], {}
            for j, (e, reads, writes, busy, edge, emit, after) in enumerate(plan):
                d = {i: (0, f) for i, f in after}
                mine = [(x, False, cols(x)) for x in reads] + [(x, True, cols(x)) for x in writes]
                for x, wr, cx in mine:
                    psum = SCRATCH[x[0]][0] == "psum"
                    for i, wr2, rows, c2 in seen.get(x[0], []):
                        if (wr or wr2) and (psum or rows[0] < x[1][1] and x[1][0] < rows[1] and not cx.isdisjoint(c2)):
                            d[i] = (0, 0.0) if psum and e == plan[i][0] == "PE" else plan[i][4]
                for x, wr, cx in mine:
                    seen.setdefault(x[0], []).append((j, wr, x[1], cx))
                pred.append(d)
            banks = [sorted({x[0] for x in p[1] + p[2] if SCRATCH[x[0]][0] == "psum"}) for p in plan]
            ORDERS[key] = best_order([p[0] for p in plan], [p[3] for p in plan], [p[4][1] for p in plan], pred, banks)
        for j in ORDERS[key]:
            plan[j][5]()

    def size(*views):
        return len(cols(views[0])) * (0.5 if all(SCRATCH[x[0]][2] in (BF, U16) for x in views) else 1.0)

    def picked(out):
        return COST["pick0"] + COST["pick"] * len(cols(out))

    def ts(out, in0, s1, op0, s2=None, op1=None):
        if op1 is None:
            return op("V", [in0, s1], [out], lambda: g.vector.tensor_scalar(ap(out), ap(in0), sc(s1), None, op0), size(out, in0))
        return op("V", [in0, s1, s2], [out], lambda: g.vector.tensor_scalar(ap(out), ap(in0), sc(s1), sc(s2), op0, op1), size(out, in0))

    def tt(out, in0, in1, alu):
        n = len(cols(out)) * (1 if SCRATCH[in0[0]][0] == "psum" else 2)
        op("V", [in0, in1], [out], lambda: g.vector.tensor_tensor(ap(out), ap(in0), ap(in1), alu), n)

    def cp(out, in_, off=None):
        a = ap(in_) if off is None else ap(in_).indirect(ap(off))
        op("V", [in_, off], [out], lambda: g.vector.tensor_copy(ap(out), a), picked(out) if off else size(out, in_))

    def fill(out, c):
        op("V", [], [out], lambda: g.vector.memset(ap(out), c), size(out))

    def red(out, in_):
        op("V", [in_], [out], lambda: g.vector.tensor_reduce(ap(out), ap(in_), AxisListType.X, ADD), len(cols(in_)))

    def running_sum(out, x, first):
        op("V", [x, first], [out], lambda: g.vector.tensor_tensor_scan(ap(out), ap(x), ap(x), sc(first), ADD, MAX), size(out, x))

    def act(out, in_, func=AF.Identity, off=None, acc=None, **kw):
        a = ap(in_) if off is None else ap(in_).indirect(ap(off))
        k2 = {k: sc(x) for k, x in kw.items()}
        if acc is not None:
            k2["accum_out"] = ap(acc)
        op("S", [in_, off] + list(kw.values()), [out] + ([acc] if acc else []), lambda: g.scalar.activation(ap(out), a, func, **k2),
           (picked(out) + 20 if off else max(COST["S"], len(cols(out)))) + (25 if acc else 0))

    def quant(name, a, b, tile, ta, after=()):
        c, s, t = v(name + "c", a, b), v(name + "s", a, b), v(tile, ta, ta + 4 * (b - a))
        return op("V", [t], [c, s], lambda: g.vector.quantize_mx(ap(c), ap(s), ap(t)), 15 + 1.06 * (b - a), after)

    def mm(bank, w, wa, x, xa, n, start=True, stop=True, after=()):
        wc, ws, xc, xs = v(w + "c", wa, wa + 128), v(w + "s", wa, wa + 128), v(x + "c", xa, xa + n), v(x + "s", xa, xa + n)
        o = v("p%d" % bank, 0, n)
        return op("PE", [wc, ws, xc, xs], [o], lambda: g.tensor.matmul_mx(ap(o), ap(wc), ap(ws), ap(xc), ap(xs), start, stop),
                  COST["mm"] * (n + 16), after)

    def pick_c(out, at, n, win, a, b, off):
        o, w = v(out + "c", at, at + n), v(win + "c", a, b)
        op("V", [w, off], [o], lambda: g.vector.tensor_copy(ap(o).bitcast(dt.uint32), ap(w).bitcast(dt.uint32).indirect(ap(off))), picked(o))

    def pick_s(out, at, n, win, a, b, off, on="S"):
        if on == "S":
            act(v(out + "s", at, at + n), v(win + "s", a, b), AF.Copy, off=off)
        else:
            cp(v(out + "s", at, at + n), v(win + "s", a, b), off=off)

    def pick(out, at, n, win, a, b, off, on="S"):
        pick_c(out, at, n, win, a, b, off)
        pick_s(out, at, n, win, a, b, off, on)

    def iota(out, pattern, base=0, cm=0, behind=None):
        n, after = 160 + 2 * len(cols(out)), [] if behind is None else [(sends[behind], 0.0)]
        if SCRATCH[out[0]][2] == I32:
            op("G", [], [out], lambda: g.iota(ap(out), pattern, base, cm), n, after)
        else:
            op("G", [], [out], lambda: g.iota(ap(out), pattern, base, cm, allow_small_or_imprecise_dtypes=True), n, after)

    j0 = {}

    def scatter_half(src, h, land, at, stage):
        for kind in "cs":
            dst = v(land + kind, at + S * q, at + S * q + S)
            block = lambda x, n=1: v(src + kind, S * x, S * (x + n))
            name = "%d%s" % (stage, kind)
            if h == 0:
                j0[kind] = send([transfer(topo, core, [c], bits(e), T.sem["ah" + name], ap(block(2 * k, 2)), ap(v("h" + name)), kind)
                                 for k, (c, e) in enumerate(zip(helpers, (far, near)))], [block(0, 4)], len(far) + len(near))
            else:
                masks = deal(far, 3, kind == "s")[0]
                j = send([transfer(topo, core, [T.cores[peers[4 + k]]], m, T.sem["a" + name], ap(block(4 + k)), ap(dst), kind)
                          for k, m in enumerate(masks)], [block(4, 3)], len(far))
                dma("Y", dst, block(NR - 1), codes=kind == "c")
                arrives("a" + name, 3 * len(far), [v(land + kind, at + S * r, at + S * r + S) for r in peers],
                        [(j, COST["straight" + kind]), (j0[kind], COST["helped" + kind])])

    cf = lambda k, n=1: v("cf", k, k + n)
    ci = lambda k, n=1: v("ci", k, k + n)
    dc = lambda k, n=1: v("dc", k, k + n)
    pb = lambda k, a, b, step=None: v("p%d" % k, a, b, step)
    shift = lambda x, b: v("dh", 4 * x + b, 4 * x + b + 1)
    io = lambda a, b, step=None: v("ib", a, b, step)
    of = lambda a, b: v("of", a, b)
    so = lambda a, b: v("so", a, b)
    junk = lambda k: v("junk", 32 * k, 32 * k + 32)
    row = lambda name, a=None, b=None, step=None: v(name, a, b, step, (0, 1))
    E, ONE, SEL, WA, WB, WD = 0, 512, 640, 768, 896, 1024
    tk = lambda at, t=None: v("tk", 4 * (at - ONE), 4 * (at - ONE) + 512) if t is None else v("tk", 4 * (at - ONE) + t, 4 * (at - ONE) + 512, 4)
    LR, MREF, LR1, PPL = v("idx", 0, 64), v("idx", 64, 128), v("idx", 128, 160), v("idx", 160, 164)
    lr1, lr2 = v("lr", 0, 32), v("lr", 32, 64)
    oR4, oRA, oRR, oLA0, oLA1 = so(0, 8), so(16, 24), so(24, 40), so(40, 41), so(74, 76)
    PP, D16x16, M16x16, Q16x16, D16, M16, D4, M32, G4, M4 = (cf(k) for k in (0, 3, 5, 8, 14, 16, 17, 18, 20, 21))
    NUM, CRA, C14, M4x4, NB32, CUT, CLA, I8, G4x, I8x = (cf(22 + k) for k in range(10))

    dma("Y", v("t1", 0, 64), v("r0"))
    dma("S", v("t1", 64, 72), v("u", 0, 8))
    fill(v("t1", 72, 512), 0.0)
    dma("Y", v("ta", 0, 256), v("r1"), behind=0.2)
    dma("Y", v("tr"), v("r2"), behind=0.6)
    dma("Y", v("tw"), v("w"), behind=1.6)
    for k, m in enumerate((1, 4, 16)):
        iota(ci(k), [[0, 1]], 0, m)
    iota(io(0, 128), [[1, 128]])
    iota(io(128, 256), [[0, 8], [1, 4], [0, 4]])
    fill(v("tz"), 0.0)
    ts(ci(3, 3), ci(0, 3), 0xF0, AND)
    ts(ci(6, 2), ci(1, 2), 0x1F0, AND)
    ts(ci(8, 3), ci(0, 3), 0x30, AND)
    cp(cf(0, 11), ci(0, 11))

    quant("q1", 0, 128, "t1", 0)
    place = lambda kind, k: ap(v("l0" + kind, LB + W1 * (NR - 2 - k), LB + W1 * (NR - 1 - k)))
    for kind in "cs":
        x = v("q1" + kind, 0, W1)
        j = send([transfer(topo, core, [T.cores[r] for r in peers[:3]], bits(far), T.sem["a0" + kind], ap(x),
                           [place(kind, k) for k in range(3)], kind)], [x], len(far))
        dma("Y", v("l0" + kind, 96 + 3 * W1, 224), v("q1" + kind, 0, 128 - 3 * W1), codes=kind == "c", behind=1.0)
        arrives("a0" + kind, 3 * len(far), [v("l0" + kind, 96, 96 + 3 * W1)], [(j, COST["a0" + kind])])
    if not CFG["fw"]:
        for kind in "cs":
            x = v("q1" + kind, 0, W1)
            j = send([transfer(topo, core, [T.cores[r] for r in peers[3:]], bits(far), T.sem["b0" + kind], ap(x),
                               [place(kind, k) for k in range(3, 7)], kind)], [x], len(far))
            arrives("b0" + kind, 4 * len(far), [v("l0" + kind, LB, 96)], [(j, COST["d0" + kind])])
    act(v("ta", 256, 328), v("t1", 0, 72))
    act(v("ta", 328, 332), v("t1", 64, 68), scale=-1.0)
    act(v("ta", 332, 448), v("t1", 76, 192))
    act(v("ta", 448, 512), v("t1", 0, 64), scale=-1.0)
    quant("qa", 0, 128, "ta", 0)
    for k, n in ((0, S), (1, 128)):
        fill(so(42 + 8 * k, 50 + 8 * k), P + 2 * k)
        pick("mq", 128 * k, n, "qa", R1, 128, so(42 + 8 * k, 42 + 8 * k + n // 16))
    for kind in "cs":
        x = v("mq" + kind, 128, 128 + S)
        j = send([transfer(topo, core, helpers, bits(near), T.sem["ah0" + kind], ap(x), ap(v("h0" + kind)), kind)], [x], len(near))
        arrives("an" + kind, len(far) * len(peers), [v("ln" + kind, 0, S * NR - S)], [(j, COST["an" + kind])])
    for kind in "cs" if CFG["fw"] else ():
        x = v("l0" + kind, 96, 96 + HALF)
        j = send([transfer(topo, core, [T.cores[peers[3]]], bits(far), T.sem["b0" + kind], ap(x), ap(v("l0" + kind, LB, 96)), kind)],
                 [x], len(far))
        arrives("b0" + kind, len(far), [v("l0" + kind, LB, 96)], [(j, COST["b0" + kind])])
    gone = [v("l0s", 96, 98)]
    for kind in "cs":
        dma("Y", v("ln" + kind, S * NR - S, S * NR), v("mq" + kind, 128, 128 + S), codes=kind == "c", landed=gone)
        dma("Y", v("l2" + kind, 0, 2), v("q1" + kind, 32, 34), codes=kind == "c", landed=gone)
        for n in (S, 2 * S):
            dma("Y", v("mq" + kind, n, 2 * n), v("mq" + kind, 0, n), codes=kind == "c", landed=gone)

    iota(LR, [[16, 8], [1, 8]], behind=1)
    iota(io(256, 384), [[16, 4], [0, 32]], behind=1)
    iota(of(58, 66), [[W1, 4], [0, 2]], P + LB, behind=1)
    iota(v("tx"), [[0, 576]], behind=5)
    iota(v("ty"), [[0, 512]], behind=5)
    iota(MREF, [[0, 2], [1, 32]], behind=5)
    iota(LR1, [[32, 4], [1, 8]], behind=5)
    iota(of(76, 100), [[1, 3], [4, 8]], behind=5)
    iota(PPL, [[1, 4]], 0, -1, behind=5)

    act(cf(11, 11), cf(0, 11), scale=1.0 / 16)
    for t in range(4):
        ts(tk(SEL, t), io(128, 256), float(t), EQ)
    act(tk(ONE), tk(SEL), scale=0.0, bias=1.0)
    ts(tk(ONE, 1), io(256, 384), Q16x16, EQ)
    act(row("ty", 256, 320, 4), row("ib", 1, 17), scale=1.0 / 32)
    act(row("ty", 258, 320, 4), row("ib", 1, 17), scale=0.0, bias=-1.0)
    ts(v("tz", 3, 515, 4), io(0, 128), PP, EQ)
    ts(oR4, io(0, 8), 4.0, MUL, G4, ADD)
    for b in range(4):
        quant("qk", E + 128 * b, E + 128 * b + 128, "tz", 3 - b)
    for out, src, mul, add in ((NUM, M16x16, 1.0, 16.0), (C14, M4, 1.0, -16.0), (M4x4, M4, 4.0, 0.0), (NB32, PP, -1.0, M32),
                               (CUT, D16x16, 1.0, M - 0.5), (CLA, NB32, -1.0, M16), (I8, NB32, 0.25, D4), (CRA, M16, 1.0, float(LB)),
                               (G4x, G4, 192.0, 0.0), (I8x, I8, 192.0, 0.0)):
        act(out, src, scale=mul, bias=add)
    act(cf(32, 2), io(0, 49, 48), bias=M16)
    pick("r4", 0, 128, "q1", 0, 128, oR4)
    for b in range(4):
        mm(b, "qk", E + 128 * b, "r4", 0, 128, True, False)
        mm(b, "qk", E + 128 * b, "qa", 0, 128, False, True)
    for k in range(2):
        act(of(8 + 4 * k, 12 + 4 * k), io(0, 4), scale=float(W1), bias=float(P + LB * (1 - k)))
        act(of(24 + 8 * k, 32 + 8 * k), io(0, 8), scale=0.0, bias=cf(32 + k))
    x0, turn = NR - 1 - q, (NR - 1 - q) or NR // 2
    act(of(16, 24 - turn), io(x0, x0 + NR - turn), scale=float(W1), bias=CRA)
    act(of(24 - turn, 24), io((x0 - turn) % NR, (x0 - turn) % NR + turn), scale=float(W1), bias=CRA)
    act(of(40, 42), io(0, 2), scale=0.0, bias=PP)
    cp(so(8, 42), of(8, 42))
    act(of(66, 74), of(58, 66), bias=float(-LB))
    act(of(74, 76), io(0, 2), scale=16.0, bias=CLA)
    cp(so(58, 76), of(58, 76))
    cp(so(76, 100), of(76, 100))
    act(cf(34, 2), io(0, 2), scale=768.0, bias=G4x)
    act(cf(36, 2), io(1, 3), scale=16.0, bias=CLA)
    fill(v("c1", 0, 288, 144), 0.0)
    ts(tk(WA), tk(SEL), M16, MUL)
    act(tk(WB), tk(SEL), scale=D16x16)
    act(tk(WD), tk(SEL), scale=M4x4)
    ts(v("diag"), io(0, 16), M16, EQ)
    ts(v("mx", 0, 1), D16, 4.0, LT, CUT, MUL)
    ts(v("mx", 1, 2), D16, 4.0, GE, CUT, MUL)
    ts(v("thra"), io(0, 128), PP, GE, TINY, MUL)
    pick("rr", 0, 256, "qa", R1, 128, oRR)
    ts(v("mask"), MREF, D4, EQ)
    for b in range(4):
        act(v("s0", 64 * b, 64 * b + 64), pb(b, 0, 64), AF.Copy)
    for at, n in ((ONE, 256), (WA, 256), (WD, 128)):
        quant("qk", at, at + n, "tk", 4 * (at - ONE))
    act(lr1, LR1, bias=NB32)
    act(lr2, lr1, bias=128.0 * (M - 1))
    act(v("step"), io(0, 64), scale=4 * TINY)
    act(v("ppb"), PPL, scale=TINY, bias=0.5 * TINY)

    def one_hot(out, ref, lcol, fcol):
        ts(out, ref, lcol, EQ, fcol, MUL)

    slots = lambda t: v(t, 0, 256, 4)
    flags = lambda t, b: v(t, 256 + 32 * b, 288 + 32 * b)

    pick("ra", 0, 128, "l0", 0, 96 + HALF, oRA, "V")
    for h in range(2):
        pick("u16", 64 * h, 64, "l0", 96 * h, 96 + HALF * h, so(8 + 4 * h, 12 + 4 * h))
        pick("u32", 128 * h, 128, "l0", 96 * h, 96 + HALF * h, so(58 + 8 * h, 66 + 8 * h))
    mm(5, "u16", 0, "rr", 0, 128, True, False)
    mm(5, "rr", 128, "u16", 0, 128, False, True)
    mm(4, "u16", 0, "ra", 0, 128)
    mm(7, "mq", 0, "ra", 0, 128, True, False)
    mm(7, "ra", 0, "mq", 128, 128, False, True)
    tt(v("cl"), pb(5, 0, 128), v("thra"), GE)
    act(v("junk", 16, 32), v("cl"), off=oLA0, acc=dc(2), bias=D16)
    ts(v("tx", 384, 448), LR, dc(2), EQ)
    one_hot(slots("tx"), LR, dc(2), NUM)
    quant("x0", 0, 128, "tx", 0)
    mm(5, "qk", WA, "x0", 0, 128, True, False)
    mm(5, "qk", WB, "x0", 0, 128, False, True)
    listed = [(ts(v("do0"), pb(5, 96, 112), 4.0, MUL, M4, ADD), 0.0)]
    for k in range(2):
        quant("qr", 128 * k, 128 * k + 128, "tr", 512 * k, listed)
    quant("qw", 0, 128, "tw", 0, listed)
    mm(6, "qk", ONE, "x0", 0, 128)
    o0 = P * q
    tt(v("dm"), pb(4, o0, o0 + P), v("diag"), MUL)
    red(dc(0), v("dm"))
    cut = min(max(o0, 32), 80) if q in (0, NR - 1) else o0
    for a, b in ((0, cut), (cut, 112)):
        low = b <= o0
        ts(v("c0", a, b), pb(4, a if low else a + P, b if low else b + P), dc(0), GE if low else GT)
    running_sum(v("run0"), v("c0"), dc(2))
    ts(v("ty", 449, 457, 4), v("mx"), v("run0", 111, 112), GT, 192.0, MUL)
    quant("xk", 0, 128, "ty", 0)
    mm(4, "qk", ONE, "xk", 0, 128)

    for h in (1, 0):
        for b in range(4):
            mm(b, "qk", E + 128 * b, "l0", LB + HALF * h, 128)
            act(v("dh", 16 * h + b, 16 * h + 16, 4), pb(b, P + 1, HALF, W1), AF.Copy)
        for x in range(4):
            for b in range(4):
                a = 1024 * h + 256 * x
                o, i = v("tch", a + b, a + 256, 4), v("s0", 64 * b, 64 * b + 64)
                if 4 * b + x < CFG["bv"][h]:
                    ts(o, i, pb(b, W1 * x + P + 1, W1 * x + P + 2) if 4 * b + 4 <= CFG["bv"][h] else shift(4 * h + x, b), ADD)
                else:
                    act(o, i, bias=shift(4 * h + x, b))
        quant("al", 256 * h, 256 * h + 256, "tch", 1024 * h)
    for b in range(3):
        act(v("hx", 128 * b, 128 * b + 128), v("dh"), AF.Copy, off=so(76 + 8 * b, 84 + 8 * b))

    tt(v("ca"), pb(7, 0, 128), v("thra"), GE)
    running_sum(v("runa"), v("ca"), 0.0)
    ts(dc(12), v("runa", 127, 128), M - 0.5, LT, NUM, MUL)
    act(v("junk", 0, 16), v("ca"), off=oLA0, acc=dc(11), bias=D16)
    one_hot(slots("ty"), LR, dc(11), dc(12))
    quant("xa", 0, 128, "ty", 0)
    mm(7, "qk", ONE, "xa", 0, 128)
    act(v("m4"), pb(7, 0, 64), scale=0.25)
    act(v("inv"), pb(7, 0, 64), AF.Relu, scale=-HUGE, bias=HUGE)
    tt(v("pm", 64, 128), pb(7, 0, 64), v("mask"), MUL)
    tt(v("pf"), v("inv"), v("step"), ADD)
    for k in range(4):
        act(v("thr", k, 256, 4), v("pf"), bias=v("ppb", k, k + 1))
    act(v("thr", 256, 512), v("thr", 0, 256), bias=-128 * TINY)
    for b in range(2):
        act(junk(1 + b), v("pm", 64 + 32 * b, 96 + 32 * b), acc=dc(14 + b))
    act(dc(16, 2), dc(14, 2), AF.Sign)
    act(dc(18, 2), dc(16, 2), scale=M4x4)
    act(v("val", 0, 256), v("thr", 0, 256), AF.Relu, scale=-1.0, bias=1.0)
    for k in range(4):
        act(row("n1", 256 + k, 512, 4), row("m4"), AF.Relu, bias=float(k - 3))
    act(row("n1", 0, 256), row("n1", 256, 512), bias=-1.0)
    dma("Y", row("nm", 0, 256), row("n1", 0, 256))

    for c in range(2):
        ts(v("ov", c, 4, 2), pb(4, 112, 114), cf(34 + c), SUB, cf(36 + c), MIN)
    ts(dc(6, 2), pb(4, 112, 114), I8x, GT)
    tt(v("pm", 0, 64), pb(6, 0, 64), v("mask"), MUL)
    for b in range(2):
        act(junk(3 + b), v("pm", 32 * b, 32 * b + 32), acc=dc(4 + b), scale=dc(6 + b))
    for h in range(2):
        pick("ch", 128 * h, 128, "al", 0, 256 * h + 256, v("do0", 8 * h, 8 * h + 8))
        mm(h, "u32", 128 * h, "ch", 128 * h, 128, True, False)
        mm(h, "ch", 128 * h, "ln", 128 * h, 128, False, True)
        scatter_half("ch", h, "l1", 0, 1)

    for b in range(2):
        tt(v("c1", 144 * b + 16, 144 * b + 144), pb(b, 0, 128), v("thra"), GE)
        act(junk(5 + b), v("c1", 144 * b, 144 * b + 144), off=v("ov", 2 * b, 2 * b + 2), acc=dc(8 + b))
        one_hot(flags("tx", b), lr1, dc(8 + b), dc(6 + b))
        one_hot(flags("tx", 2 + b), lr1, dc(8 + b), dc(4 + b))
    quant("x1", 0, 144, "tx", 0)
    mm(4, "qk", WA, "x1", 0, 128, True, False)
    mm(4, "qk", WB, "x1", 0, 128, False, True)
    mm(5, "qk", SEL, "x1", 16, 128, True, False)
    mm(5, "qk", WD, "x1", 0, 128, False, True)
    first = len(plan)
    ts(v("do1", 0, 16), pb(4, 64, 80), 0.0, ADD)
    ts(v("do1", 16, 32), pb(5, 64, 80), C14, ADD, 0.0, MAX)
    for h in range(2):
        pick("pv", 128 * h, 128, "ch", 128 * h, 128 * h + 128, v("do1", 8 * h, 8 * h + 8))
        pick("pe", 128 * h, 128, "qr", 0, 256, v("do1", 16 + 8 * h, 24 + 8 * h))
    turns = (((0, 3), (0, 0), (0, 1), (1, 3), (1, 0), (0, 2), (1, 1), (1, 2)), [(x, b) for b in (3, 0, 1, 2) for x in (0, 1)])
    for h in range(2):
        made = [(mm(4 * h + b, "qk", E + 128 * b, ("pv", "pe")[x], 128 * h, 128, x == 0, x == 1), 0.0) for x, b in turns[h]]

    for h in range(2):
        for b in range(3):
            for r in range(2):
                a = 64 * (2 * b + h)
                tt(v("tgr", 512 * h + 4 * r + b, 512 * h + 512, 8), pb(4 * h + b, r, 128, 2), v("hx", a, a + 64), ADD)
        for x in range(4):
            a = 512 * h + 128 * x
            act(v("tgr", a + 3, a + 128, 4), pb(4 * h + 3, 32 * x, 32 * x + 32), bias=shift(4 * h + x, 3))
        quant("gr", 128 * h, 128 * h + 128, "tgr", 512 * h)
        scatter_half("gr", h, "l2", Z, 2)
    in_turn(first, ("S", "PE"))

    for b in range(2):
        for h in range(2):
            mm(2 * b + h, "mq", 0, "l1", 128 * h, 128, True, False, made)
            mm(2 * b + h, "l1", 128 * b, "mq", 128, 128, False, True)
    mm(4, "qw", 0, "l1", 0, 256)
    for b in range(2):
        for h in range(2):
            a = 256 * b + 128 * h
            tt(v("cb", a, a + 128), pb(2 * b + h, 0, 128), v("thr", a, a + 128), GE)
        act(junk(7 + b), v("cb", 384 * b, 384 * b + 128), off=oLA1, acc=dc(20 + b), bias=4.0 * (M - 1))
        running_sum(v("runb", 256 * b, 256 * b + 256), v("cb", 256 * b, 256 * b + 256), 0.0)
        ts(dc(24 + b), v("runb", 256 * b + 255, 256 * b + 256), 128.0, MUL, dc(20 + b), MAX)
    for b in range(2):
        one_hot(flags("ty", b), lr2, dc(24 + b), dc(16 + b))
        one_hot(v("ty", 128 * b, 128 * b + 128, 4), lr2, dc(24 + b), dc(14 + b))
        one_hot(v("ty", 128 * b + 2, 128 * b + 128, 4), lr2, dc(24 + b), dc(18 + b))
    quant("x2", 0, 128, "ty", 0)
    mm(5, "qk", ONE, "xa", 0, 128, True, False)
    mm(5, "qk", SEL, "x2", 0, 128, False, True)
    mm(7, "qk", ONE, "x2", 0, 128)
    mm(6, "qk", ONE, "x2", 0, 128)
    ts(v("do2"), pb(5, 64, 80), 512.0, MUL, M16, ADD)
    for k in range(4):
        act(v("val", 256 + k, 512, 4), pb(7, 0, 64), AF.Sign)
    for k in range(4):
        ts(row("n2", k, 256, 4), row("p6", 0, 64), float(k - 16), ADD, -1.0, MAX)
    dma("Y", row("nm", 256, 512), row("n2"))
    for h in range(2):
        tt(v("yy", 128 * h, 128 * h + 128), pb(4, 128 * h, 128 * h + 128), v("val", 128 * h, 128 * h + 128), MUL)
    dma("Y", v("y", 0, 256), v("yy", 0, 256))

    for h in range(2):
        pick_c("fin", 128 * h, 128, "l2", 0, Z + 256, v("do2", 8 * h, 8 * h + 8))
        dma("Y", v("oc", 512 * h, 512 * h + 512), v("finc", 128 * h, 128 * h + 128), codes=True)
    first = len(plan)
    for h in range(2):
        pick_s("fin", 128 * h, 128, "l2", 0, Z + 256, v("do2", 8 * h, 8 * h + 8))
    for h in range(2):
        lo, hi = 256 + 128 * h, 384 + 128 * h
        mm(h, "qw", 0, "l2", Z + 128 * h, 128)
        tt(v("yy", lo, hi), pb(h, 0, 128), v("val", lo, hi), MUL)
        dma("YS"[h], v("y", lo, hi), v("yy", lo, hi))
    in_turn(first, ("S", "V"))
    for k in range(4):
        dma("YSYS"[k], v("osc", rows=(4 * k, 4 * k + 4)), v("fins", rows=(32 * k, 32 * k + 4)))

    schedule()
    for sem, n in final.items():
        wait("G", (sem, n))
